import numpy as np, ml_dtypes
CORES = [1,5,17,21,33,37,49,53]
N = 8
BF = ml_dtypes.bfloat16
W, I, D, T = 4096, 128, 8, 5
B = W // I
def basic(rng):
    return (rng.integers(0, 256, (N, 8, 16, W)), rng.integers(0, W, (N, 8, 16, I)), rng.integers(0, D, (N, 8, 16, I)), rng.integers(0, W, (N, 8, 16, I, D)),
            rng.integers(0, 16, (N, 8, 16)), rng.integers(800, 1151, (N, 8, 16)))
def some(rng, a):
    return np.argsort(rng.random((N, 8, 16, I)), axis=2) < a[:, :, None, :]
def seat(rng, on):
    place = np.argsort(rng.random((N, 8, 16, I)), axis=2)
    near = place + rng.integers(0, 225, (N, 8, 1, I)); far = 15 * place + rng.integers(0, 15, (N, 8, 16, I))
    return np.where(on, np.where(rng.random((N, 8, 1, I)) < 0.5, near, far), -1)
def blame(rng, on, free_, dead):
    o = on.astype(np.int64); order = np.argsort(np.where(on, 0.0, 2.0) + rng.random(on.shape), axis=2); loc = np.argsort(order, axis=2)[..., None]
    cnt = (np.add.reduce(o, axis=2)[:, :, None, :] - o)[..., None]
    m = (rng.random((N, 8, 16, I, D)) * cnt).astype(np.int64); m = np.where(on[..., None] & (m >= loc), m + 1, m)
    who = np.take_along_axis(order[..., None], np.minimum(m, 15), axis=2); who = np.where(cnt > 0, who, -1)
    u = rng.random((N, 8, 16, I, D))
    return np.where(u < free_, -1, np.where(u < free_ + dead, -2, who))
def pack(x, n, q, v, e, c, w, t):
    return {"xt": x.reshape(N, 128, W).astype(BF), "nm": n.reshape(N, 128, I).astype(np.int32), "ps": q.reshape(N, 128, I).astype(BF), "dv": v.reshape(N, 128, I).astype(BF),
            "ex": e.reshape(N, 128, I * D).astype(BF), "dn": c.reshape(N, 128, I * D).astype(np.int32), "wt": w.reshape(N, 128, 1).astype(np.int32), "th": t.reshape(N, 128, 1).astype(np.int32)}
def setup_inputs(rng):
    x, n, v, c, w, t = basic(rng); on = some(rng, rng.integers(0, 17, (N, 8, I)))
    return pack(x, n, seat(rng, on), v, blame(rng, on, rng.choice(np.array([0.03, 0.1, 0.3, 0.7]), (N, 8, 1, I, 1)), 0.1), c, w, t)
def setup_inputs_spread(rng):
    x, n, v, c, w, t = basic(rng)
    x = np.floor(rng.random((N, 8, 16, W)) * np.exp2(rng.integers(0, 9, (N, 8, 1, W)))).astype(np.int64)
    n = (W * rng.random((N, 8, 16, I)) ** 3).astype(np.int64); c = (W * rng.random((N, 8, 16, I, D)) ** 2).astype(np.int64)
    t = np.minimum(np.exp2(12 * rng.random((N, 8, 16))).astype(np.int64) - 1, 4080)
    on = some(rng, (17 * rng.random((N, 8, I)) ** 2).astype(np.int64))
    return pack(x, n, seat(rng, on), v, blame(rng, on, rng.choice(np.array([0.0, 0.2, 0.6]), (N, 8, 1, I, 1)), 0.15), c, w, t)
def setup_inputs_ends(rng):
    x, n, v, c, w, t = basic(rng)
    kind = rng.integers(0, 4, (N, 8, 1, W)); x = np.where(kind == 0, 0, np.where(kind == 1, 255, 255 * rng.integers(0, 2, (N, 8, 16, W))))
    x[..., 0] = 0; x[..., W - 1] = 255; x[..., W - 37] = 0; x[:, ::2, :, W - W // 16 - 38] = 255; x[:, 1::2, :, W - W // 16 - 38] = 0
    x[:, 3, :, W - 37] = np.where(np.argsort(rng.random((N, 16)), axis=1) < 9, 0, 255)
    x[:, 3, :, W - W // 16 - 38] = np.where(np.argsort(rng.random((N, 16)), axis=1) < 11, 0, 255)
    x[:, 5, :, W - 37] = 255
    n = np.where(rng.random(n.shape) < 0.85, (W - 1) * rng.integers(0, 2, n.shape), n); c = np.where(rng.random(c.shape) < 0.85, (W - 1) * rng.integers(0, 2, c.shape), c)
    v = (D - 1) * rng.integers(0, 2, v.shape); w = 15 * rng.integers(0, 2, w.shape); w[:, 7] = 15; w[:, 0, 0] = 0
    z = np.array([0, 4080, 4079, 1])
    t[:, ::2] = rng.choice(z, (N, 4, 16), p=[0.85, 0.05, 0.05, 0.05]); t[:, 1::2] = rng.choice(z, (N, 4, 16), p=[0.3, 0.5, 0.1, 0.1])
    t[:, 7] = 4079; t[:, 7, 5] = 4080; t[:, 7, 14] = 4080; t[:, 5] = 0; t[:, 3] = rng.choice(np.array([2295, 2804]), (N, 16))
    on = some(rng, rng.choice(np.array([0, 1, 2, 4, 8, 15, 16]), (N, 8, I))); on[:, :, 15] |= rng.random((N, 8, I)) < 0.85
    on[:, 7, :, I - 1] = True; on[:, 7, 15, I - 1] = False
    on[:, 7, :, I - 2] = True
    for k in (5, 14, 15): on[:, 7, k, I - 2] = False
    climb = (0, I // 2, (W - W // 16 - 38) // B, (W - 37) // B, I - 1)
    crest = (1, I // 2 + 1, (W - 37) // B - 1)
    for i in climb + crest: on[:, 5, :, i] = False; on[:, 5, 15, i] = True
    place = np.argsort(rng.random((N, 8, 16, I)), axis=2); q = np.where(on, np.where(place < 8, place, 224 + place), -1)
    kk = np.arange(16).reshape(1, 1, 16, 1, 1); u = rng.random((N, 8, 16, I, D)); b = blame(rng, on, 0.5, 0.0)
    hot = np.where(u < 0.4, 15, np.where(u < 0.75, -2, np.where(u < 0.9, -1, b))); calm = np.where(u < 0.7, -2, np.where(u < 0.85, -1, b))
    e = np.where(on[:, :, 15][:, :, None, :, None] & (kk != 15), hot, calm)
    e[:, 7, 15, I - 1] = -1; c[:, 7, 15, I - 1] = W - 1; n[:, 7, 0:15:2, I - 1] = 0; n[:, 7, 1:15:2, I - 1] = W - 1
    e[:, 7, 5, I - 2] = -1; c[:, 7, 5, I - 2] = 0; n[:, 7, :, I - 2] = W - 1
    for i in climb + crest: q[:, 5, 15, i] = 239; e[:, 5, :, i] = -1; n[:, 5, :, i] = W - 1; c[:, 5, :, i] = W - 1
    for i in crest: c[:, 5, T - 2, i] = 0
    return pack(x, n, q, v, e, c, w, t)
def setup_inputs_corners(rng):
    x, n, v, c, w, t = basic(rng)
    x = 32 * rng.integers(0, 8, (N, 8, 16, W)); t = 32 * rng.integers(26, 36, (N, 8, 16)) - rng.integers(0, 2, (N, 8, 16))
    t = np.where(rng.random(t.shape) < 0.08, rng.choice(np.array([0, 4080]), t.shape), t); w = rng.choice(np.array([0, 1, 15]), w.shape)
    n = np.where(rng.random(n.shape) < 0.05, 0, n); c = np.where(rng.random(c.shape) < 0.05, 0, c)
    a = rng.choice(np.array([0, 1, 2, 15, 16]), (N, 8, I)); a[:, 3] = 16; a[1::2, 3, I - 1] = 15
    on = some(rng, a); q = seat(rng, on)
    full = blame(rng, on, 0.0, 0.0); mix = blame(rng, on, 0.0, 0.6); last = full.copy(); last[..., D - 1] = -1
    kk = np.arange(16).reshape(1, 1, 16, 1, 1); j = np.argmax(q, axis=2)[:, :, None, :, None]; some_on = np.any(on, axis=2)[:, :, None, :, None]
    top = np.where((kk != j) & some_on, j, -2); m = rng.integers(0, 7, (N, 8, 1, I, 1))
    e = np.where(m == 0, -1, np.where(m == 1, -2, np.where(m == 2, full, np.where(m == 3, last, np.where(m == 4, full[..., :1], np.where(m == 5, mix, top))))))
    e = np.where(m >= 0, e, np.zeros((N, 8, 16, I, D), np.int64))
    return pack(x, n, q, v, e, c, w, t)
def setup_inputs_crowd(rng):
    x, n, v, c, w, t = basic(rng)
    on = some(rng, rng.choice(np.array([1, 2, 8, 14, 15]), (N, 8, I))); q = seat(rng, on)
    kk = np.arange(16).reshape(1, 1, 16, 1, 1); j = np.argmax(q, axis=2)[:, :, None, :, None]
    own = blame(rng, on, 0.3, 0.1); other = blame(rng, on, 0.0, 0.2)
    own[:, 5] = -1; own[1::2, 5, :, 0] = -2
    e = np.where(kk == j, own, j); alt = np.where(kk == j, own, other); e[:, 1::2, :, :, D - 1] = alt[:, 1::2, :, :, D - 1]
    p = np.argmax(q < 0, axis=2)
    for r in range(1, N, 2): e[r, 7, p[r, 7, I - 1], I - 1, 0] = -1
    t[:, ::3] = 4080; t[:, 1::3] = 4080; t[:, 1::3, 5] = 0; t[:, 5] = 0
    n[:, 0:2] = n[:, 0:2, :1].copy(); c[:, 2] = c[:, 2, :1, :, :1].copy()
    n[:, 5] = (W // 2) * rng.integers(0, 2, (N, 16, I)); c[:, 5] = np.where(c[:, 5] % (W // 8) == 0, c[:, 5] + 1, c[:, 5])
    return pack(x, n, q, v, e, c, w, t)
def setup_inputs_few(rng):
    x, n, v, c, w, t = basic(rng); on = some(rng, rng.integers(0, 17, (N, 8, I))); chains = []
    for r in range(N):
        for g in rng.permutation(8)[:r % 4]:
            i = (0, I - 1, int(rng.integers(0, I)))[int(rng.integers(0, 3))]; on[r, g, :, i] = True; on[r, g, int(rng.integers(0, 16)), i] = False
            chains.append((r, int(g), i, T if r < 4 else int(rng.integers(1, T + 1))))
    q = seat(rng, on); e = np.where(on[..., None], blame(rng, on, 0.2, 0.2), -1)
    for r, g, i, k in chains:
        o = np.argsort(-q[r, g, :, i])
        e[r, g, :, i] = -1; e[r, g, o[15], i] = o[0]
        for m in range(k - 1): e[r, g, o[m], i] = o[m + 1]
    return pack(x, n, q, v, e, c, w, t)
def check_inputs(d):
    bad = []
    for k, lo, hi in (("xt", 0, 255), ("nm", 0, W - 1), ("ps", -1, 239), ("dv", 0, D - 1), ("ex", -2, 15), ("dn", 0, W - 1), ("wt", 0, 15), ("th", 0, 4080)):
        v = np.asarray(d[k]).astype(np.float64)
        if not (np.min(v) >= lo and np.max(v) <= hi and np.all(v == np.floor(v))): bad.append("range of " + k)
    if not bad:
        q = d["ps"].astype(np.int64).reshape(N, 8, 16, I); e = d["ex"].astype(np.int64).reshape(N, 8, 16, I, D); s = np.sort(q, axis=2)
        if np.any((s[:, :, 1:] == s[:, :, :-1]) & (s[:, :, 1:] >= 0)): bad.append("equal places in a puzzle of ps")
        if np.any(e == np.arange(16).reshape(1, 1, 16, 1, 1)): bad.append("a variable is its own culprit in ex")
        if np.any((e >= 0) & (np.take_along_axis(q[..., None], np.maximum(e, 0), axis=2) < 0)): bad.append("an unassigned culprit in ex")
    return bad
def reference(xt, nm, ps, dv, ex, dn, wt, th):
    X = xt.astype(np.int32).reshape(N, 8, 16, W); names = nm.astype(np.int64).reshape(N, 8, 16, I); place = ps.astype(np.int64).reshape(N, 8, 16, I)
    value = dv.astype(np.int64).reshape(N, 8, 16, I); expl = ex.astype(np.int64).reshape(N, 8, 16, I, D); dom = dn.astype(np.int64).reshape(N, 8, 16, I, D)
    w = wt.astype(np.int64).reshape(N, 8, 16, 1); thr = th.astype(np.int64).reshape(N, 8, 16, 1)
    pend = np.full((N, 8, I), -1, np.int64); A = [0] * N
    gi = np.arange(8)[:, None]; ii = np.arange(I)[None, :]; rows = np.arange(16)[None, :, None]
    for t in range(T):
        cuts = [0] * N
        for r in range(N):
            s = (r + t) % N
            n, q, v, e, pe, xs = names[r], place[r], value[r], expl[r], pend[r], X[s]
            full = np.all(q >= 0, axis=1); o = np.argmin(q, axis=1)
            p = np.where(pe >= 0, pe, np.where(full, o, np.argmax(q < 0, axis=1)))
            out = full[:, None, :] & (rows == o[:, None, :])
            q[out] = -1; e[out] = -1; e[full[:, None, :, None] & (e == o[:, None, :, None])] = -1
            mine = e[gi, p, ii]
            none = np.all(mine == -2, axis=2); cut = np.all(mine != -1, axis=2) & ~none
            e[(rows == p[:, None, :]) & none[:, None, :]] = -1
            key = np.where(np.any(mine[:, None] == rows[..., None], axis=3), q, -1); j = np.argmax(key, axis=1)
            key = np.where(rows == j[:, None, :], -1, key); j2 = np.where(np.max(key, axis=1) >= 0, np.argmax(key, axis=1), -2)
            g1, i1 = np.nonzero(cut); jj = j[cut]
            e[g1, jj, i1, v[g1, jj, i1]] = j2[cut]
            e[cut[:, None, :, None] & (e == j[:, None, :, None])] = -1
            q[g1, jj, i1] = -1; pe[cut] = jj; p = np.where(cut, j, p); cuts[r] = int(np.count_nonzero(cut))
            free_ = e[gi, p, ii] == -1; has = np.any(free_, axis=2); d = np.argmax(free_, axis=2); c = dom[s][gi, p, ii, d]
            cc = c[:, None, :]; at = ((n * cc >> 5) + n + 37 * cc) & (W - 1)
            xc = np.take_along_axis(xs, cc, 2); y = np.take_along_axis(xs, at.reshape(8, 1, 16 * I), 2).reshape(8, 16, 16, I)
            on = q >= 0
            clash = on & (np.add.reduce(np.abs(y - xc[:, :, None, :]), axis=1) <= thr[s] + 32 * (A[r] & 7)); hit = np.any(clash, axis=1)
            bad = has & hit; g1, i1 = np.nonzero(bad)
            e[g1, p[bad], i1, d[bad]] = np.argmin(np.where(clash, q, 1000), axis=1)[bad]
            ok = has & ~hit; g1, i1 = np.nonzero(ok); pp = p[ok]
            big = np.max(np.where(on[:, None], y, 0), axis=2); h = np.add.reduce(w[s] * big, axis=1) & (B - 1)
            young = np.max(q, axis=1) + 1
            n[g1, pp, i1] = c[ok]; v[g1, pp, i1] = d[ok]; q[g1, pp, i1] = young[ok]; pe[ok] = -1
            xs[g1, :, B * i1 + h[ok]] = ((xc + big) >> 1)[g1, :, i1]
        A = cuts
    shown = np.where(pend[:, :, None, :] == rows[None], -2, place)
    here = [(s - T + 1) % N for s in range(N)]
    return {"yn": names[here].reshape(N, 128, I).astype(np.float32), "yp": shown[here].reshape(N, 128, I).astype(BF), "yd": value[here].reshape(N, 128, I).astype(BF),
            "yg": expl[here].reshape(N, 128, I * D).astype(BF), "yx": X.reshape(N, 128, W).astype(BF)}

@@ -1,0 +1,555 @@
+import math
+import numpy as np
+from concourse.bass import DstId, RemoteDMATransfer
+from concourse.mybir import AluOpType as A, ActivationFunctionType as F
+
+NV = 5
+OPT = dict(selv=1, seed=0, amp=2.5, span=4.0, rounds=500, gap=0.2, pe=0.00045, hop=0.12, bias=2.0, call=0.5, lat=0.0, ov=0.01, osc=0.03)
+XW = 8224
+LN2 = math.log(2.0)
+BIG = 2097152.0
+MATS = ["I", "B", "Bh", "L2", "I32", "D", "I2", "B64", "M1", "M2", "Bm1", "Bk", "Bj", "Im256", "Bm4", "Bm8", "B4k", "Ih", "Imh", "Ic", "IBh", "IB", "ImB",
+        "BmB", "I264", "Bm264", "I64k", "Im1k", "Im1", "I260", "Im255", "I4k", "I8k", "Im4k", "Im33", "I127", "Im127", "Iv0", "Iv1", "Iv2", "Iv3", "Iv4"]
+BF, F32, I32, U16 = "bfloat16", "float32", "int32", "uint16"
+SCRATCH = {}
+for _d, _l in ((BF, dict(X=XW, exr=1024, q1=1024, q2=1024, ne=1024, wv=1024, sel=1024, Sg=1024, EZ=12 * 1024, EZi=8 * 1024, og=1024, MB=10 * 272,
+                         MBi=8 * 272, FO=10 * 128, FI=8 * 128, F0=256, xcr=2048, dd=2048, ad=2048, mxs=2048, m0=1024, CM=128 * len(MATS), ONE=512,
+                         Ws=144, Ww=144, cpos=8)),
+               (F32, dict(hf=16, dk=1024, Ks=1024, MI=10 * 136, MIi=8 * 136, CF=512, col=16, cp0=8, thr=8, acc=8)),
+               (I32, dict(dnI=1024, coli=8, wtI=4, thI=4, hi=24, ai=8)), (U16, dict(at=128, cu=128, hu=8)),
+               (BF, dict.fromkeys("psr dvr dvx0 u b1 pw P onp pc0 pf flag key Jh Pp key2 J2h vb Bh2 vj ps4 ps2 pw2 mx mp has Ph clash key3 "
+                                  "nok Yb rb s1 s2 s3 op od".split(), 128)),
+               (F32, dict.fromkeys("diff chi key0 key7 kr PK PK2 sf yf rf wc".split(), 128)),
+               (I32, dict.fromkeys("nmr n dv1 ki cc t1 ta t3 t4 t5 dd1 nf ndi ndx".split(), 128))):
+    for _k, _w in _l.items():
+        SCRATCH[_k] = ("sbuf", [128, _w], _d)
+for _b in range(8):
+    SCRATCH["B%d" % _b] = ("psum", [128, 512], F32)
+LOADS = ["ps", "ex", "dv", "nm", "dn", "xt", "wt", "th"]
+STORES = ["yn", "yp", "yd", "yg0", "yg1", "yx0", "yx1"]
+SEMAPHORES = ["sV", "sS", "sP", "sG", "sent"] + ["l" + x for x in LOADS] + ["o" + x for x in STORES] + \
+             ["%s%d" % (k, t) for k in "emf" for t in range(2 * NV - 2)]
+
+
+def R(name, lo=0, hi=None, step=1):
+    if hi is None:
+        hi = SCRATCH[name][1][1]
+    return ("ap", name, lo, hi, step)
+
+
+def W(name, lo, n):
+    return ("ap", name, lo, lo + n, 1)
+
+
+def IND(win, off):
+    return ("ind", win, off)
+
+
+def M(name):
+    return W("CM", 128 * MATS.index(name), 128)
+
+
+def _isap(x):
+    return isinstance(x, tuple) and len(x) > 0 and x[0] in ("ap", "ind")
+
+
+def _parts(x):
+    return [x] if x[0] == "ap" else [x[1], x[2]]
+
+
+def _n(x):
+    if x[0] == "ind":
+        return 16 * _n(x[2])
+    return len(range(x[2], x[3], x[4]))
+
+
+def _meet(a, b):
+    if a[3] <= b[2] or b[3] <= a[2]:
+        return False
+    return not (a[4] == b[4] and a[4] > 1 and (a[2] - b[2]) % a[4] != 0)
+
+
+def build():
+    ops = []
+    cur = [0]
+
+    def add(eng, calls, reads, writes, cost, lat=0.0, sem=None, **kw):
+        rd = [p for x in reads if _isap(x) for p in _parts(x)]
+        wr = []
+        for x in writes:
+            if x[0] == "ind":
+                wr.append(x[1]); rd.append(x[2])
+            else:
+                wr.append(x)
+        ops.append(dict(eng=eng, calls=calls, rd=rd, wr=wr, cost=cost, lat=lat, sem=sem, h=cur[0], **kw))
+
+    def two(*xs):
+        return all(SCRATCH[p[1]][2] in (BF, U16) for x in xs if _isap(x) for p in _parts(x)[:1])
+
+    def vc(out, ins, tt=False):
+        n = _n(out)
+        if out[0] == "ind":
+            c = 3.5 * n
+        elif ins and ins[0][0] == "ind":
+            c = 1.5 * n
+        elif tt:
+            c = n * (1 if any(SCRATCH[x[1]][0] == "psum" for x in ins) else (1.5 if two(out, *ins) else 2))
+        else:
+            c = n * (0.5 if two(out, *ins) else 1)
+        return OPT["ov"] + max(64, c) * 0.00083
+
+    def tt(out, a, b, op):
+        add("V", [("tensor_tensor", (out, a, b, op), {})], [a, b], [out], vc(out, [a, b], True))
+
+    def ts(out, a, s1, s2, op0, op1=None):
+        args = (out, a, s1, s2, op0) if op1 is None else (out, a, s1, s2, op0, op1)
+        add("V", [("tensor_scalar", args, {})], [a, s1, s2], [out], vc(out, [a]))
+
+    def cp(out, a):
+        add("V", [("tensor_copy", (out, a), {})], [a], [out], vc(out, [a]))
+
+    def ms(out, v):
+        add("V", [("memset", (out, v), {})], [], [out], vc(out, []))
+
+    def scan(out, d0, d1, op0, op1):
+        add("V", [("tensor_tensor_scan", (out, d0, d1, 0.0, op0, op1), {})], [d0, d1], [out], vc(out, [d0, d1]))
+
+    def act(out, a, f, bias=None, scale=None, acc=None):
+        kw = {k: v for k, v in (("bias", bias), ("scale", scale), ("accum_out", acc)) if v is not None}
+        c = _n(out) * (1.5 if a[0] == "ind" else 1)
+        add("S", [("activation", (out, a, f), kw)], [a, bias, scale], [out] + ([acc] if acc else []), OPT["osc"] + max(64, c) * 0.00083)
+
+    def mm(terms, start=True, stop=True, each=False):
+        calls, rd, wr, c = [], [], [], 0.0
+        for j, (o, l, r) in enumerate(terms):
+            calls.append(("matmul", (o, l, r, each or (start and j == 0), each or (stop and j == len(terms) - 1)), {}))
+            rd += [l, r]; wr.append(o)
+            c += max(64, _n(r)) * (4 if SCRATCH[r[1]][2] == F32 else 1) * OPT["pe"]
+        add("P", calls, rd, wr, c, lat=0.08, grp=not (start and stop))
+
+    def sm(o, *terms, **kw):
+        mm([(o, M(m) if isinstance(m, str) else m, r) for m, r in terms], **kw)
+
+    def rep(bank, mat, tile):
+        return [(R(bank, d, 512, 8), M(mat), tile) for d in range(8)]
+
+    def load(name, dst, lat, q="Y"):
+        add(q, [("load", (dst, name), {})], [], [dst], 0.06 if q == "Y" else 0.3, lat=lat, sem="l" + name)
+
+    def store(name, src, lat, q, cols=None):
+        add(q, [("store", (src, name, cols), {})], [src], [], 0.06, lat=lat, sem="o" + name)
+
+    def send(sem, pairs, lat):
+        add("G", [("send", (sem, pairs), {})], [p[0] for p in pairs], [p[1] for p in pairs], OPT["call"], lat=lat + OPT["lat"], sem=sem, remote=True)
+
+    def iota(out, pat, base, cm):
+        kw = {} if SCRATCH[out[1]][2] == I32 else {"allow_small_or_imprecise_dtypes": True}
+        add("G", [("iota", (out, pat, base, cm), kw)], [], [out], 0.13 + 2 * _n(out) * 0.00083)
+
+    c = lambda j: W("col", j, 1)
+    ci = lambda j: W("coli", j, 1)
+    load("ps", R("psr"), 2.0); load("ex", R("exr"), 2.8); load("dv", R("dvr"), 2.2); load("nm", R("nmr"), 2.4)
+    load("dn", R("dnI"), 4.0); load("xt", R("X", 0, 4096), 7.0)
+    iota(ci(0), [[1, 1]], 0, 1); iota(R("chi"), [[1, 8], [0, 16]], 0, 0); iota(R("diff"), [[-1, 128]], 0, 1); iota(R("cp0"), [[512, 8]], 0, 0)
+    load("wt", W("wtI", 0, 1), 3.0, "G"); load("th", W("thI", 0, 1), 3.0, "G")
+    ts(ci(1), ci(0), 15, None, A.bitwise_and); ts(ci(2), ci(0), 4, None, A.arith_shift_right)
+    cp(c(0), ci(1)); cp(c(1), ci(2))
+    ts(M("B"), R("chi"), c(1), None, A.is_equal); ts(M("I"), R("diff"), 0.0, None, A.is_equal)
+    ts(c(2), c(0), 1.5, None, A.add); ts(c(3), c(0), 1.0, None, A.add); ts(c(5), c(0), -16.0, None, A.add)
+    ts(c(6), c(0), 0.0, -8.0, A.is_equal, A.mult); ts(c(7), c(6), 64.5, None, A.add)
+    ts(c(8), c(0), 32.0, None, A.mult); ts(R("cpos"), R("cp0"), c(8), None, A.add)
+    ts(R("s1"), R("diff"), 0.0, 15.0 / 16, A.is_lt, A.mult); ts(R("s2"), M("I"), -1.0 / 16, -7.0 / 16, A.mult, A.add)
+    tt(R("op"), R("s1"), R("s2"), A.add); tt(R("od"), R("op"), M("B"), A.mult); ts(M("L2"), R("od"), 2.0 ** 62, 2.0 ** 61, A.mult, A.mult)
+    ts(R("s3"), R("diff"), -1.0, None, A.is_equal); tt(R("vj"), R("s3"), M("B"), A.mult); tt(M("D"), M("I"), R("vj"), A.subtract)
+    for nme, v in (("I32", 32), ("I2", 2), ("Im256", -256), ("I264", 264), ("I64k", 65536), ("Im1k", -1024), ("Im1", -1), ("I260", 260),
+                   ("Im255", -255), ("I4k", 4096), ("I8k", 8192), ("Im4k", -4096), ("Im33", -33), ("Ih", 0.5), ("Imh", -0.5), ("IB", BIG),
+                   ("ImB", -BIG), ("Ic", 49 * 65536), ("IBh", BIG / 2)) + tuple(("Iv%d" % t, 131072 * (t + 1)) for t in range(NV)):
+        if nme in ("I32", "I64k", "Ic", "IBh", "ImB", "IB", "Ih"):
+            ts(M(nme), M("I"), float(v), None, A.mult)
+        else:
+            act(M(nme), M("I"), F.Copy, scale=float(v))
+    ts(M("I127"), M("I"), 2.0 ** 64, 2.0 ** 63, A.mult, A.mult); ts(M("Im127"), M("I"), 2.0 ** 64, -2.0 ** 63, A.mult, A.mult)
+    for nme, v in (("Bh", 0.5), ("B64", 64.0), ("Bm1", -1.0), ("Bm4", -4.0), ("Bm8", -8.0), ("Bm264", -264.0), ("BmB", -BIG), ("Bk", c(3)), ("Bj", c(5))):
+        ts(M(nme), M("B"), v, None, A.mult)
+    tt(M("M1"), M("I2"), M("B"), A.subtract)
+    Bf, Bf37, Of, If = (W("CF", 128 * j, 128) for j in range(4))
+    act(Bf, M("B"), F.Copy); act(Bf37, M("B"), F.Copy, scale=37.0); ms(Of, 1.0); ms(R("ONE"), 1.0); act(If, M("I"), F.Copy)
+    ms(R("Ws"), 0.0); cp(R("Ws", 15, 143, 16), R("CM", M("B")[2], M("B")[3], 16))
+    tt(R("vb"), M("I"), R("Ws", 15, 143), A.subtract); ts(M("M2"), R("vb"), 2.0, None, A.mult)
+    ts(c(9), W("wtI", 0, 1), 32.0, None, A.add); ts(R("Ww"), R("Ws"), c(9), None, A.mult); ts(M("B4k"), M("B"), 4096.0, None, A.mult)
+    ts(c(10), W("thI", 0, 1), -4096.0, None, A.add)
+    ms(R("m0"), 0.0); ms(R("m0", 0, 1024, 16), -1024.0); ms(R("X", 4096, 4112), 0.0)
+    for z in range(2 * NV - 2):
+        ms(W("MB", 272 * z + 256, 16), 0.0); ms(W("MI", 136 * z + 128, 8), 0.0)
+    ONE = W("ONE", 0, 64)
+    ts(R("key0"), R("dnI", 0, 1024, 8), 4096.0, None, A.add); ts(R("key7"), R("dnI", 7, 1024, 8), 32768.0, None, A.add)
+    ts(R("s1"), R("psr"), 0.0, -4.0, A.is_lt, A.mult); ts(R("s2"), R("psr"), 9.0, None, A.add)
+    ts(R("sf"), R("dvr"), 4096.0, 4096.0, A.mult, A.add)
+    ts(R("op"), R("psr"), 0.0, None, A.is_ge); ts(R("od"), R("dvr"), 1.0, None, A.add); tt(R("dvx0"), R("op"), R("od"), A.mult)
+    for h in range(2):
+        cur[0] = h
+        o, x = 512 * h, "B%d" % (4 * h)
+        tt(W("Ks", o + 1, 511), W("dnI", o, 511), W("dnI", o + 1, 511), A.subtract)
+        act(W("dk", o + 1, 511), W("Ks", o + 1, 511), F.Identity, bias=-4096.0); ms(R("dk", o, o + 512, 8), 4194304.0)
+        tt(W("F0", 128 * h, 64), W("s1", 64 * h, 64), W("s2", 64 * h, 64), A.add); ms(W("F0", 128 * h + 64, 64), 0.0)
+        ts(W("q1", o, 512), W("exr", o, 512), -2.0, 18.0, A.is_equal, A.mult)
+        sm(R(x), ("I", W("exr", o, 512)), ("I", W("q1", o, 512))); act(W("EZ", 1024 * h, 512), R(x), F.Identity, bias=1.0)
+        tt(W("MI", 136 * h, 64), W("sf", 64 * h, 64), W("nmr", 64 * h, 64), A.add)
+
+    def zplane(base, tile):
+        for d in range(8):
+            ts(R("EZ", base + 512 + d, base + 1024, 8), tile, float(d + 1), None, A.is_equal)
+
+    def update(h, src, so, mb, mo, do):
+        Rr, Pc, val = (W(mb, mo + 64 * j, 64) for j in range(3))
+        x, y = "B%d" % (4 * h), "B%d" % (4 * h + 1)
+        E, Z, ne, wv = W(src, so, 512), W(src, so + 512, 512), W("ne", 512 * h, 512), W("wv", 512 * h, 512)
+        mm(rep(x, "I", Rr), each=True); tt(ne, R(x), E, A.is_equal)
+        mm([(R(y), M("I32"), Z)] + rep(y, "I", val)); act(wv, R(y), F.Relu, bias=-32.0)
+        mm([(R(x), M("I"), E)] + rep(x, "Im1k", Pc) + [(R(x), M("Im1k"), wv), (R(x), M("Im1k"), ne)])
+        tt(W("EZ", do, 512), R(x), wv, A.max)
+
+    def visit(t, h):
+        cur[0] = h
+        last, z, o = t == NV - 1, 2 * t + h, 512 * h
+        H = lambda name: W(name, 64 * h, 64)
+        x, y, a, b = ("B%d" % (4 * h + j) for j in range(4))
+        S = lambda bank, j: W(bank, 64 * j, 64)
+        eo, mo, io_, fo = 1024 * z, 272 * z, 136 * z, 128 * z
+        fin = ("F0", 128 * h) if t == 0 else ("FI", fo - 256)
+        ps9, Bh = W(fin[0], fin[1], 64), W(fin[0], fin[1] + 64, 64)
+        ndv, cand = W("MI", io_, 64), W("MI", io_ + 64, 64)
+        Ro, Pc, val, dvx = (W("MB", mo + 64 * j, 64) for j in range(4))
+        P, Jh, Pp, pf, pc0, b1, E = H("P"), H("Jh"), H("Pp"), H("pf"), H("pc0"), H("b1"), W("EZ", eo, 512)
+        if t == 0:
+            zplane(eo, H("dvx0")); thr = c(10)
+        else:
+            update(h, "EZi", eo - 2048, "MBi", mo - 544, eo)
+            zplane(eo, W("MBi", mo - 544 + 192, 64))
+            thr = W("thr", t, 1)
+            if h == 0:
+                act(thr, W("MBi", 272 * (2 * t - 1) + 256, 1), F.Identity, bias=c(10))
+        if not last:
+            send("e%d" % z, [(W("EZ", eo, 1024), W("EZi", eo, 1024))], 3.2)
+        sm(R(y), ("I64k", W("EZ", eo + 512, 512)), ("I64k", E))
+        scan(W("Ks", o, 512), W("dk", o, 512), R(y), A.add, A.min)
+        tt(H("kr"), R("Ks", o + 7, o + 512, 8), H("key7"), A.add)
+        act(H("u"), ps9, F.Exp, bias=127 * LN2, scale=-LN2); act(b1, ps9, F.Relu, bias=16.0, scale=-3.75)
+        act(H("onp"), ps9, F.Sign, bias=-8.5); act(H("pw"), ps9, F.Exp, bias=-126 * LN2, scale=LN2)
+        sm(S(a, 0), ("Bh", H("u")), ("L2", b1)); tt(P, H("u"), S(a, 0), A.is_gt)
+        if t > 0:
+            sm(S(b, 0), (If, W("MIi", io_ - 272 + 64, 64)), ("ImB", b1)); tt(ndv, S(b, 0), W("MIi", io_ - 272, 64), A.max)
+        cp(H("ndi"), ndv); ts(H("n"), H("ndi"), 4095, None, A.bitwise_and); ts(H("ps4"), ps9, 4.0, None, A.max)
+        sel, Sg = W("sel", o, 512), W("Sg", o, 512)
+        if OPT["selv"]:
+            mm(rep(x, "I", P), each=True); tt(sel, R(x), E, A.mult)
+        else:
+            mm([(R(x), M("I"), E)] + rep(x, "I32", P)); act(sel, R(x), F.Relu, bias=-32.0)
+        sm(R(y), ("B", sel)); act(Sg, R(y), F.Sign, bias=c(2), scale=-1.0)
+        sm(S(a, 1), ("I", P), ("Ih", H("onp"))); act(pf, S(a, 1), F.Relu, bias=-0.5)
+        sm(S(b, 1), ("Ic", ONE), ("IBh", H("onp")), ("ImB", P)); tt(pc0, S(b, 1), H("kr"), A.is_le)
+        G, Ka, Kb, S1 = S(x, 0), S(a, 2), S(b, 2), S(x, 1)
+        sm(G, ("M2", Bh), ("B64", pc0), *[("D", R("Sg", o + d, o + 512, 8)) for d in range(8)])
+        sm(Ka, (If, H("kr")), ("IB", P), ("ImB", pc0), ("ImB", pf), stop=False)
+        sm(Kb, (If, H("key0")), ("IB", pc0), ("IB", pf), stop=False)
+        ts(H("flag"), G, c(7), None, A.is_gt); tt(H("key"), H("flag"), H("pw"), A.mult)
+        sm(S1, ("Bh", H("key"))); tt(Jh, H("key"), S1, A.is_gt)
+        sm(Ka, ("IB", Jh), start=False); act(H("PK"), Ka, F.Relu, bias=-BIG)
+        sm(Kb, ("BmB", Jh), start=False); act(H("PK2"), Kb, F.Relu, bias=-BIG)
+        sm(S(x, 2), ("I", P), ("M1", Jh)); act(Pp, S(x, 2), F.Relu)
+        sm(S(y, 0), ("I", pf), ("I", pc0), ("Bm1", Jh)); act(Pc, S(y, 0), F.Relu)
+        K, K37, OF = S(a, 3), S(b, 3), S(x, 3)
+        sm(K, ("Iv%d" % t, ONE), (Bf, H("PK")), (Bf, H("PK2")))
+        sm(K37, (If, ndv), (Bf37, H("PK")), (Bf37, H("PK2")))
+        sm(OF, ("I4k", b1), ("I4k", Pp))
+        cp(H("ki"), K); ts(H("cc"), H("ki"), 4095, None, A.bitwise_and); cp(H("cu"), H("cc"))
+        tt(H("t1"), H("n"), H("cc"), A.mult); ts(H("ta"), H("t1"), 5, None, A.arith_shift_right)
+        tt(H("t3"), K37, H("ta"), A.add); ts(H("t4"), H("t3"), 4095, None, A.bitwise_and); tt(H("t5"), OF, H("t4"), A.add)
+        ts(H("at"), H("t5"), 4096.0, None, A.min)
+        act(H("has"), K, F.Sign, bias=131072.0 * (t + 1) + 65535.5, scale=-1.0)
+        sm(S(y, 1), ("I", Pp), ("Ih", H("has"))); act(H("Ph"), S(y, 1), F.Relu, bias=-0.5)
+        tt(cand, K, H("Ph"), A.mult)
+        sm(S(y, 2), ("I260", ONE), ("I", ps9), ("Im1", H("ps4")), ("Bm4", Jh), ("Im256", Pp)); tt(H("ps2"), S(y, 2), H("ps4"), A.min)
+        if not last:
+            sm(S(y, 3), (If, ndv), ("ImB", b1), ("ImB", Pp)); tt(H("ndx"), S(y, 3), cand, A.max)
+        else:
+            cp(H("ndx"), cand)
+        ts(H("dd1"), H("ndx"), 12, 15, A.arith_shift_right, A.bitwise_and); cp(dvx, H("dd1"))
+        sm(S(x, 4), ("I127", ONE), ("Im127", Jh)); tt(H("key2"), S(x, 4), H("key"), A.min)
+        sm(S(y, 4), ("Bh", H("key2"))); tt(H("J2h"), H("key2"), S(y, 4), A.is_gt)
+        sm(S(x, 5), ("I32", Jh), ("Bj", H("J2h")))
+        sm(S(y, 5), ("Bk", pf), ("Bk", Jh)); act(Ro, S(y, 5), F.Copy)
+        if t == 0:
+            act(val, S(x, 5), F.Relu, bias=-15.0)
+        else:
+            act(H("vj"), S(x, 5), F.Relu, bias=-15.0); tt(H("Bh2"), Bh, Jh, A.is_gt)
+            sm(S(x, 6), ("I32", P), ("Bk", H("Bh2"))); act(H("vb"), S(x, 6), F.Relu, bias=-32.0)
+            tt(val, H("vb"), H("vj"), A.add)
+        if not last:
+            act(H("s1"), Jh, F.Copy, acc=W("acc", 4 * h, 1))
+            if h == 1:
+                Ap = W(x, 448, 1)
+                sm(Ap, (Of, W("acc", 0, 1)), (Of, W("acc", 4, 1)))
+                cp(W("ai", 0, 1), Ap); ts(W("ai", 1, 1), W("ai", 0, 1), 7, None, A.bitwise_and)
+                ts(W("MB", mo + 256, 1), W("ai", 1, 1), 32.0, None, A.mult)
+            send("m%d" % z, [(W("MB", mo, 272), W("MBi", mo, 272)), (W("MI", io_, 136), W("MIi", io_, 136))], 2.7)
+        act(H("pw2"), H("ps2"), F.Exp, bias=-126 * LN2, scale=LN2); sm(S(y, 7), ("Bh", H("pw2")))
+        tt(H("mx"), H("pw2"), S(y, 7), A.is_gt)
+        sm(S(y, 6), ("I", H("ps2")), ("I264", H("mx"))); act(H("mp"), S(y, 6), F.Relu, bias=-264.0)
+        if last:
+            update(h, "EZ", eo, "MB", mo, eo + 2048)
+            zplane(eo + 2048, dvx)
+            ts(W("q1", o, 512), W("EZ", eo + 2048, 512), 17.0, -18.0, A.is_equal, A.mult)
+            sm(R(x), ("I", W("EZ", eo + 2048, 512)), ("I", W("q1", o, 512))); act(W("q2", o, 512), R(x), F.Identity, bias=-1.0)
+        win, g0 = R("X", 0, 4112), 1024 * h
+        for j in range(2):
+            q = g0 + 512 * j
+            act(W("xcr", q, 512), IND(win, W("cu", 64 * h + 32 * j, 32)), F.Copy)
+            tt(W("dd", q, 512), IND(win, W("at", 64 * h + 32 * j, 32)), W("xcr", q, 512), A.subtract)
+            act(W("ad", q, 512), W("dd", q, 512), F.Abs)
+        SM, UP = S(a, 4), S(b, 4)
+        sm(SM, ("I8k", b1), ("I8k", Pp), ("Im4k", H("has")), *[(R("Ws", 15 - k, 143 - k), R("ad", g0 + k, g0 + 1024, 16)) for k in range(16)])
+        ts(H("clash"), SM, thr, None, A.is_le)
+        tt(H("key3"), H("clash"), H("u"), A.mult)
+        sm(UP, ("Im255", ONE), ("B", H("mp")), ("Bm8", H("mx")), ("I264", H("Ph")), ("Bm264", H("clash")))
+        sm(S(a, 5), ("Bh", H("key3")))
+        tt(W("FO", fo, 64), UP, H("ps2"), A.max); tt(W("FO", fo + 64, 64), H("key3"), S(a, 5), A.is_gt)
+        if not last:
+            send("f%d" % z, [(W("FO", fo, 128), W("FI", fo, 128))], 2.2)
+        scan(W("mxs", g0, 1024), R("m0"), W("dd", g0, 1024), A.add, A.max)
+        mxv, xc = R("mxs", g0 + 15, g0 + 1024, 16), R("xcr", g0, g0 + 1024, 16)
+        sm(S(b, 6), ("Imh", ONE), ("I2", xc), ("I", mxv))
+        act(H("rf"), S(b, 6), F.Identity, bias=12582912.0, scale=0.5); act(H("rb"), H("rf"), F.Identity, bias=-12582912.0)
+        sm(S(b, 5), ("I", xc), ("I", mxv), ("Im4k", H("has")), ("B4k", H("clash"))); act(H("Yb"), S(b, 5), F.Identity, bias=4096.0)
+        if last:
+            p9, Bo = W("FO", fo, 64), W("FO", fo + 64, 64)
+            sm(S(a, 0), ("I32", Pp), ("Bk", Bo)); act(H("vb"), S(a, 0), F.Relu, bias=-32.0)
+            mm([(R(y), M("Im33"), R("ONE")), (R(y), M("I32"), W("EZ", eo + 2560, 512))] + rep(y, "I", H("vb")))
+            tt(W("og", o, 512), R(y), W("q2", o, 512), A.max)
+            store("yg%d" % h, W("og", o, 512), 2.2, "Y", (o, o + 512))
+            ts(H("s1"), p9, 1.0, -2.0, A.is_ge, A.add); ts(H("s2"), p9, -9.0, None, A.add); tt(H("op"), H("s1"), H("s2"), A.max)
+            ts(H("onp"), p9, 8.5, None, A.is_gt); tt(H("wc"), cand, H("onp"), A.mult); tt(H("nf"), ndv, H("wc"), A.max)
+            ts(H("n"), H("nf"), 4095, None, A.bitwise_and); cp(H("yf"), H("n"))
+            ts(H("dv1"), H("nf"), 12, 15, A.arith_shift_right, A.bitwise_and); ts(H("od"), H("dv1"), -1.0, None, A.add)
+
+    for t in range(NV):
+        visit(t, 0); visit(t, 1)
+        for lo, n in (((0, 4), (4, 4)) if t == NV - 1 else ((0, 8),)):
+            cur[0] = 1 if lo + n == 8 else 0
+            hs = W("B%d" % (2 + 4 * cur[0]), 384, n)
+            sm(hs, *[(R("Ww", 15 - k, 143 - k), R("Yb", 16 * lo + k, 16 * (lo + n), 16)) for k in range(16)])
+            cp(W("hi", lo, n), hs); ts(W("hi", 8 + lo, n), W("hi", lo, n), 31, None, A.bitwise_and)
+            ts(W("hf", lo, n), hs, 500000.0, 4128.0, A.is_ge, A.mult); tt(W("hf", 8 + lo, n), W("hf", lo, n), W("cpos", lo, n), A.add)
+            tt(W("hi", 16 + lo, n), W("hf", 8 + lo, n), W("hi", 8 + lo, n), A.add)
+            ts(W("hu", lo, n), W("hi", 16 + lo, n), -512.0 * lo, None, A.add)
+            cp(IND(R("X", 512 * lo, XW), W("hu", lo, n)), W("rb", 16 * lo, 16 * n))
+            if n == 4:
+                store("yx%d" % cur[0], W("X", 512 * lo, 2048), 3.0, "YS"[cur[0]], (512 * lo, 512 * lo + 2048))
+    store("yp", R("op"), 2.0, "Y"); store("yn", R("yf"), 2.0, "Y"); store("yd", R("od"), 2.0, "Y")
+    return ops
+
+
+def depend(ops):
+    deps, hist = [set() for _ in ops], {}
+    for i, o in enumerate(ops):
+        for x in o["rd"]:
+            deps[i].update(j for j, y, w in hist.get(x[1], []) if w and _meet(x, y))
+        for x in o["wr"]:
+            deps[i].update(j for j, y, w in hist.get(x[1], []) if _meet(x, y) or (w and (o.get("grp") or ops[j].get("grp"))))
+        for x in set(o["rd"]):
+            hist.setdefault(x[1], []).append((i, x, False))
+        for x in set(o["wr"]):
+            hist[x[1]] = [e for e in hist.get(x[1], []) if e[1] != x or ops[e[0]].get("grp")] + [(i, x, True)]
+        deps[i].discard(i)
+    return deps
+
+
+def replay(ops, s, hop, sc):
+    fin, free = {}, {}
+    for i in s["order"]:
+        o = ops[i]; e = o["eng"]; t = free.get(e, 0.0)
+        for j in s["waits"][i]:
+            t = max(t, fin[j] + hop)
+        free[e] = t + o["cost"] * sc.get(e, 1.0)
+        fin[i] = free[e] + o["lat"] * (sc.get("L", 1.0) if o.get("remote") else 1.0)
+    return max(fin.values())
+
+
+CASES = ((0.12, {}), (0.05, {}), (0.25, {"L": 1.5, "G": 2.0}), (0.12, {"P": 1.5}), (0.12, {"V": 1.25, "S": 1.25, "P": 1.25}))
+
+
+def plan(ops, rounds):
+    deps, rs, n = depend(ops), np.random.RandomState(OPT["seed"]), len(ops)
+    dp = [0.0] * n
+    best = schedule(ops, deps, dp); score = sum(replay(ops, best, h, sc) for h, sc in CASES)
+    for _ in range(rounds):
+        t0 = rs.rand() * max(best["fin"]); amp = OPT["amp"] * rs.rand()
+        d2 = [x + (amp * float(y) if t0 <= st < t0 + OPT["span"] else 0.0) for x, y, st in zip(dp, rs.randn(n), best["start"])]
+        s = schedule(ops, deps, d2); sc2 = sum(replay(ops, s, h, sc) for h, sc in CASES)
+        if sc2 <= score:
+            best, score, dp = s, sc2, d2
+    return best
+
+
+def schedule(ops, deps0, dp):
+    n, HOP = len(ops), OPT["hop"]
+    deps = [set(d) for d in deps0]
+    succ = [[] for _ in ops]
+    for i in range(n):
+        for j in deps[i]:
+            succ[j].append(i)
+    pri = [0.0] * n
+    for i in range(n - 1, -1, -1):
+        pri[i] = ops[i]["cost"] + ops[i]["lat"] + max([pri[k] + HOP for k in succ[i]] + [0.0])
+    pri = [p + x - OPT["bias"] * o["h"] for p, x, o in zip(pri, dp, ops)]
+    banks = [set(x[1] for x in o["rd"] + o["wr"] if SCRATCH[x[1]][0] == "psum") for o in ops]
+    left = [len(d) for d in deps]
+    ready = {e: [] for e in "VSPGY"}
+    for i in range(n):
+        if left[i] == 0:
+            ready[ops[i]["eng"]].append(i)
+    free = {e: 0.0 for e in ready}
+    fin, start, order, users, rdy = [0.0] * n, [0.0] * n, [], {}, [0.0] * n
+    while len(order) < n:
+        pick = None
+        for e, lst in ready.items():
+            if not lst:
+                continue
+            st = {}
+            for i in lst:
+                s = max(free[e], rdy[i])
+                for b in banks[i]:
+                    for e2, j in users.get(b, {}).items():
+                        if e2 != e:
+                            s = max(s, fin[j] + HOP)
+                st[i] = s
+            best = max(lst, key=lambda i: pri[i])
+            cand = [i for i in lst if i == best or st[i] + ops[i]["cost"] <= st[best] + OPT["gap"]]
+            first = min(st[i] for i in cand)
+            i = max((i for i in cand if st[i] <= first + 0.03), key=lambda i: pri[i])
+            if pick is None or st[i] < pick[0]:
+                pick = (st[i], i)
+        s, i = pick
+        e = ops[i]["eng"]
+        ready[e].remove(i)
+        for b in banks[i]:
+            deps[i].update(j for e2, j in users.get(b, {}).items() if e2 != e)
+            users.setdefault(b, {})[e] = i
+        start[i] = s; free[e] = s + ops[i]["cost"]; fin[i] = free[e] + ops[i]["lat"]; order.append(i)
+        for k in succ[i]:
+            left[k] -= 1
+            rdy[k] = max(rdy[k], free[e] if e == "P" and ops[k]["eng"] == "P" else fin[i] + HOP)
+            if left[k] == 0:
+                ready[ops[k]["eng"]].append(k)
+    pos, cnt, seen, done, waits, marked = {}, {}, {e: {} for e in ready}, {}, {}, set()
+    for i in order:
+        o = ops[i]; e = o["eng"]
+        key = o["sem"] or "s" + e
+        cnt[key] = cnt.get(key, 0) + 1; pos[i] = (key, cnt[key])
+        w = []
+        for j in sorted(deps[i], key=lambda j: -start[j]):
+            if e == "P" and ops[j]["eng"] == "P":
+                continue
+            k, v = pos[j]
+            if seen[e].get(k, 0) < v:
+                w.append(j); marked.add(j)
+                for k2, v2 in done[j].items():
+                    seen[e][k2] = max(seen[e].get(k2, 0), v2)
+        waits[i] = w
+        done[i] = {} if o.get("remote") else dict(seen[e])
+        done[i][key] = cnt[key]
+    lastof = {}
+    for i in order:
+        lastof[pos[i][0]] = i
+    marked.update(lastof.values())
+    val, tot = {}, {}
+    for i in order:
+        if i in marked:
+            k = pos[i][0]; tot[k] = tot.get(k, 0) + 1; val[i] = tot[k]
+    return dict(order=order, waits=waits, val=val, pos=pos, last=lastof, start=start, fin=fin)
+
+
+PLAN = {}
+
+
+def _share(engs, parts):
+    m = len(engs) // parts
+    return [sum(1 << e for e in engs[j * m:(j + 1) * m]) for j in range(parts)]
+
+
+def rank_program(g, core, T, topo):
+    rank = T.rank_of(core)
+    if rank is None:
+        return
+    if not PLAN:
+        PLAN["ops"] = build(); PLAN["s"] = plan(PLAN["ops"], OPT["rounds"])
+    ops, s = PLAN["ops"], PLAN["s"]
+    nr = len(T.cores)
+    nxt, prv = T.cores[(rank + 1) % nr], T.cores[(rank - 1) % nr]
+    rid, pid = topo.addr(nxt)[0], topo.addr(nxt)[1]
+    eng_out, n_in = list(topo.engines(core, nxt)), len(topo.engines(prv, core))
+    Q = {"V": g.vector, "S": g.scalar, "P": g.tensor, "G": g, "Y": g.sync}
+
+    def ap(x):
+        if not _isap(x):
+            return x
+        if x[0] == "ind":
+            return ap(x[1]).indirect(ap(x[2]))
+        return T[x[1]][:, x[2]:x[3]] if x[4] == 1 else T[x[1]][:, x[2]:x[3]:x[4]]
+
+    def count(j):
+        o = ops[j]
+        if o.get("remote"):
+            return n_in
+        return 16 if o["sem"] else s["val"][j]
+
+    sent = 0
+    for i in s["order"]:
+        o = ops[i]; q = Q[o["eng"]]
+        for j in s["waits"][i]:
+            q.wait_ge(T.sem[s["pos"][j][0]], count(j))
+        ins = None
+        for name, args, kw in o["calls"]:
+            if name == "load":
+                if o["eng"] == "G":
+                    ins = q.dma_start(ap(args[0]), T[args[1]][:], allow_slow_non_contiguous=True)
+                else:
+                    ins = q.dma_start(ap(args[0]), T[args[1]][:])
+            elif name == "store":
+                dst = T[args[1]][:] if args[2] is None else T[args[1][:2]][:, args[2][0]:args[2][1]]
+                ins = q.dma_start(dst, ap(args[0]))
+            elif name == "send":
+                masks = _share(eng_out, len(args[1]))
+                if len(masks) == 1:
+                    q.remote_dma(ap(args[1][0][1]), ap(args[1][0][0]), T.sem[args[0]], T.sem.sent, pid, rid, masks[0])
+                else:
+                    q.remote_dma_fused([RemoteDMATransfer(dst_ids=[DstId(rid=rid, pnc=pid)], dma_engine_mask=m, remote_sem=T.sem[args[0]],
+                                                          src=ap(a), dst=ap(b)) for m, (a, b) in zip(masks, args[1])], local_sem=T.sem.sent)
+                sent += len(eng_out)
+            else:
+                a = [ap(x) for x in args]; k = {kk: ap(v) for kk, v in kw.items()}
+                if name == "tensor_tensor":
+                    ins = q.tensor_tensor(*a)
+                elif name == "tensor_scalar":
+                    ins = q.tensor_scalar(*a)
+                elif name == "tensor_copy":
+                    ins = q.tensor_copy(*a)
+                elif name == "memset":
+                    ins = q.memset(*a)
+                elif name == "tensor_tensor_scan":
+                    ins = q.tensor_tensor_scan(*a)
+                elif name == "activation":
+                    ins = q.activation(*a, **k)
+                elif name == "matmul":
+                    ins = q.matmul(*a)
+                else:
+                    ins = q.iota(*a, **k)
+        if o.get("remote"):
+            continue
+        if o["sem"]:
+            ins.then_inc(T.sem[o["sem"]], 16)
+        elif i in s["val"]:
+            ins.then_inc(T.sem["s" + o["eng"]], 1)
+    for k, j in s["last"].items():
+        g.wait_ge(T.sem[k], count(j))
+    g.wait_ge(T.sem.sent, sent)

@@ -4,28 +4,36 @@ from concourse.bass import DstId, RemoteDMATransfer
 from concourse.mybir import AluOpType as A, ActivationFunctionType as F
 
 NV = 5
-OPT = dict(selv=1, seed=0, amp=2.5, span=4.0, rounds=500, gap=0.2, pe=0.00045, hop=0.12, bias=2.0, call=0.5, lat=0.0, ov=0.01, osc=0.03)
+OPT = dict(selv=0, seed=0, amp=2.5, span=4.0, rounds=500, gap=0.2, pe=0.00045, hop=0.12, bias=2.0, call=0.5, lat=0.0, ov=0.01, osc=0.03, keep=2,
+           pd=(0, 0), xcs=1, ys=(1, 0))
 XW = 8224
 LN2 = math.log(2.0)
 BIG = 2097152.0
-MATS = ["I", "B", "Bh", "L2", "I32", "D", "I2", "B64", "M1", "M2", "Bm1", "Bk", "Bj", "Im256", "Bm4", "Bm8", "B4k", "Ih", "Imh", "Ic", "IBh", "IB", "ImB",
-        "BmB", "I264", "Bm264", "I64k", "Im1k", "Im1", "I260", "Im255", "I4k", "I8k", "Im4k", "Im33", "I127", "Im127", "Iv0", "Iv1", "Iv2", "Iv3", "Iv4"]
+Q = 65536.0
+MW = 336
+SCALED = dict(I32=("I", 32), Iq=("I", Q), Imq=("I", -Q), Im1=("I", -1), I300=("I", 300), O300=("O", 300), Om300=("O", -300), Bh=("B", 0.5),
+              I60k=("I", 61440), Im60k=("I", -61440), I4M=("I", 4194304), I64q=("I", 64 * Q), Is=("I", 2.0 ** 124), O256=("O", 256), Bm4=("B", -4),
+              Os=("O", 2.0 ** 126), Ims=("I", -2.0 ** 126), Om32=("O", -32), I128=("I", 128), I8k=("I", 8192), Bm8k=("B", -8192), B4k=("B", 4096),
+              Im224=("I", -224), Im256=("I", -256), B2k=("B", 2048), Im3k=("I", -3072), B3k=("B", 3072), I3=("I", 3), Im64q=("I", -64 * Q),
+              Im251=("I", -251), I256=("I", 256), Bm256=("B", -256), Imh=("I", -0.5), I2=("I", 2), I4k=("I", 4096), ImB=("I", -BIG), Im1k=("I", -1024),
+              Iiq=("I", 1 / Q), Im2iq=("I", -2 / Q), I63=("I", 63), **{"Iv%d" % t: ("I", 131072 * (t + 1)) for t in range(NV)})
+MATS = ["I", "B", "O", "L2", "D", "MP", "T33", "Hm", "Bk", "Bj"] + list(SCALED)
 BF, F32, I32, U16 = "bfloat16", "float32", "int32", "uint16"
 SCRATCH = {}
-for _d, _l in ((BF, dict(X=XW, exr=1024, q1=1024, q2=1024, ne=1024, wv=1024, sel=1024, Sg=1024, EZ=12 * 1024, EZi=8 * 1024, og=1024, MB=10 * 272,
-                         MBi=8 * 272, FO=10 * 128, FI=8 * 128, F0=256, xcr=2048, dd=2048, ad=2048, mxs=2048, m0=1024, CM=128 * len(MATS), ONE=512,
+for _d, _l in ((BF, dict(X=XW, exr=1024, q1=1024, q2=1024, ne=1024, dl=1024, sel=1024, Sg=1024, Zn=1024, EZ=12 * 512, EZi=8 * 512, og=1024, MB=10 * MW,
+                         MBi=8 * MW, FO=10 * 128, FI=8 * 128, F0=128, xcr=2048, dd=2048, ad=2048, mxs=2048, m0=1024, CM=128 * len(MATS), ONE=512,
                          Ws=144, Ww=144, cpos=8)),
-               (F32, dict(hf=16, dk=1024, Ks=1024, MI=10 * 136, MIi=8 * 136, CF=512, col=16, cp0=8, thr=8, acc=8)),
+               (F32, dict(hf=16, dk=1024, Ks=1024, MI=5 * MW, MIi=4 * MW, CF=512, col=16, cp0=8, thr=8, acc=8)),
                (I32, dict(dnI=1024, coli=8, wtI=4, thI=4, hi=24, ai=8)), (U16, dict(at=128, cu=128, hu=8)),
-               (BF, dict.fromkeys("psr dvr dvx0 u b1 pw P onp pc0 pf flag key Jh Pp key2 J2h vb Bh2 vj ps4 ps2 pw2 mx mp has Ph clash key3 "
-                                  "nok Yb rb s1 s2 s3 op od".split(), 128)),
-               (F32, dict.fromkeys("diff chi key0 key7 kr PK PK2 sf yf rf wc".split(), 128)),
-               (I32, dict.fromkeys("nmr n dv1 ki cc t1 ta t3 t4 t5 dd1 nf ndi ndx".split(), 128))):
+               (BF, dict.fromkeys("psr dvr dvx0 O0 u b1 pwc P pcx pf key Jh Pp key2 J2h vb Bh2 vj val neo ps4 ps2 pw2 mx mp clash key3 khi klo "
+                                  "Yb rb s1 s2 s3 s4 op od xc".split(), 128)),
+               (F32, dict.fromkeys("diff chi key7 kr sf yf rf cs".split(), 128)), (F32, dict(dg=64)),
+               (I32, dict.fromkeys("nmr n dv1 ki kc kd t1 ta t3 t4 nf ndi".split(), 128))):
     for _k, _w in _l.items():
         SCRATCH[_k] = ("sbuf", [128, _w], _d)
 for _b in range(8):
     SCRATCH["B%d" % _b] = ("psum", [128, 512], F32)
-LOADS = ["ps", "ex", "dv", "nm", "dn", "xt", "wt", "th"]
+LOADS = ["ps", "ex0", "dn0", "dv", "nm", "ex1", "xt", "dn1", "wt", "th"]
 STORES = ["yn", "yp", "yd", "yg0", "yg1", "yx0", "yx1"]
 SEMAPHORES = ["sV", "sS", "sP", "sG", "sent"] + ["l" + x for x in LOADS] + ["o" + x for x in STORES] + \
              ["%s%d" % (k, t) for k in "emf" for t in range(2 * NV - 2)]
@@ -69,9 +77,12 @@ def _meet(a, b):
     return not (a[4] == b[4] and a[4] > 1 and (a[2] - b[2]) % a[4] != 0)
 
 
+def _psum(x):
+    return x[1][0] == "#"
+
+
 def build():
-    ops = []
-    cur = [0]
+    ops, cur, tiles = [], [0], [0]
 
     def add(eng, calls, reads, writes, cost, lat=0.0, sem=None, **kw):
         rd = [p for x in reads if _isap(x) for p in _parts(x)]
@@ -81,19 +92,20 @@ def build():
                 wr.append(x[1]); rd.append(x[2])
             else:
                 wr.append(x)
-        ops.append(dict(eng=eng, calls=calls, rd=rd, wr=wr, cost=cost, lat=lat, sem=sem, h=cur[0], **kw))
+        tile = [x[1] for x in rd + wr if _psum(x)]
+        ops.append(dict(eng=eng, calls=calls, rd=rd, wr=wr, cost=cost, lat=lat, sem=sem, h=cur[0], tile=tile[0] if tile else None, **kw))
 
     def two(*xs):
-        return all(SCRATCH[p[1]][2] in (BF, U16) for x in xs if _isap(x) for p in _parts(x)[:1])
+        return all(not _psum(p) and SCRATCH[p[1]][2] in (BF, U16) for x in xs if _isap(x) for p in _parts(x)[:1])
 
     def vc(out, ins, tt=False):
         n = _n(out)
         if out[0] == "ind":
-            c = 3.5 * n
+            c = 3.5 * n + 60
         elif ins and ins[0][0] == "ind":
-            c = 1.5 * n
+            c = 1.5 * n + 60
         elif tt:
-            c = n * (1 if any(SCRATCH[x[1]][0] == "psum" for x in ins) else (1.5 if two(out, *ins) else 2))
+            c = n * (1 if any(_psum(x) for x in ins) else 2)
         else:
             c = n * (0.5 if two(out, *ins) else 1)
         return OPT["ov"] + max(64, c) * 0.00083
@@ -116,25 +128,40 @@ def build():
 
     def act(out, a, f, bias=None, scale=None, acc=None):
         kw = {k: v for k, v in (("bias", bias), ("scale", scale), ("accum_out", acc)) if v is not None}
-        c = _n(out) * (1.5 if a[0] == "ind" else 1)
+        c = _n(out) * 1.5 + 60 if a[0] == "ind" else _n(out)
         add("S", [("activation", (out, a, f), kw)], [a, bias, scale], [out] + ([acc] if acc else []), OPT["osc"] + max(64, c) * 0.00083)
 
-    def mm(terms, start=True, stop=True, each=False):
-        calls, rd, wr, c = [], [], [], 0.0
-        for j, (o, l, r) in enumerate(terms):
-            calls.append(("matmul", (o, l, r, each or (start and j == 0), each or (stop and j == len(terms) - 1)), {}))
-            rd += [l, r]; wr.append(o)
-            c += max(64, _n(r)) * (4 if SCRATCH[r[1]][2] == F32 else 1) * OPT["pe"]
-        add("P", calls, rd, wr, c, lat=0.08, grp=not (start and stop))
+    def sm(*pieces, n=64):
+        tiles[0] += 1
+        name = "#%d" % tiles[0]
+        pieces = [p if isinstance(p, list) else [p] for p in pieces]
+        pieces = [p for p in pieces if p]
+        for a, piece in enumerate(pieces):
+            calls, rd, c = [], [], 0.0
+            for b, term in enumerate(piece):
+                l, r = M(term[0]) if isinstance(term[0], str) else term[0], term[1]
+                outs = [R(name, d, 512, 8) for d in range(8)] if len(term) == 3 else [W(name, 0, n)]
+                for d, o in enumerate(outs):
+                    first, end = a == 0 and b == 0, a == len(pieces) - 1 and b == len(piece) - 1
+                    alone = first and end
+                    calls.append(("matmul", (o, l, r, alone or (first and d == 0), alone or (end and d == len(outs) - 1)), {}))
+                    c += max(64, _n(r)) * (4 if SCRATCH[r[1]][2] == F32 else 1) * OPT["pe"]
+                rd += [l, r]
+            add("P", calls, rd, [W(name, 0, n)], c, lat=0.08)
+        return W(name, 0, n)
 
-    def sm(o, *terms, **kw):
-        mm([(o, M(m) if isinstance(m, str) else m, r) for m, r in terms], **kw)
+    def planes(groups):
+        tiles[0] += 1
+        name, calls, rd = "#%d" % tiles[0], [], []
+        for p, terms in enumerate(groups):
+            for b, (m, r) in enumerate(terms):
+                calls.append(("matmul", (W(name, 64 * p, 64), M(m), r, b == 0, b == len(terms) - 1), {})); rd += [M(m), r]
+        add("P", calls, rd, [W(name, 0, 512)], 64 * len(calls) * OPT["pe"], lat=0.08)
+        return W(name, 0, 512)
 
-    def rep(bank, mat, tile):
-        return [(R(bank, d, 512, 8), M(mat), tile) for d in range(8)]
-
-    def load(name, dst, lat, q="Y"):
-        add(q, [("load", (dst, name), {})], [], [dst], 0.06 if q == "Y" else 0.3, lat=lat, sem="l" + name)
+    def load(name, dst, lat, q="Y", cols=None):
+        add(q, [("load", (dst, name[:2], cols), {})], [], [dst], 0.06 if q != "G" else 0.3, lat=lat, sem="l" + name,
+            up=100.0 * (len(LOADS) - LOADS.index(name)) if q != "G" else 0.0)
 
     def store(name, src, lat, q, cols=None):
         add(q, [("store", (src, name, cols), {})], [src], [], 0.06, lat=lat, sem="o" + name)
@@ -144,191 +171,196 @@ def build():
 
     def iota(out, pat, base, cm):
         kw = {} if SCRATCH[out[1]][2] == I32 else {"allow_small_or_imprecise_dtypes": True}
-        add("G", [("iota", (out, pat, base, cm), kw)], [], [out], 0.13 + 2 * _n(out) * 0.00083)
+        add("G", [("iota", (out, pat, base, cm), kw)], [], [out], 0.13 + 2 * _n(out) * 0.00083, up=50.0)
 
     c = lambda j: W("col", j, 1)
     ci = lambda j: W("coli", j, 1)
-    load("ps", R("psr"), 2.0); load("ex", R("exr"), 2.8); load("dv", R("dvr"), 2.2); load("nm", R("nmr"), 2.4)
-    load("dn", R("dnI"), 4.0); load("xt", R("X", 0, 4096), 7.0)
+    load("ps", R("psr"), 2.1); load("ex0", W("exr", 0, 512), 2.6, cols=(0, 512)); load("dn0", W("dnI", 0, 512), 3.5, cols=(0, 512))
+    load("dv", R("dvr"), 3.6); load("nm", R("nmr"), 3.8); load("ex1", W("exr", 512, 512), 4.3, cols=(512, 1024))
+    load("xt", R("X", 0, 4096), 8.2); load("dn1", W("dnI", 512, 512), 9.2, cols=(512, 1024))
     iota(ci(0), [[1, 1]], 0, 1); iota(R("chi"), [[1, 8], [0, 16]], 0, 0); iota(R("diff"), [[-1, 128]], 0, 1); iota(R("cp0"), [[512, 8]], 0, 0)
     load("wt", W("wtI", 0, 1), 3.0, "G"); load("th", W("thI", 0, 1), 3.0, "G")
     ts(ci(1), ci(0), 15, None, A.bitwise_and); ts(ci(2), ci(0), 4, None, A.arith_shift_right)
-    cp(c(0), ci(1)); cp(c(1), ci(2))
-    ts(M("B"), R("chi"), c(1), None, A.is_equal); ts(M("I"), R("diff"), 0.0, None, A.is_equal)
-    ts(c(2), c(0), 1.5, None, A.add); ts(c(3), c(0), 1.0, None, A.add); ts(c(5), c(0), -16.0, None, A.add)
-    ts(c(6), c(0), 0.0, -8.0, A.is_equal, A.mult); ts(c(7), c(6), 64.5, None, A.add)
+    cp(W("col", 0, 2), W("coli", 1, 2))
+    ts(M("B"), R("chi"), c(1), None, A.is_equal); ts(M("I"), R("diff"), 0.0, None, A.is_equal); tt(M("O"), M("B"), M("I"), A.subtract)
+    ts(c(2), c(0), 1.5, None, A.add); ts(c(3), c(0), 1.0, None, A.add); ts(c(5), c(0), 0.5, -8.0, A.mult, A.add)
     ts(c(8), c(0), 32.0, None, A.mult); ts(R("cpos"), R("cp0"), c(8), None, A.add)
     ts(R("s1"), R("diff"), 0.0, 15.0 / 16, A.is_lt, A.mult); ts(R("s2"), M("I"), -1.0 / 16, -7.0 / 16, A.mult, A.add)
     tt(R("op"), R("s1"), R("s2"), A.add); tt(R("od"), R("op"), M("B"), A.mult); ts(M("L2"), R("od"), 2.0 ** 62, 2.0 ** 61, A.mult, A.mult)
-    ts(R("s3"), R("diff"), -1.0, None, A.is_equal); tt(R("vj"), R("s3"), M("B"), A.mult); tt(M("D"), M("I"), R("vj"), A.subtract)
-    for nme, v in (("I32", 32), ("I2", 2), ("Im256", -256), ("I264", 264), ("I64k", 65536), ("Im1k", -1024), ("Im1", -1), ("I260", 260),
-                   ("Im255", -255), ("I4k", 4096), ("I8k", 8192), ("Im4k", -4096), ("Im33", -33), ("Ih", 0.5), ("Imh", -0.5), ("IB", BIG),
-                   ("ImB", -BIG), ("Ic", 49 * 65536), ("IBh", BIG / 2)) + tuple(("Iv%d" % t, 131072 * (t + 1)) for t in range(NV)):
-        if nme in ("I32", "I64k", "Ic", "IBh", "ImB", "IB", "Ih"):
-            ts(M(nme), M("I"), float(v), None, A.mult)
+    ts(R("s3"), R("diff"), -1.0, None, A.is_equal); tt(R("vj"), R("s3"), M("B"), A.mult); tt(R("s4"), M("I"), R("vj"), A.subtract)
+    ts(M("D"), R("s4"), 2.0 ** 62, 2.0 ** 61, A.mult, A.mult)
+    for j, (nme, (base, v)) in enumerate(SCALED.items()):
+        if abs(v) > 1e29:
+            ts(M(nme), M(base), v / 2.0 ** 63, 2.0 ** 63, A.mult, A.mult)
+        elif j % 3 == 0:
+            ts(M(nme), M(base), float(v), None, A.mult)
         else:
-            act(M(nme), M("I"), F.Copy, scale=float(v))
-    ts(M("I127"), M("I"), 2.0 ** 64, 2.0 ** 63, A.mult, A.mult); ts(M("Im127"), M("I"), 2.0 ** 64, -2.0 ** 63, A.mult, A.mult)
-    for nme, v in (("Bh", 0.5), ("B64", 64.0), ("Bm1", -1.0), ("Bm4", -4.0), ("Bm8", -8.0), ("Bm264", -264.0), ("BmB", -BIG), ("Bk", c(3)), ("Bj", c(5))):
-        ts(M(nme), M("B"), v, None, A.mult)
-    tt(M("M1"), M("I2"), M("B"), A.subtract)
+            act(M(nme), M(base), F.Copy, scale=float(v))
+    act(M("Bk"), M("B"), F.Copy, scale=c(3)); act(M("Bj"), M("B"), F.Copy, scale=c(5))
+    tt(M("Hm"), M("I"), M("Bh"), A.subtract)
+    ts(R("key"), M("O"), 33.0 * Q, None, A.mult); tt(M("T33"), R("key"), M("Iq"), A.add)
     Bf, Bf37, Of, If = (W("CF", 128 * j, 128) for j in range(4))
     act(Bf, M("B"), F.Copy); act(Bf37, M("B"), F.Copy, scale=37.0); ms(Of, 1.0); ms(R("ONE"), 1.0); act(If, M("I"), F.Copy)
     ms(R("Ws"), 0.0); cp(R("Ws", 15, 143, 16), R("CM", M("B")[2], M("B")[3], 16))
-    tt(R("vb"), M("I"), R("Ws", 15, 143), A.subtract); ts(M("M2"), R("vb"), 2.0, None, A.mult)
-    ts(c(9), W("wtI", 0, 1), 32.0, None, A.add); ts(R("Ww"), R("Ws"), c(9), None, A.mult); ts(M("B4k"), M("B"), 4096.0, None, A.mult)
-    ts(c(10), W("thI", 0, 1), -4096.0, None, A.add)
+    ts(R("key2"), R("Ws", 15, 143), 4.0, None, A.mult); tt(R("key3"), R("key2"), M("I"), A.add); ts(M("MP"), R("key3"), 2.0 ** 62, 2.0 ** 62, A.mult, A.mult)
+    ts(c(9), W("wtI", 0, 1), 32.0, None, A.add); ts(R("Ww"), R("Ws"), c(9), None, A.mult)
+    ts(c(10), W("thI", 0, 1), -8192.0, None, A.add)
+    ms(c(11), 2.0 ** -60); ts(c(11), c(11), -2.0 ** -63, None, A.mult)
+    iota(W("sf", 0, 64), [[0, 4], [1, 16]], 0, 0); ts(ci(3), ci(0), 1, None, A.add); ts(ci(4), ci(3), 15, None, A.bitwise_and); cp(c(13), ci(4))
+    ts(W("kr", 0, 64), W("sf", 0, 64), c(0), 16384.0, A.is_equal, A.mult); ts(W("yf", 0, 64), W("sf", 0, 64), c(13), -8192.0, A.is_equal, A.mult)
+    tt(R("dg"), W("kr", 0, 64), W("yf", 0, 64), A.add); ts(c(12), c(0), 14.5, 8192.0, A.is_lt, A.mult)
     ms(R("m0"), 0.0); ms(R("m0", 0, 1024, 16), -1024.0); ms(R("X", 4096, 4112), 0.0)
     for z in range(2 * NV - 2):
-        ms(W("MB", 272 * z + 256, 16), 0.0); ms(W("MI", 136 * z + 128, 8), 0.0)
+        ms(W("MB", MW * z + 320, 16), 0.0); ms(W("MI", MW // 2 * z + 128, MW // 2 - 128), 0.0)
     ONE = W("ONE", 0, 64)
-    ts(R("key0"), R("dnI", 0, 1024, 8), 4096.0, None, A.add); ts(R("key7"), R("dnI", 7, 1024, 8), 32768.0, None, A.add)
-    ts(R("s1"), R("psr"), 0.0, -4.0, A.is_lt, A.mult); ts(R("s2"), R("psr"), 9.0, None, A.add)
-    ts(R("sf"), R("dvr"), 4096.0, 4096.0, A.mult, A.add)
+    ts(R("s1"), R("psr"), 0.0, -4.0, A.is_lt, A.mult); ts(R("s2"), R("psr"), 5.0, None, A.add); tt(R("F0"), R("s1"), R("s2"), A.add)
+    act(R("sf"), R("dvr"), F.Identity, bias=4096.0, scale=4096.0)
     ts(R("op"), R("psr"), 0.0, None, A.is_ge); ts(R("od"), R("dvr"), 1.0, None, A.add); tt(R("dvx0"), R("op"), R("od"), A.mult)
+
+    def marks(h, tile):
+        for d in range(8):
+            ts(R("Zn", 512 * h + d, 512 * h + 512, 8), tile, float(d + 1), 32 * Q, A.is_equal, A.mult)
+        return W("Zn", 512 * h, 512)
+
     for h in range(2):
         cur[0] = h
-        o, x = 512 * h, "B%d" % (4 * h)
+        o, H = 512 * h, lambda name: W(name, 64 * h, 64)
         tt(W("Ks", o + 1, 511), W("dnI", o, 511), W("dnI", o + 1, 511), A.subtract)
         act(W("dk", o + 1, 511), W("Ks", o + 1, 511), F.Identity, bias=-4096.0); ms(R("dk", o, o + 512, 8), 4194304.0)
-        tt(W("F0", 128 * h, 64), W("s1", 64 * h, 64), W("s2", 64 * h, 64), A.add); ms(W("F0", 128 * h + 64, 64), 0.0)
-        ts(W("q1", o, 512), W("exr", o, 512), -2.0, 18.0, A.is_equal, A.mult)
-        sm(R(x), ("I", W("exr", o, 512)), ("I", W("q1", o, 512))); act(W("EZ", 1024 * h, 512), R(x), F.Identity, bias=1.0)
-        tt(W("MI", 136 * h, 64), W("sf", 64 * h, 64), W("nmr", 64 * h, 64), A.add)
+        ts(H("key7"), R("dnI", o + 7, o + 512, 8), 32768.0, None, A.add)
+        ts(H("ta"), R("dnI", o, o + 512, 8), 5, None, A.arith_shift_right); ts(H("khi"), H("ta"), 128.0, None, A.add)
+        ts(H("t4"), R("dnI", o, o + 512, 8), 31, None, A.bitwise_and); cp(H("klo"), H("t4"))
+        ex, q1, Z = W("exr", o, 512), W("q1", o, 512), marks(h, H("dvx0"))
+        ts(q1, ex, -2.0, 18.0, A.is_equal, A.mult)
+        tt(W("EZ", o, 512), sm(("Iq", R("ONE")), ("Iq", ex), ("Iq", q1), n=512), Z, A.max)
+        act(W("dl", o, 512), sm([("I", ex), ("I", q1), ("Iiq", Z)], n=512), F.Relu, bias=-31.0)
+        act(H("O0"), sm([("I", R("dl", o + d, o + 512, 8)) for d in range(8)]), F.Copy)
+        tt(W("MI", MW // 2 * h, 64), H("sf"), H("nmr"), A.add)
 
-    def zplane(base, tile):
-        for d in range(8):
-            ts(R("EZ", base + 512 + d, base + 1024, 8), tile, float(d + 1), None, A.is_equal)
+    def update(h, E, mb, mo, out):
+        Rr, Tv, dP = (W(mb, mo + 64 * j, 64) for j in range(3))
+        ne, dl = W("ne", 512 * h, 512), W("dl", 512 * h, 512)
+        tt(ne, sm(("Iq", Rr, 8), n=512), E, A.is_equal)
+        act(dl, sm(("I3", E), ("Imq", Tv, 8), n=512), F.Relu, bias=-64 * Q)
+        Z = marks(h, dP)
+        tt(out, sm(("I", E), ("Im64q", ne), ("Im1", dl), n=512), Z, A.max)
 
-    def update(h, src, so, mb, mo, do):
-        Rr, Pc, val = (W(mb, mo + 64 * j, 64) for j in range(3))
-        x, y = "B%d" % (4 * h), "B%d" % (4 * h + 1)
-        E, Z, ne, wv = W(src, so, 512), W(src, so + 512, 512), W("ne", 512 * h, 512), W("wv", 512 * h, 512)
-        mm(rep(x, "I", Rr), each=True); tt(ne, R(x), E, A.is_equal)
-        mm([(R(y), M("I32"), Z)] + rep(y, "I", val)); act(wv, R(y), F.Relu, bias=-32.0)
-        mm([(R(x), M("I"), E)] + rep(x, "Im1k", Pc) + [(R(x), M("Im1k"), wv), (R(x), M("Im1k"), ne)])
-        tt(W("EZ", do, 512), R(x), wv, A.max)
+    def record(out, mi, io_, mb, mo, t, b1):
+        tt(out, sm([(If, W(mi, io_ + 64, 64)), ("I4k", W(mb, mo + 128, 64)), ("Iv%d" % t, W(mb, mo + 192, 64))], ("ImB", b1)), W(mi, io_, 64), A.max)
 
     def visit(t, h):
         cur[0] = h
         last, z, o = t == NV - 1, 2 * t + h, 512 * h
         H = lambda name: W(name, 64 * h, 64)
-        x, y, a, b = ("B%d" % (4 * h + j) for j in range(4))
-        S = lambda bank, j: W(bank, 64 * j, 64)
-        eo, mo, io_, fo = 1024 * z, 272 * z, 136 * z, 128 * z
-        fin = ("F0", 128 * h) if t == 0 else ("FI", fo - 256)
-        ps9, Bh = W(fin[0], fin[1], 64), W(fin[0], fin[1] + 64, 64)
-        ndv, cand = W("MI", io_, 64), W("MI", io_ + 64, 64)
-        Ro, Pc, val, dvx = (W("MB", mo + 64 * j, 64) for j in range(4))
-        P, Jh, Pp, pf, pc0, b1, E = H("P"), H("Jh"), H("Pp"), H("pf"), H("pc0"), H("b1"), W("EZ", eo, 512)
+        eo, mo, io_, fo = 512 * z, MW * z, MW // 2 * z, 128 * z
+        ps, Bh = (H("F0"), None) if t == 0 else (W("FI", fo - 256, 64), W("FI", fo - 192, 64))
+        ndv, PK = W("MI", io_, 64), W("MI", io_ + 64, 64)
+        Ro, Tv, dP, Ph, On = (W("MB", mo + 64 * j, 64) for j in range(5))
+        P, Jh, Pp, pf, pcx, b1, E = H("P"), H("Jh"), H("Pp"), H("pf"), H("pcx"), H("b1"), W("EZ", eo, 512)
         if t == 0:
-            zplane(eo, H("dvx0")); thr = c(10)
+            Oo, thr = H("O0"), c(10)
         else:
-            update(h, "EZi", eo - 2048, "MBi", mo - 544, eo)
-            zplane(eo, W("MBi", mo - 544 + 192, 64))
-            thr = W("thr", t, 1)
+            Oo, thr = W("MBi", mo - 2 * MW + 256, 64), W("thr", t, 1)
+            update(h, W("EZi", eo - 1024, 512), "MBi", mo - 2 * MW, E)
             if h == 0:
-                act(thr, W("MBi", 272 * (2 * t - 1) + 256, 1), F.Identity, bias=c(10))
+                act(thr, W("MBi", MW * (2 * t - 1) + 320, 1), F.Identity, bias=c(10), scale=32.0)
         if not last:
-            send("e%d" % z, [(W("EZ", eo, 1024), W("EZi", eo, 1024))], 3.2)
-        sm(R(y), ("I64k", W("EZ", eo + 512, 512)), ("I64k", E))
-        scan(W("Ks", o, 512), W("dk", o, 512), R(y), A.add, A.min)
+            send("e%d" % z, [(E, W("EZi", eo, 512))], 2.7)
+        scan(W("Ks", o, 512), W("dk", o, 512), E, A.add, A.min)
         tt(H("kr"), R("Ks", o + 7, o + 512, 8), H("key7"), A.add)
-        act(H("u"), ps9, F.Exp, bias=127 * LN2, scale=-LN2); act(b1, ps9, F.Relu, bias=16.0, scale=-3.75)
-        act(H("onp"), ps9, F.Sign, bias=-8.5); act(H("pw"), ps9, F.Exp, bias=-126 * LN2, scale=LN2)
-        sm(S(a, 0), ("Bh", H("u")), ("L2", b1)); tt(P, H("u"), S(a, 0), A.is_gt)
+        act(H("u"), ps, F.Exp, bias=123 * LN2, scale=-LN2); act(b1, ps, F.Relu, bias=1.0, scale=-3.75); act(H("ps4"), ps, F.Relu)
+        tt(P, H("u"), sm(("L2", b1), ("Bh", H("u"))), A.is_gt)
         if t > 0:
-            sm(S(b, 0), (If, W("MIi", io_ - 272 + 64, 64)), ("ImB", b1)); tt(ndv, S(b, 0), W("MIi", io_ - 272, 64), A.max)
-        cp(H("ndi"), ndv); ts(H("n"), H("ndi"), 4095, None, A.bitwise_and); ts(H("ps4"), ps9, 4.0, None, A.max)
+            record(ndv, "MIi", io_ - MW, "MBi", mo - 2 * MW, t - 1, b1)
+        cp(H("ndi"), ndv); ts(H("n"), H("ndi"), 4095, None, A.bitwise_and)
         sel, Sg = W("sel", o, 512), W("Sg", o, 512)
         if OPT["selv"]:
-            mm(rep(x, "I", P), each=True); tt(sel, R(x), E, A.mult)
+            tt(sel, sm(("I", P, 8), n=512), E, A.mult)
         else:
-            mm([(R(x), M("I"), E)] + rep(x, "I32", P)); act(sel, R(x), F.Relu, bias=-32.0)
-        sm(R(y), ("B", sel)); act(Sg, R(y), F.Sign, bias=c(2), scale=-1.0)
-        sm(S(a, 1), ("I", P), ("Ih", H("onp"))); act(pf, S(a, 1), F.Relu, bias=-0.5)
-        sm(S(b, 1), ("Ic", ONE), ("IBh", H("onp")), ("ImB", P)); tt(pc0, S(b, 1), H("kr"), A.is_le)
-        G, Ka, Kb, S1 = S(x, 0), S(a, 2), S(b, 2), S(x, 1)
-        sm(G, ("M2", Bh), ("B64", pc0), *[("D", R("Sg", o + d, o + 512, 8)) for d in range(8)])
-        sm(Ka, (If, H("kr")), ("IB", P), ("ImB", pc0), ("ImB", pf), stop=False)
-        sm(Kb, (If, H("key0")), ("IB", pc0), ("IB", pf), stop=False)
-        ts(H("flag"), G, c(7), None, A.is_gt); tt(H("key"), H("flag"), H("pw"), A.mult)
-        sm(S1, ("Bh", H("key"))); tt(Jh, H("key"), S1, A.is_gt)
-        sm(Ka, ("IB", Jh), start=False); act(H("PK"), Ka, F.Relu, bias=-BIG)
-        sm(Kb, ("BmB", Jh), start=False); act(H("PK2"), Kb, F.Relu, bias=-BIG)
-        sm(S(x, 2), ("I", P), ("M1", Jh)); act(Pp, S(x, 2), F.Relu)
-        sm(S(y, 0), ("I", pf), ("I", pc0), ("Bm1", Jh)); act(Pc, S(y, 0), F.Relu)
-        K, K37, OF = S(a, 3), S(b, 3), S(x, 3)
-        sm(K, ("Iv%d" % t, ONE), (Bf, H("PK")), (Bf, H("PK2")))
-        sm(K37, (If, ndv), (Bf37, H("PK")), (Bf37, H("PK2")))
-        sm(OF, ("I4k", b1), ("I4k", Pp))
-        cp(H("ki"), K); ts(H("cc"), H("ki"), 4095, None, A.bitwise_and); cp(H("cu"), H("cc"))
-        tt(H("t1"), H("n"), H("cc"), A.mult); ts(H("ta"), H("t1"), 5, None, A.arith_shift_right)
-        tt(H("t3"), K37, H("ta"), A.add); ts(H("t4"), H("t3"), 4095, None, A.bitwise_and); tt(H("t5"), OF, H("t4"), A.add)
-        ts(H("at"), H("t5"), 4096.0, None, A.min)
-        act(H("has"), K, F.Sign, bias=131072.0 * (t + 1) + 65535.5, scale=-1.0)
-        sm(S(y, 1), ("I", Pp), ("Ih", H("has"))); act(H("Ph"), S(y, 1), F.Relu, bias=-0.5)
-        tt(cand, K, H("Ph"), A.mult)
-        sm(S(y, 2), ("I260", ONE), ("I", ps9), ("Im1", H("ps4")), ("Bm4", Jh), ("Im256", Pp)); tt(H("ps2"), S(y, 2), H("ps4"), A.min)
+            act(sel, sm(("I", E), ("I64q", P, 8), n=512), F.Relu, bias=-64 * Q)
+        act(Sg, sm(("B", sel), n=512), F.Sign, bias=c(2), scale=-1.0 / Q)
+        act(pf, sm([("Im1", b1), ("I", P)]), F.Relu)
+        tt(pcx, sm([("T33", P), ("Imq", pf)]), H("kr"), A.is_le)
+        act(H("pwc"), sm([("I", H("ps4")), ("I300", P), ("Om300", pf), ("O300", pcx)]), F.Exp, bias=-425 * LN2, scale=LN2)
+        tt(H("ki"), sm([("I32", H("khi")), ("I", H("klo")), ("I60k", ONE), ("Im60k", pcx)]), H("kr"), A.min)
+        ts(H("kc"), H("ki"), 4095, None, A.bitwise_and); ts(H("kd"), H("ki"), 12, 15, A.arith_shift_right, A.bitwise_and)
+        G = sm([("MP", P)] + ([("Is", Bh)] if t else []), [("D", R("Sg", o + d, o + 512, 8)) for d in range(8)])
+        tt(H("key"), G, H("pwc"), A.min)
+        tt(Pp, H("key"), sm(("Bh", H("key"))), A.is_gt)
+        tt(PK, H("kc"), Pp, A.mult)
+        K = sm((Bf, PK))
+        K37 = sm([(If, ndv), ("I4M", b1)], ("I4M", Pp), (Bf37, PK))
+        tt(H("t1"), K, H("n"), A.mult)
+        if OPT["pd"][h]:
+            scan(H("cs"), W("dg", 0, 64), K, A.add, A.min); ts(W("cu", 4 * h, 4), R("cs", 64 * h + 15, 64 * h + 64, 16), c(12), None, A.add)
+        else:
+            cp(H("cu"), K)
+        ts(H("ta"), H("t1"), 5, None, A.arith_shift_right)
+        tt(H("t3"), K37, H("ta"), A.add); ts(H("t4"), H("t3"), 4095 | 19 << 22, None, A.bitwise_and)
+        ts(H("at"), H("t4"), 4096.0, None, A.min)
+        tt(dP, H("kd"), Pp, A.mult); act(Ph, dP, F.Sign)
+        act(Jh, sm([("Im1", P), ("I", Pp)]), F.Relu, acc=None if last else W("acc", 4 * h, 1))
+        tt(H("ps2"), sm([("I", ps), ("Im1", H("ps4")), ("O256", Pp), ("Bm4", Jh)]), H("ps4"), A.min)
+        tt(H("key2"), sm([("Ims", P), ("Os", Pp)]), H("key"), A.min)
+        act(H("J2h"), sm(("Hm", H("key2"))), F.Sign, bias=c(11))
+        act(H("vj"), sm([("Im256", b1), ("Im224", Pp), ("Bj", H("J2h"))]), F.Relu, bias=173.0)
+        act(Ro, sm([("Bk", pf), ("Bk", Jh)]), F.Copy)
+        if t:
+            tt(H("Bh2"), Bh, Pp, A.is_gt)
+            tt(H("val"), sm([("Om32", P), ("Bk", H("Bh2"))]), H("vj"), A.max)
+        tt(Tv, sm([("B2k", P), ("Im3k", pcx), ("B3k", Jh)]), H("val" if t else "vj"), A.min)
+        tt(H("neo"), Ro, Oo, A.is_equal)
+        act(On, sm([("I", Oo), ("Im1k", Pp), ("Im1k", H("neo"))]), F.Relu)
         if not last:
-            sm(S(y, 3), (If, ndv), ("ImB", b1), ("ImB", Pp)); tt(H("ndx"), S(y, 3), cand, A.max)
-        else:
-            cp(H("ndx"), cand)
-        ts(H("dd1"), H("ndx"), 12, 15, A.arith_shift_right, A.bitwise_and); cp(dvx, H("dd1"))
-        sm(S(x, 4), ("I127", ONE), ("Im127", Jh)); tt(H("key2"), S(x, 4), H("key"), A.min)
-        sm(S(y, 4), ("Bh", H("key2"))); tt(H("J2h"), H("key2"), S(y, 4), A.is_gt)
-        sm(S(x, 5), ("I32", Jh), ("Bj", H("J2h")))
-        sm(S(y, 5), ("Bk", pf), ("Bk", Jh)); act(Ro, S(y, 5), F.Copy)
-        if t == 0:
-            act(val, S(x, 5), F.Relu, bias=-15.0)
-        else:
-            act(H("vj"), S(x, 5), F.Relu, bias=-15.0); tt(H("Bh2"), Bh, Jh, A.is_gt)
-            sm(S(x, 6), ("I32", P), ("Bk", H("Bh2"))); act(H("vb"), S(x, 6), F.Relu, bias=-32.0)
-            tt(val, H("vb"), H("vj"), A.add)
-        if not last:
-            act(H("s1"), Jh, F.Copy, acc=W("acc", 4 * h, 1))
             if h == 1:
-                Ap = W(x, 448, 1)
-                sm(Ap, (Of, W("acc", 0, 1)), (Of, W("acc", 4, 1)))
-                cp(W("ai", 0, 1), Ap); ts(W("ai", 1, 1), W("ai", 0, 1), 7, None, A.bitwise_and)
-                ts(W("MB", mo + 256, 1), W("ai", 1, 1), 32.0, None, A.mult)
-            send("m%d" % z, [(W("MB", mo, 272), W("MBi", mo, 272)), (W("MI", io_, 136), W("MIi", io_, 136))], 2.7)
-        act(H("pw2"), H("ps2"), F.Exp, bias=-126 * LN2, scale=LN2); sm(S(y, 7), ("Bh", H("pw2")))
-        tt(H("mx"), H("pw2"), S(y, 7), A.is_gt)
-        sm(S(y, 6), ("I", H("ps2")), ("I264", H("mx"))); act(H("mp"), S(y, 6), F.Relu, bias=-264.0)
+                Ap = sm([(Of, W("acc", 0, 1)), (Of, W("acc", 4, 1))], n=1)
+                cp(W("ai", 0, 1), Ap); ts(W("ai", 1, 1), W("ai", 0, 1), 7, None, A.bitwise_and); cp(W("MB", mo + 320, 1), W("ai", 1, 1))
+            send("m%d" % z, [(W("MB", mo, MW), W("MBi", mo, MW)), (W("MI", io_, MW // 2), W("MIi", io_, MW // 2))], 2.8)
+        act(H("pw2"), H("ps2"), F.Exp, bias=-122 * LN2, scale=LN2)
+        act(H("mx"), sm(("Hm", H("pw2"))), F.Sign)
+        act(H("mp"), sm([("I", H("ps2")), ("I128", H("mx"))]), F.Relu, bias=-132.0)
         if last:
-            update(h, "EZ", eo, "MB", mo, eo + 2048)
-            zplane(eo + 2048, dvx)
-            ts(W("q1", o, 512), W("EZ", eo + 2048, 512), 17.0, -18.0, A.is_equal, A.mult)
-            sm(R(x), ("I", W("EZ", eo + 2048, 512)), ("I", W("q1", o, 512))); act(W("q2", o, 512), R(x), F.Identity, bias=-1.0)
+            Ef = W("EZ", eo + 1024, 512)
+            update(h, E, "MB", mo, Ef)
+            ts(W("q1", o, 512), Ef, 17 * Q, -18.0, A.is_equal, A.mult)
+            act(W("q2", o, 512), sm(("Iiq", Ef), ("I", W("q1", o, 512)), n=512), F.Identity, bias=-1.0)
+            ts(H("s4"), On, 17.0, -18.0, A.is_equal, A.mult); tt(H("O0"), H("s4"), On, A.add)
         win, g0 = R("X", 0, 4112), 1024 * h
-        for j in range(2):
-            q = g0 + 512 * j
-            act(W("xcr", q, 512), IND(win, W("cu", 64 * h + 32 * j, 32)), F.Copy)
-            tt(W("dd", q, 512), IND(win, W("at", 64 * h + 32 * j, 32)), W("xcr", q, 512), A.subtract)
-            act(W("ad", q, 512), W("dd", q, 512), F.Abs)
-        SM, UP = S(a, 4), S(b, 4)
-        sm(SM, ("I8k", b1), ("I8k", Pp), ("Im4k", H("has")), *[(R("Ws", 15 - k, 143 - k), R("ad", g0 + k, g0 + 1024, 16)) for k in range(16)])
+        mxv, lanes = R("mxs", g0 + 15, g0 + 1024, 16), lambda k: R("Ws", 15 - k, 143 - k)
+        if OPT["pd"][h]:
+            xc = H("xc"); part = [("I", mxv)]
+            (act(xc, IND(win, W("cu", 4 * h, 4)), F.Copy) if OPT["xcs"] else cp(xc, IND(win, W("cu", 4 * h, 4))))
+            for j in range(2):
+                y, o_ = W("dd", g0 + 512 * j, 512), IND(win, W("at", 64 * h + 32 * j, 32))
+                (act(y, o_, F.Copy) if OPT["ys"][j] else cp(y, o_))
+            for j in range(2):
+                act(W("ad", g0 + 512 * j, 512), planes([[("I", R("dd", g0 + k, g0 + 1024, 16)), ("Im1", xc)] for k in range(8 * j, 8 * j + 8)]), F.Abs)
+            SM = sm([("I8k", b1), ("I8k", Pp), ("Bm8k", Ph)], *[[(lanes(k), W("ad", g0 + 64 * k, 64)) for k in range(8 * j, 8 * j + 8)] for j in range(2)])
+        else:
+            xc = R("xcr", g0, g0 + 1024, 16); part = [("I", xc), ("I", mxv)]
+            for j in range(2):
+                q = g0 + 512 * j
+                act(W("xcr", q, 512), IND(win, W("cu", 64 * h + 32 * j, 32)), F.Copy)
+                tt(W("dd", q, 512), IND(win, W("at", 64 * h + 32 * j, 32)), W("xcr", q, 512), A.subtract)
+                act(W("ad", q, 512), W("dd", q, 512), F.Abs)
+            SM = sm([("I8k", b1), ("I8k", Pp), ("Bm8k", Ph)], [(lanes(k), R("ad", g0 + k, g0 + 1024, 16)) for k in range(16)])
         ts(H("clash"), SM, thr, None, A.is_le)
         tt(H("key3"), H("clash"), H("u"), A.mult)
-        sm(UP, ("Im255", ONE), ("B", H("mp")), ("Bm8", H("mx")), ("I264", H("Ph")), ("Bm264", H("clash")))
-        sm(S(a, 5), ("Bh", H("key3")))
-        tt(W("FO", fo, 64), UP, H("ps2"), A.max); tt(W("FO", fo + 64, 64), H("key3"), S(a, 5), A.is_gt)
+        tt(W("FO", fo, 64), sm([("Im251", ONE), ("B", H("mp")), ("I256", Ph)], ("Bm256", H("clash"))), H("ps2"), A.max)
+        tt(W("FO", fo + 64, 64), H("key3"), sm(("Bh", H("key3"))), A.is_gt)
         if not last:
             send("f%d" % z, [(W("FO", fo, 128), W("FI", fo, 128))], 2.2)
         scan(W("mxs", g0, 1024), R("m0"), W("dd", g0, 1024), A.add, A.max)
-        mxv, xc = R("mxs", g0 + 15, g0 + 1024, 16), R("xcr", g0, g0 + 1024, 16)
-        sm(S(b, 6), ("Imh", ONE), ("I2", xc), ("I", mxv))
-        act(H("rf"), S(b, 6), F.Identity, bias=12582912.0, scale=0.5); act(H("rb"), H("rf"), F.Identity, bias=-12582912.0)
-        sm(S(b, 5), ("I", xc), ("I", mxv), ("Im4k", H("has")), ("B4k", H("clash"))); act(H("Yb"), S(b, 5), F.Identity, bias=4096.0)
+        act(H("rf"), sm([("Imh", ONE), ("I" if OPT["pd"][h] else "I2", xc), ("I", mxv)]), F.Identity, bias=12582912.0, scale=0.5)
+        act(H("rb"), H("rf"), F.Identity, bias=-12582912.0)
+        act(H("Yb"), sm(part + [("Bm8k", Ph)], ("B4k", H("clash"))), F.Identity, bias=8192.0)
         if last:
             p9, Bo = W("FO", fo, 64), W("FO", fo + 64, 64)
-            sm(S(a, 0), ("I32", Pp), ("Bk", Bo)); act(H("vb"), S(a, 0), F.Relu, bias=-32.0)
-            mm([(R(y), M("Im33"), R("ONE")), (R(y), M("I32"), W("EZ", eo + 2560, 512))] + rep(y, "I", H("vb")))
-            tt(W("og", o, 512), R(y), W("q2", o, 512), A.max)
+            tt(H("vb"), sm(("Om32", Pp), ("Bk", Bo)), H("O0"), A.max)
+            tt(W("og", o, 512), sm([("I63", R("ONE")), ("Im2iq", Ef)], ("I", H("vb"), 8), n=512), W("q2", o, 512), A.min)
             store("yg%d" % h, W("og", o, 512), 2.2, "Y", (o, o + 512))
-            ts(H("s1"), p9, 1.0, -2.0, A.is_ge, A.add); ts(H("s2"), p9, -9.0, None, A.add); tt(H("op"), H("s1"), H("s2"), A.max)
-            ts(H("onp"), p9, 8.5, None, A.is_gt); tt(H("wc"), cand, H("onp"), A.mult); tt(H("nf"), ndv, H("wc"), A.max)
+            ts(H("s1"), p9, -1.0, -2.0, A.is_ge, A.add); ts(H("s2"), p9, -5.0, None, A.add); tt(H("op"), H("s1"), H("s2"), A.max)
+            act(H("s3"), p9, F.Relu, bias=1.0, scale=-3.75); record(H("nf"), "MI", io_, "MB", mo, t, H("s3"))
             ts(H("n"), H("nf"), 4095, None, A.bitwise_and); cp(H("yf"), H("n"))
             ts(H("dv1"), H("nf"), 12, 15, A.arith_shift_right, A.bitwise_and); ts(H("od"), H("dv1"), -1.0, None, A.add)
 
@@ -336,8 +368,7 @@ def build():
         visit(t, 0); visit(t, 1)
         for lo, n in (((0, 4), (4, 4)) if t == NV - 1 else ((0, 8),)):
             cur[0] = 1 if lo + n == 8 else 0
-            hs = W("B%d" % (2 + 4 * cur[0]), 384, n)
-            sm(hs, *[(R("Ww", 15 - k, 143 - k), R("Yb", 16 * lo + k, 16 * (lo + n), 16)) for k in range(16)])
+            hs = sm([(R("Ww", 15 - k, 143 - k), R("Yb", 16 * lo + k, 16 * (lo + n), 16)) for k in range(16)], n=n)
             cp(W("hi", lo, n), hs); ts(W("hi", 8 + lo, n), W("hi", lo, n), 31, None, A.bitwise_and)
             ts(W("hf", lo, n), hs, 500000.0, 4128.0, A.is_ge, A.mult); tt(W("hf", 8 + lo, n), W("hf", lo, n), W("cpos", lo, n), A.add)
             tt(W("hi", 16 + lo, n), W("hf", 8 + lo, n), W("hi", 8 + lo, n), A.add)
@@ -355,11 +386,11 @@ def depend(ops):
         for x in o["rd"]:
             deps[i].update(j for j, y, w in hist.get(x[1], []) if w and _meet(x, y))
         for x in o["wr"]:
-            deps[i].update(j for j, y, w in hist.get(x[1], []) if _meet(x, y) or (w and (o.get("grp") or ops[j].get("grp"))))
+            deps[i].update(j for j, y, w in hist.get(x[1], []) if _meet(x, y))
         for x in set(o["rd"]):
             hist.setdefault(x[1], []).append((i, x, False))
         for x in set(o["wr"]):
-            hist[x[1]] = [e for e in hist.get(x[1], []) if e[1] != x or ops[e[0]].get("grp")] + [(i, x, True)]
+            hist[x[1]] = [e for e in hist.get(x[1], []) if e[1] != x] + [(i, x, True)]
         deps[i].discard(i)
     return deps
 
@@ -385,7 +416,10 @@ def plan(ops, rounds):
     for _ in range(rounds):
         t0 = rs.rand() * max(best["fin"]); amp = OPT["amp"] * rs.rand()
         d2 = [x + (amp * float(y) if t0 <= st < t0 + OPT["span"] else 0.0) for x, y, st in zip(dp, rs.randn(n), best["start"])]
-        s = schedule(ops, deps, d2); sc2 = sum(replay(ops, s, h, sc) for h, sc in CASES)
+        s = schedule(ops, deps, d2)
+        if s is None:
+            continue
+        sc2 = sum(replay(ops, s, h, sc) for h, sc in CASES)
         if sc2 <= score:
             best, score, dp = s, sc2, d2
     return best
@@ -401,40 +435,62 @@ def schedule(ops, deps0, dp):
     pri = [0.0] * n
     for i in range(n - 1, -1, -1):
         pri[i] = ops[i]["cost"] + ops[i]["lat"] + max([pri[k] + HOP for k in succ[i]] + [0.0])
-    pri = [p + x - OPT["bias"] * o["h"] for p, x, o in zip(pri, dp, ops)]
-    banks = [set(x[1] for x in o["rd"] + o["wr"] if SCRATCH[x[1]][0] == "psum") for o in ops]
+    pri = [p + x - OPT["bias"] * o["h"] + o.get("up", 0.0) for p, x, o in zip(pri, dp, ops)]
+    tile = [o["tile"] for o in ops]
+    users = {}
+    for i in range(n):
+        if tile[i]:
+            users.setdefault(tile[i], []).append(i)
+    todo = {v: len(u) for v, u in users.items()}
+    outer = {v: set(j for i in u for j in deps0[i]) - set(u) for v, u in users.items()}
+    bank, held, lastuse = {}, [None] * 8, [{} for _ in range(8)]
     left = [len(d) for d in deps]
     ready = {e: [] for e in "VSPGY"}
     for i in range(n):
         if left[i] == 0:
             ready[ops[i]["eng"]].append(i)
     free = {e: 0.0 for e in ready}
-    fin, start, order, users, rdy = [0.0] * n, [0.0] * n, [], {}, [0.0] * n
+    fin, start, order, rdy, did = [0.0] * n, [0.0] * n, [], [0.0] * n, [False] * n
     while len(order) < n:
         pick = None
-        for e, lst in ready.items():
-            if not lst:
-                continue
-            st = {}
-            for i in lst:
-                s = max(free[e], rdy[i])
-                for b in banks[i]:
-                    for e2, j in users.get(b, {}).items():
-                        if e2 != e:
-                            s = max(s, fin[j] + HOP)
-                st[i] = s
-            best = max(lst, key=lambda i: pri[i])
-            cand = [i for i in lst if i == best or st[i] + ops[i]["cost"] <= st[best] + OPT["gap"]]
-            first = min(st[i] for i in cand)
-            i = max((i for i in cand if st[i] <= first + 0.03), key=lambda i: pri[i])
-            if pick is None or st[i] < pick[0]:
-                pick = (st[i], i)
-        s, i = pick
+        idle = [b for b in range(8) if held[b] is None]
+        for force in (False, True):
+            for e, lst in ready.items():
+                st, bk = {}, {}
+                for i in lst:
+                    s, v = max(free[e], rdy[i]), tile[i]
+                    if v:
+                        if v in bank:
+                            b = bank[v]
+                        elif idle and (force or len(idle) > OPT["keep"] or all(did[j] for j in outer[v])):
+                            b = min(idle, key=lambda b: max([fin[j] for e2, j in lastuse[b].items() if e2 != e] + [0.0]))
+                        else:
+                            continue
+                        bk[i] = b
+                        for e2, j in lastuse[b].items():
+                            if e2 != e:
+                                s = max(s, fin[j] + HOP)
+                    st[i] = s
+                if not st:
+                    continue
+                best = max(st, key=lambda i: pri[i])
+                cand = [i for i in st if i == best or st[i] + ops[i]["cost"] <= st[best] + OPT["gap"]]
+                first = min(st[i] for i in cand)
+                i = max((i for i in cand if st[i] <= first + 0.03), key=lambda i: pri[i])
+                if pick is None or st[i] < pick[0]:
+                    pick = (st[i], i, bk.get(i))
+            if pick:
+                break
+        if pick is None:
+            return None
+        s, i, b = pick
         e = ops[i]["eng"]
-        ready[e].remove(i)
-        for b in banks[i]:
-            deps[i].update(j for e2, j in users.get(b, {}).items() if e2 != e)
-            users.setdefault(b, {})[e] = i
+        ready[e].remove(i); did[i] = True
+        if b is not None:
+            v = tile[i]
+            deps[i].update(j for e2, j in lastuse[b].items() if e2 != e)
+            bank[v] = b; lastuse[b][e] = i; todo[v] -= 1
+            held[b] = v if todo[v] else None
         start[i] = s; free[e] = s + ops[i]["cost"]; fin[i] = free[e] + ops[i]["lat"]; order.append(i)
         for k in succ[i]:
             left[k] -= 1
@@ -466,7 +522,7 @@ def schedule(ops, deps0, dp):
     for i in order:
         if i in marked:
             k = pos[i][0]; tot[k] = tot.get(k, 0) + 1; val[i] = tot[k]
-    return dict(order=order, waits=waits, val=val, pos=pos, last=lastof, start=start, fin=fin)
+    return dict(order=order, waits=waits, val=val, pos=pos, last=lastof, start=start, fin=fin, bank=bank)
 
 
 PLAN = {}
@@ -488,14 +544,15 @@ def rank_program(g, core, T, topo):
     nxt, prv = T.cores[(rank + 1) % nr], T.cores[(rank - 1) % nr]
     rid, pid = topo.addr(nxt)[0], topo.addr(nxt)[1]
     eng_out, n_in = list(topo.engines(core, nxt)), len(topo.engines(prv, core))
-    Q = {"V": g.vector, "S": g.scalar, "P": g.tensor, "G": g, "Y": g.sync}
+    Qu = {"V": g.vector, "S": g.scalar, "P": g.tensor, "G": g, "Y": g.sync}
 
     def ap(x):
         if not _isap(x):
             return x
         if x[0] == "ind":
             return ap(x[1]).indirect(ap(x[2]))
-        return T[x[1]][:, x[2]:x[3]] if x[4] == 1 else T[x[1]][:, x[2]:x[3]:x[4]]
+        t = T["B%d" % s["bank"][x[1]]] if _psum(x) else T[x[1]]
+        return t[:, x[2]:x[3]] if x[4] == 1 else t[:, x[2]:x[3]:x[4]]
 
     def count(j):
         o = ops[j]
@@ -503,21 +560,23 @@ def rank_program(g, core, T, topo):
             return n_in
         return 16 if o["sem"] else s["val"][j]
 
+    def hbm(name, cols):
+        return T[name][:] if cols is None else T[name][:, cols[0]:cols[1]]
+
     sent = 0
     for i in s["order"]:
-        o = ops[i]; q = Q[o["eng"]]
+        o = ops[i]; q = Qu[o["eng"]]
         for j in s["waits"][i]:
             q.wait_ge(T.sem[s["pos"][j][0]], count(j))
         ins = None
         for name, args, kw in o["calls"]:
             if name == "load":
                 if o["eng"] == "G":
-                    ins = q.dma_start(ap(args[0]), T[args[1]][:], allow_slow_non_contiguous=True)
+                    ins = q.dma_start(ap(args[0]), hbm(args[1], args[2]), allow_slow_non_contiguous=True)
                 else:
-                    ins = q.dma_start(ap(args[0]), T[args[1]][:])
+                    ins = q.dma_start(ap(args[0]), hbm(args[1], args[2]))
             elif name == "store":
-                dst = T[args[1]][:] if args[2] is None else T[args[1][:2]][:, args[2][0]:args[2][1]]
-                ins = q.dma_start(dst, ap(args[0]))
+                ins = q.dma_start(hbm(args[1][:2], args[2]), ap(args[0]))
             elif name == "send":
                 masks = _share(eng_out, len(args[1]))
                 if len(masks) == 1:

@@ -4,36 +4,34 @@ from concourse.bass import DstId, RemoteDMATransfer
 from concourse.mybir import AluOpType as A, ActivationFunctionType as F
 
 NV = 5
-OPT = dict(selv=0, seed=0, amp=2.5, span=4.0, rounds=500, gap=0.2, pe=0.00045, hop=0.12, bias=2.0, call=0.5, lat=0.0, ov=0.01, osc=0.03, keep=2,
-           pd=(0, 0), xcs=1, ys=(1, 0))
+OPT = dict(selv=0, seed=0, amp=2.5, span=4.0, rounds=60, moves=30000, temp=0.06, gap=0.2, pe=0.00045, hop=0.12, bias=2.0, call=0.5, lat=0.0,
+           ov=0.01, osc=0.03, keep=2, pd=(0, 0), xcs=1, ys=(1, 0), rmw=0, zcs=0, xr=(4,), c2=1, cu=1, cx=2)
 XW = 8224
 LN2 = math.log(2.0)
-BIG = 2097152.0
 Q = 65536.0
-MW = 336
-SCALED = dict(I32=("I", 32), Iq=("I", Q), Imq=("I", -Q), Im1=("I", -1), I300=("I", 300), O300=("O", 300), Om300=("O", -300), Bh=("B", 0.5),
-              I60k=("I", 61440), Im60k=("I", -61440), I4M=("I", 4194304), I64q=("I", 64 * Q), Is=("I", 2.0 ** 124), O256=("O", 256), Bm4=("B", -4),
-              Os=("O", 2.0 ** 126), Ims=("I", -2.0 ** 126), Om32=("O", -32), I128=("I", 128), I8k=("I", 8192), Bm8k=("B", -8192), B4k=("B", 4096),
-              Im224=("I", -224), Im256=("I", -256), B2k=("B", 2048), Im3k=("I", -3072), B3k=("B", 3072), I3=("I", 3), Im64q=("I", -64 * Q),
-              Im251=("I", -251), I256=("I", 256), Bm256=("B", -256), Imh=("I", -0.5), I2=("I", 2), I4k=("I", 4096), ImB=("I", -BIG), Im1k=("I", -1024),
-              Iiq=("I", 1 / Q), Im2iq=("I", -2 / Q), I63=("I", 63), **{"Iv%d" % t: ("I", 131072 * (t + 1)) for t in range(NV)})
-MATS = ["I", "B", "O", "L2", "D", "MP", "T33", "Hm", "Bk", "Bj"] + list(SCALED)
+MW = 320
+SCALED = dict(I32=("I", 32), Iq=("I", Q), Imq=("I", -Q), Im1=("I", -1), Om256=("O", -256), Bh=("B", 0.5), Im60k=("I", -61440), I64q=("I", 64 * Q),
+              O256=("O", 256), Bm4=("B", -4), Bm1=("B", -1), Os=("O", 2.0 ** 126), Ims=("I", -2.0 ** 126), Bm8k=("B", -8192),
+              B4k=("B", 4096), Im224=("I", -224), Im256=("I", -256), I4=("I", 4), Im64q=("I", -64 * Q), Im251=("I", -251), I256=("I", 256),
+              Bm256=("B", -256), Imh=("I", -0.5), I2=("I", 2), I4k=("I", 4096), Iiq=("I", 1 / Q), Im2iq=("I", -2 / Q), Im33=("I", -33),
+              Bq=("B", Q), Bmq=("B", -Q), **{"Iv%d" % t: ("I", Q * (t + 1)) for t in range(1, NV)})
+MATS = ["I", "B", "O", "L2", "D", "Is", "MP", "MA", "T33", "Hm", "Bk", "Bj"] + list(SCALED)
 BF, F32, I32, U16 = "bfloat16", "float32", "int32", "uint16"
 SCRATCH = {}
 for _d, _l in ((BF, dict(X=XW, exr=1024, q1=1024, q2=1024, ne=1024, dl=1024, sel=1024, Sg=1024, Zn=1024, EZ=12 * 512, EZi=8 * 512, og=1024, MB=10 * MW,
                          MBi=8 * MW, FO=10 * 128, FI=8 * 128, F0=128, xcr=2048, dd=2048, ad=2048, mxs=2048, m0=1024, CM=128 * len(MATS), ONE=512,
-                         Ws=144, Ww=144, cpos=8)),
-               (F32, dict(hf=16, dk=1024, Ks=1024, MI=5 * MW, MIi=4 * MW, CF=512, col=16, cp0=8, thr=8, acc=8)),
-               (I32, dict(dnI=1024, coli=8, wtI=4, thI=4, hi=24, ai=8)), (U16, dict(at=128, cu=128, hu=8)),
-               (BF, dict.fromkeys("psr dvr dvx0 O0 u b1 pwc P pcx pf key Jh Pp key2 J2h vb Bh2 vj val neo ps4 ps2 pw2 mx mp clash key3 khi klo "
-                                  "Yb rb s1 s2 s3 s4 op od xc".split(), 128)),
-               (F32, dict.fromkeys("diff chi key7 kr sf yf rf cs".split(), 128)), (F32, dict(dg=64)),
+                         Ws=144, Ww=144, cpos=8, ramp=64)),
+               (F32, dict(hf=16, dk=1024, Ks=1024, MI=32 + 5 * 288, MIi=8 * 160, CF=512, col=16, cp0=8, thr=8, acc=8, dg=64)),
+               (I32, dict(dnI=1024, coli=8, wtI=4, thI=4, hi=24, ai=64)), (U16, dict(at=128, cu=128, hu=8, zu=8)),
+               (BF, dict.fromkeys("psr dvr dvx0 O0 u b1 pwc P pcx pf key Jh Pp key2 J2h vb Bh2 vj neo ps4 ps2 pw2 mx mp clash key3 khi klo "
+                                  "Yb rb s1 s2 s3 s4 op od xc zc zm Bh old keep new".split(), 128)),
+               (F32, dict.fromkeys("diff chi key7 kr sf yf rf cs zs".split(), 128)),
                (I32, dict.fromkeys("nmr n dv1 ki kc kd t1 ta t3 t4 nf ndi".split(), 128))):
     for _k, _w in _l.items():
         SCRATCH[_k] = ("sbuf", [128, _w], _d)
 for _b in range(8):
     SCRATCH["B%d" % _b] = ("psum", [128, 512], F32)
-LOADS = ["ps", "ex0", "dn0", "dv", "nm", "ex1", "xt", "dn1", "wt", "th"]
+LOADS = ["ps", "dv", "ex0", "dn0", "nm", "ex1", "xt", "dn1", "wt", "th"]
 STORES = ["yn", "yp", "yd", "yg0", "yg1", "yx0", "yx1"]
 SEMAPHORES = ["sV", "sS", "sP", "sG", "sent"] + ["l" + x for x in LOADS] + ["o" + x for x in STORES] + \
              ["%s%d" % (k, t) for k in "emf" for t in range(2 * NV - 2)]
@@ -47,6 +45,11 @@ def R(name, lo=0, hi=None, step=1):
 
 def W(name, lo, n):
     return ("ap", name, lo, lo + n, 1)
+
+
+def part(x, j, parts):
+    n = (x[3] - x[2]) // parts
+    return W(x[1], x[2] + j * n, n)
 
 
 def IND(win, off):
@@ -126,38 +129,43 @@ def build():
     def scan(out, d0, d1, op0, op1):
         add("V", [("tensor_tensor_scan", (out, d0, d1, 0.0, op0, op1), {})], [d0, d1], [out], vc(out, [d0, d1]))
 
-    def act(out, a, f, bias=None, scale=None, acc=None):
+    def act(out, a, f, bias=None, scale=None, acc=None, more=0.0):
         kw = {k: v for k, v in (("bias", bias), ("scale", scale), ("accum_out", acc)) if v is not None}
         c = _n(out) * 1.5 + 60 if a[0] == "ind" else _n(out)
-        add("S", [("activation", (out, a, f), kw)], [a, bias, scale], [out] + ([acc] if acc else []), OPT["osc"] + max(64, c) * 0.00083)
+        add("S", [("activation", (out, a, f), kw)], [a, bias, scale], [out] + ([acc] if acc else []), more + OPT["osc"] + max(64, c) * 0.00083)
 
-    def sm(*pieces, n=64):
+    def fetch(out, a, scalar):
+        act(out, a, F.Copy) if scalar else cp(out, a)
+
+    def fresh(n):
         tiles[0] += 1
-        name = "#%d" % tiles[0]
+        return W("#%d" % tiles[0], 0, n)
+
+    def sm(*pieces, n=64, gate=None):
+        whole = fresh(n)
         pieces = [p if isinstance(p, list) else [p] for p in pieces]
         pieces = [p for p in pieces if p]
         for a, piece in enumerate(pieces):
-            calls, rd, c = [], [], 0.0
+            calls, rd, c = [], [gate], 0.0
             for b, term in enumerate(piece):
                 l, r = M(term[0]) if isinstance(term[0], str) else term[0], term[1]
-                outs = [R(name, d, 512, 8) for d in range(8)] if len(term) == 3 else [W(name, 0, n)]
+                outs = [R(whole[1], d, 512, 8) for d in range(8)] if len(term) == 3 else [whole]
                 for d, o in enumerate(outs):
                     first, end = a == 0 and b == 0, a == len(pieces) - 1 and b == len(piece) - 1
                     alone = first and end
                     calls.append(("matmul", (o, l, r, alone or (first and d == 0), alone or (end and d == len(outs) - 1)), {}))
                     c += max(64, _n(r)) * (4 if SCRATCH[r[1]][2] == F32 else 1) * OPT["pe"]
                 rd += [l, r]
-            add("P", calls, rd, [W(name, 0, n)], c, lat=0.08)
-        return W(name, 0, n)
+            add("P", calls, rd, [whole], c, lat=0.08)
+        return whole
 
     def planes(groups):
-        tiles[0] += 1
-        name, calls, rd = "#%d" % tiles[0], [], []
+        whole, calls, rd = fresh(512), [], []
         for p, terms in enumerate(groups):
             for b, (m, r) in enumerate(terms):
-                calls.append(("matmul", (W(name, 64 * p, 64), M(m), r, b == 0, b == len(terms) - 1), {})); rd += [M(m), r]
-        add("P", calls, rd, [W(name, 0, 512)], 64 * len(calls) * OPT["pe"], lat=0.08)
-        return W(name, 0, 512)
+                calls.append(("matmul", (part(whole, p, 8), M(m), r, b == 0, b == len(terms) - 1), {})); rd += [M(m), r]
+        add("P", calls, rd, [whole], 64 * len(calls) * OPT["pe"], lat=0.08)
+        return whole
 
     def load(name, dst, lat, q="Y", cols=None):
         add(q, [("load", (dst, name[:2], cols), {})], [], [dst], 0.06 if q != "G" else 0.3, lat=lat, sem="l" + name,
@@ -171,18 +179,22 @@ def build():
 
     def iota(out, pat, base, cm):
         kw = {} if SCRATCH[out[1]][2] == I32 else {"allow_small_or_imprecise_dtypes": True}
-        add("G", [("iota", (out, pat, base, cm), kw)], [], [out], 0.13 + 2 * _n(out) * 0.00083, up=50.0)
+        add("G", [("iota", (out, pat, base, cm), kw)], [], [out], 0.13 + 2 * _n(out) * 0.00083)
+
+    def fill(out, v):
+        iota(out, [[0, _n(out)]], v, 0)
 
     c = lambda j: W("col", j, 1)
     ci = lambda j: W("coli", j, 1)
-    load("ps", R("psr"), 2.1); load("ex0", W("exr", 0, 512), 2.6, cols=(0, 512)); load("dn0", W("dnI", 0, 512), 3.5, cols=(0, 512))
-    load("dv", R("dvr"), 3.6); load("nm", R("nmr"), 3.8); load("ex1", W("exr", 512, 512), 4.3, cols=(512, 1024))
+    load("ps", R("psr"), 2.1); load("dv", R("dvr"), 2.2); load("ex0", W("exr", 0, 512), 2.7, cols=(0, 512))
+    load("dn0", W("dnI", 0, 512), 3.6, cols=(0, 512)); load("nm", R("nmr"), 3.8); load("ex1", W("exr", 512, 512), 4.3, cols=(512, 1024))
     load("xt", R("X", 0, 4096), 8.2); load("dn1", W("dnI", 512, 512), 9.2, cols=(512, 1024))
     iota(ci(0), [[1, 1]], 0, 1); iota(R("chi"), [[1, 8], [0, 16]], 0, 0); iota(R("diff"), [[-1, 128]], 0, 1); iota(R("cp0"), [[512, 8]], 0, 0)
     load("wt", W("wtI", 0, 1), 3.0, "G"); load("th", W("thI", 0, 1), 3.0, "G")
     ts(ci(1), ci(0), 15, None, A.bitwise_and); ts(ci(2), ci(0), 4, None, A.arith_shift_right)
     cp(W("col", 0, 2), W("coli", 1, 2))
     ts(M("B"), R("chi"), c(1), None, A.is_equal); ts(M("I"), R("diff"), 0.0, None, A.is_equal); tt(M("O"), M("B"), M("I"), A.subtract)
+    act(M("Is"), M("I"), F.Exp, bias=-200.0, scale=200.0 + 124 * LN2, more=1.3)
     ts(c(2), c(0), 1.5, None, A.add); ts(c(3), c(0), 1.0, None, A.add); ts(c(5), c(0), 0.5, -8.0, A.mult, A.add)
     ts(c(8), c(0), 32.0, None, A.mult); ts(R("cpos"), R("cp0"), c(8), None, A.add)
     ts(R("s1"), R("diff"), 0.0, 15.0 / 16, A.is_lt, A.mult); ts(R("s2"), M("I"), -1.0 / 16, -7.0 / 16, A.mult, A.add)
@@ -198,29 +210,32 @@ def build():
             act(M(nme), M(base), F.Copy, scale=float(v))
     act(M("Bk"), M("B"), F.Copy, scale=c(3)); act(M("Bj"), M("B"), F.Copy, scale=c(5))
     tt(M("Hm"), M("I"), M("Bh"), A.subtract)
-    ts(R("key"), M("O"), 33.0 * Q, None, A.mult); tt(M("T33"), R("key"), M("Iq"), A.add)
+    ts(R("key"), M("I"), -32.0 * Q, 33.0 * Q, A.mult, A.add); tt(M("T33"), R("key"), M("B"), A.mult)
+    ts(R("neo"), M("I"), 272.0, 112.0, A.mult, A.add); tt(M("MA"), R("neo"), M("B"), A.mult)
     Bf, Bf37, Of, If = (W("CF", 128 * j, 128) for j in range(4))
-    act(Bf, M("B"), F.Copy); act(Bf37, M("B"), F.Copy, scale=37.0); ms(Of, 1.0); ms(R("ONE"), 1.0); act(If, M("I"), F.Copy)
-    ms(R("Ws"), 0.0); cp(R("Ws", 15, 143, 16), R("CM", M("B")[2], M("B")[3], 16))
-    ts(R("key2"), R("Ws", 15, 143), 4.0, None, A.mult); tt(R("key3"), R("key2"), M("I"), A.add); ts(M("MP"), R("key3"), 2.0 ** 62, 2.0 ** 62, A.mult, A.mult)
+    act(Bf, M("B"), F.Copy); act(Bf37, M("B"), F.Copy, scale=37.0); fill(Of, 1); fill(R("ONE"), 1); act(If, M("I"), F.Copy)
+    fill(R("Ws"), 0); cp(R("Ws", 15, 143, 16), R("CM", M("B")[2], M("B")[3], 16))
+    ts(R("key2"), R("Ws", 15, 143), 2.0 ** 63, 2.0 ** 63, A.mult, A.mult); tt(M("MP"), R("key2"), M("Is"), A.add)
     ts(c(9), W("wtI", 0, 1), 32.0, None, A.add); ts(R("Ww"), R("Ws"), c(9), None, A.mult)
     ts(c(10), W("thI", 0, 1), -8192.0, None, A.add)
-    ms(c(11), 2.0 ** -60); ts(c(11), c(11), -2.0 ** -63, None, A.mult)
-    iota(W("sf", 0, 64), [[0, 4], [1, 16]], 0, 0); ts(ci(3), ci(0), 1, None, A.add); ts(ci(4), ci(3), 15, None, A.bitwise_and); cp(c(13), ci(4))
-    ts(W("kr", 0, 64), W("sf", 0, 64), c(0), 16384.0, A.is_equal, A.mult); ts(W("yf", 0, 64), W("sf", 0, 64), c(13), -8192.0, A.is_equal, A.mult)
-    tt(R("dg"), W("kr", 0, 64), W("yf", 0, 64), A.add); ts(c(12), c(0), 14.5, 8192.0, A.is_lt, A.mult)
-    ms(R("m0"), 0.0); ms(R("m0", 0, 1024, 16), -1024.0); ms(R("X", 4096, 4112), 0.0)
-    for z in range(2 * NV - 2):
-        ms(W("MB", MW * z + 320, 16), 0.0); ms(W("MI", MW // 2 * z + 128, MW // 2 - 128), 0.0)
+    ts(c(11), W("ONE", 0, 1), -2.0 ** -60, 2.0 ** -63, A.mult, A.mult)
+    iota(W("rf", 0, 64), [[0, 4], [1, 16]], 0, 0); ts(ci(3), ci(0), 1, None, A.add); ts(ci(4), ci(3), 15, None, A.bitwise_and); cp(c(13), ci(4))
+    ts(W("cs", 0, 64), W("rf", 0, 64), c(0), 16384.0, A.is_equal, A.mult); ts(W("yf", 0, 64), W("rf", 0, 64), c(13), -8192.0, A.is_equal, A.mult)
+    tt(R("dg"), W("cs", 0, 64), W("yf", 0, 64), A.add); ts(c(12), c(0), 14.5, 8192.0, A.is_lt, A.mult)
+    iota(R("ramp"), [[8, 64]], 0, 0)
+    fill(W("m0", 0, 512), 0); fill(W("m0", 512, 512), 0); ms(R("m0", 0, 1024, 16), -1024.0); fill(R("X", 4096, 4112), 0); fill(W("MI", 0, 32), 0)
     ONE = W("ONE", 0, 64)
-    ts(R("s1"), R("psr"), 0.0, -4.0, A.is_lt, A.mult); ts(R("s2"), R("psr"), 5.0, None, A.add); tt(R("F0"), R("s1"), R("s2"), A.add)
+    ts(R("s1"), R("psr"), 0.0, 4.0, A.is_ge, A.mult); tt(R("F0"), R("s1"), R("psr"), A.add)
     act(R("sf"), R("dvr"), F.Identity, bias=4096.0, scale=4096.0)
-    ts(R("op"), R("psr"), 0.0, None, A.is_ge); ts(R("od"), R("dvr"), 1.0, None, A.add); tt(R("dvx0"), R("op"), R("od"), A.mult)
+    ts(R("op"), R("psr"), 16.0, 16.0, A.mult, A.add); ts(R("od"), R("dvr"), 1.0, None, A.add); tt(R("dvx0"), R("op"), R("od"), A.min)
 
     def marks(h, tile):
         for d in range(8):
             ts(R("Zn", 512 * h + d, 512 * h + 512, 8), tile, float(d + 1), 32 * Q, A.is_equal, A.mult)
         return W("Zn", 512 * h, 512)
+
+    def names(z):
+        return 32 + 288 * (z // 2) + 160 * (z % 2)
 
     for h in range(2):
         cur[0] = h
@@ -228,32 +243,53 @@ def build():
         tt(W("Ks", o + 1, 511), W("dnI", o, 511), W("dnI", o + 1, 511), A.subtract)
         act(W("dk", o + 1, 511), W("Ks", o + 1, 511), F.Identity, bias=-4096.0); ms(R("dk", o, o + 512, 8), 4194304.0)
         ts(H("key7"), R("dnI", o + 7, o + 512, 8), 32768.0, None, A.add)
-        ts(H("ta"), R("dnI", o, o + 512, 8), 5, None, A.arith_shift_right); ts(H("khi"), H("ta"), 128.0, None, A.add)
+        ts(H("ta"), R("dnI", o, o + 512, 8), 5, None, A.arith_shift_right); cp(H("khi"), H("ta"))
         ts(H("t4"), R("dnI", o, o + 512, 8), 31, None, A.bitwise_and); cp(H("klo"), H("t4"))
         ex, q1, Z = W("exr", o, 512), W("q1", o, 512), marks(h, H("dvx0"))
         ts(q1, ex, -2.0, 18.0, A.is_equal, A.mult)
-        tt(W("EZ", o, 512), sm(("Iq", R("ONE")), ("Iq", ex), ("Iq", q1), n=512), Z, A.max)
+        tt(W("EZ", o, 512), sm([("Iq", R("ONE")), ("Iq", ex), ("Iq", q1)], n=512), Z, A.max)
         act(W("dl", o, 512), sm([("I", ex), ("I", q1), ("Iiq", Z)], n=512), F.Relu, bias=-31.0)
         act(H("O0"), sm([("I", R("dl", o + d, o + 512, 8)) for d in range(8)]), F.Copy)
-        tt(W("MI", MW // 2 * h, 64), H("sf"), H("nmr"), A.add)
+        tt(W("MI", names(h), 64), H("sf"), H("nmr"), A.add)
 
-    def update(h, E, mb, mo, out):
-        Rr, Tv, dP = (W(mb, mo + 64 * j, 64) for j in range(3))
-        ne, dl = W("ne", 512 * h, 512), W("dl", 512 * h, 512)
+    def diagonal(out, tile, tmp):
+        scan(tmp, R("dg"), tile, A.add, A.min); ts(out, R(tmp[1], tmp[2] + 15, tmp[3], 16), c(12), None, A.add)
+
+    def update(h, E, mb, mo, out, final=False):
+        Rr, Tv, dP, Ph = (W(mb, mo + 64 * j, 64) for j in range(4))
+        ne, dl, n = W("ne", 512 * h, 512), W("dl", 512 * h, 512), OPT["cu"]
         tt(ne, sm(("Iq", Rr, 8), n=512), E, A.is_equal)
-        act(dl, sm(("I3", E), ("Imq", Tv, 8), n=512), F.Relu, bias=-64 * Q)
-        Z = marks(h, dP)
-        tt(out, sm(("I", E), ("Im64q", ne), ("Im1", dl), n=512), Z, A.max)
+        strip = sm(("I4", E), ("Imq", Tv, 8), n=512, gate=Rr)
+        Z = None if OPT["rmw"] or final else marks(h, dP)
+        for j in range(n):
+            act(part(dl, j, n), part(strip, j, n), F.Relu, bias=32 * Q)
+        for j in range(n):
+            rest = sm([("I", part(E, j, n)), ("Im64q", part(ne, j, n))], ("Im1", part(dl, j, n)), n=512 // n)
+            if Z:
+                tt(part(out, j, n), rest, part(Z, j, n), A.max)
+            else:
+                act(part(out, j, n), rest, F.Relu)
+        if Z:
+            return
+        zu, zc, zm = W("zu", 4 * h, 4), W("zc", 64 * h, 64), W("zm", 64 * h, 64)
+        diagonal(zu, sm([("I", R("ramp")), ("B", dP), ("Bm1", Ph)]), W("zs", 64 * h, 64))
+        if final:
+            return
+        act(zm, Ph, F.Copy, scale=32 * Q)
+        fetch(zc, IND(out, zu), OPT["zcs"])
+        tt(IND(out, zu), zc, zm, A.add)
 
-    def record(out, mi, io_, mb, mo, t, b1):
-        tt(out, sm([(If, W(mi, io_ + 64, 64)), ("I4k", W(mb, mo + 128, 64)), ("Iv%d" % t, W(mb, mo + 192, 64))], ("ImB", b1)), W(mi, io_, 64), A.max)
+    def record(out, ndv, PK, mb, mo, t, b1):
+        tt(out, sm([(If, PK), ("I4k", W(mb, mo + 128, 64)), ("Iv%d" % t if t else "Iq", W(mb, mo + 192, 64))], ("Im64q", b1)), ndv, A.max)
 
     def visit(t, h):
         cur[0] = h
         last, z, o = t == NV - 1, 2 * t + h, 512 * h
         H = lambda name: W(name, 64 * h, 64)
-        eo, mo, io_, fo = 512 * z, MW * z, MW // 2 * z, 128 * z
-        ps, Bh = (H("F0"), None) if t == 0 else (W("FI", fo - 256, 64), W("FI", fo - 192, 64))
+        eo, mo, io_, fo = 512 * z, MW * z, names(z), 128 * z
+        ps, Bh = H("F0") if t == 0 else W("FI", fo - 256, 64), H("Bh")
+        if t:
+            tt(Bh, W("FI", fo - 192, 64), sm(("Bh", W("FI", fo - 192, 64))), A.is_gt)
         ndv, PK = W("MI", io_, 64), W("MI", io_ + 64, 64)
         Ro, Tv, dP, Ph, On = (W("MB", mo + 64 * j, 64) for j in range(5))
         P, Jh, Pp, pf, pcx, b1, E = H("P"), H("Jh"), H("Pp"), H("pf"), H("pcx"), H("b1"), W("EZ", eo, 512)
@@ -263,104 +299,115 @@ def build():
             Oo, thr = W("MBi", mo - 2 * MW + 256, 64), W("thr", t, 1)
             update(h, W("EZi", eo - 1024, 512), "MBi", mo - 2 * MW, E)
             if h == 0:
-                act(thr, W("MBi", MW * (2 * t - 1) + 320, 1), F.Identity, bias=c(10), scale=32.0)
+                act(thr, W("MIi", 160 * (2 * t - 1), 1), F.Identity, bias=c(10), scale=32.0)
         if not last:
             send("e%d" % z, [(E, W("EZi", eo, 512))], 2.7)
-        scan(W("Ks", o, 512), W("dk", o, 512), E, A.add, A.min)
-        tt(H("kr"), R("Ks", o + 7, o + 512, 8), H("key7"), A.add)
-        act(H("u"), ps, F.Exp, bias=123 * LN2, scale=-LN2); act(b1, ps, F.Relu, bias=1.0, scale=-3.75); act(H("ps4"), ps, F.Relu)
-        tt(P, H("u"), sm(("L2", b1), ("Bh", H("u"))), A.is_gt)
+        first = fresh(512)
+        scan(first, W("dk", o, 512), E, A.add, A.min)
+        tt(H("kr"), R(first[1], 7, 512, 8), H("key7"), A.add)
+        low = 0.0 if t else 1.0
+        act(H("u"), ps, F.Exp, bias=(123 - low) * LN2, scale=-LN2); act(b1, ps, F.Relu, bias=1.0 - low, scale=-3.75 if t else -1.0)
+        act(H("ps4"), ps, F.Relu, bias=low)
+        tt(P, H("u"), sm([("L2", b1), ("Bh", H("u"))]), A.is_gt)
         if t > 0:
-            record(ndv, "MIi", io_ - MW, "MBi", mo - 2 * MW, t - 1, b1)
+            record(ndv, W("MIi", 160 * (z - 2) + 32, 64), W("MIi", 160 * (z - 2) + 96, 64), "MBi", mo - 2 * MW, t - 1, b1)
         cp(H("ndi"), ndv); ts(H("n"), H("ndi"), 4095, None, A.bitwise_and)
-        sel, Sg = W("sel", o, 512), W("Sg", o, 512)
-        if OPT["selv"]:
-            tt(sel, sm(("I", P, 8), n=512), E, A.mult)
+        sel, Sg, n = W("sel", o, 512), W("Sg", o, 512), OPT["c2"]
+        if OPT["selv"] and t:
+            row = sm(("I", P, 8), n=512)
         else:
-            act(sel, sm(("I", E), ("I64q", P, 8), n=512), F.Relu, bias=-64 * Q)
-        act(Sg, sm(("B", sel), n=512), F.Sign, bias=c(2), scale=-1.0 / Q)
+            row = sm([("I", E)] if t else [("Iq", W("exr", o, 512)), ("Iq", W("q1", o, 512))], ("I64q", P, 8), n=512, gate=ps)
+        for j in range(n):
+            if OPT["selv"] and t:
+                tt(part(sel, j, n), part(row, j, n), part(E, j, n), A.mult)
+            else:
+                act(part(sel, j, n), part(row, j, n), F.Relu, bias=(low - 64) * Q)
+        for j in range(n):
+            act(part(Sg, j, n), sm(("B", part(sel, j, n)), n=512 // n), F.Sign, bias=c(2), scale=-1.0 / Q)
         act(pf, sm([("Im1", b1), ("I", P)]), F.Relu)
         tt(pcx, sm([("T33", P), ("Imq", pf)]), H("kr"), A.is_le)
-        act(H("pwc"), sm([("I", H("ps4")), ("I300", P), ("Om300", pf), ("O300", pcx)]), F.Exp, bias=-425 * LN2, scale=LN2)
-        tt(H("ki"), sm([("I32", H("khi")), ("I", H("klo")), ("I60k", ONE), ("Im60k", pcx)]), H("kr"), A.min)
+        act(H("pwc"), sm([("I", H("ps4")), ("I256", P), ("Om256", pf), ("O256", pcx)]), F.Exp, bias=-381 * LN2, scale=LN2)
+        tt(H("ki"), sm([("I32", H("khi")), ("I", H("klo")), ("Iq", ONE), ("Im60k", pcx)]), H("kr"), A.min)
         ts(H("kc"), H("ki"), 4095, None, A.bitwise_and); ts(H("kd"), H("ki"), 12, 15, A.arith_shift_right, A.bitwise_and)
-        G = sm([("MP", P)] + ([("Is", Bh)] if t else []), [("D", R("Sg", o + d, o + 512, 8)) for d in range(8)])
+        G = sm([("MP", P)] + ([("Is", Bh)] if t else []), [("D", R("Sg", o + d, o + 512, 8)) for d in range(8)], gate=part(sel, 0, n))
         tt(H("key"), G, H("pwc"), A.min)
         tt(Pp, H("key"), sm(("Bh", H("key"))), A.is_gt)
         tt(PK, H("kc"), Pp, A.mult)
         K = sm((Bf, PK))
-        K37 = sm([(If, ndv), ("I4M", b1)], ("I4M", Pp), (Bf37, PK))
-        tt(H("t1"), K, H("n"), A.mult)
+        K37 = sm([(If, ndv), ("I64q", b1)], ("I64q", Pp), (Bf37, PK), gate=H("key"))
         if OPT["pd"][h]:
-            scan(H("cs"), W("dg", 0, 64), K, A.add, A.min); ts(W("cu", 4 * h, 4), R("cs", 64 * h + 15, 64 * h + 64, 16), c(12), None, A.add)
+            tt(H("t1"), K, H("n"), A.mult); diagonal(W("cu", 4 * h, 4), K, H("cs"))
         else:
-            cp(H("cu"), K)
+            cp(H("cu"), K); tt(H("t1"), K, H("n"), A.mult)
         ts(H("ta"), H("t1"), 5, None, A.arith_shift_right)
         tt(H("t3"), K37, H("ta"), A.add); ts(H("t4"), H("t3"), 4095 | 19 << 22, None, A.bitwise_and)
         ts(H("at"), H("t4"), 4096.0, None, A.min)
         tt(dP, H("kd"), Pp, A.mult); act(Ph, dP, F.Sign)
-        act(Jh, sm([("Im1", P), ("I", Pp)]), F.Relu, acc=None if last else W("acc", 4 * h, 1))
-        tt(H("ps2"), sm([("I", ps), ("Im1", H("ps4")), ("O256", Pp), ("Bm4", Jh)]), H("ps4"), A.min)
+        act(Jh, sm([("Im1", P), ("I", Pp)]), F.Relu, acc=None if last else W("acc", h, 1))
+        tt(H("ps2"), sm(([("I", ps), ("Im1", H("ps4"))] if t else []) + [("O256", Pp), ("Bm4", Jh)]), H("ps4"), A.min)
         tt(H("key2"), sm([("Ims", P), ("Os", Pp)]), H("key"), A.min)
         act(H("J2h"), sm(("Hm", H("key2"))), F.Sign, bias=c(11))
-        act(H("vj"), sm([("Im256", b1), ("Im224", Pp), ("Bj", H("J2h"))]), F.Relu, bias=173.0)
-        act(Ro, sm([("Bk", pf), ("Bk", Jh)]), F.Copy)
+        act(H("vj"), sm([("Im256", b1), ("Im256", pf), ("Im224", Pp), ("Bj", H("J2h"))]), F.Relu, bias=301.0)
+        Rp = sm([("Bk", pf), ("Bk", Jh)]); act(Ro, Rp, F.Copy); tt(H("neo"), Rp, Oo, A.is_equal)
         if t:
-            tt(H("Bh2"), Bh, Pp, A.is_gt)
-            tt(H("val"), sm([("Om32", P), ("Bk", H("Bh2"))]), H("vj"), A.max)
-        tt(Tv, sm([("B2k", P), ("Im3k", pcx), ("B3k", Jh)]), H("val" if t else "vj"), A.min)
-        tt(H("neo"), Ro, Oo, A.is_equal)
-        act(On, sm([("I", Oo), ("Im1k", Pp), ("Im1k", H("neo"))]), F.Relu)
+            act(H("Bh2"), sm([("I", Bh), ("Im1", Pp)]), F.Relu)
+        tt(Tv, sm([("MA", P), ("Im256", pcx), ("Im256", Pp)] + ([("Bk", H("Bh2"))] if t else [])), H("vj"), A.max)
+        act(On, sm([("I", Oo), ("Im256", Pp), ("Im256", H("neo"))]), F.Relu)
         if not last:
             if h == 1:
-                Ap = sm([(Of, W("acc", 0, 1)), (Of, W("acc", 4, 1))], n=1)
-                cp(W("ai", 0, 1), Ap); ts(W("ai", 1, 1), W("ai", 0, 1), 7, None, A.bitwise_and); cp(W("MB", mo + 320, 1), W("ai", 1, 1))
-            send("m%d" % z, [(W("MB", mo, MW), W("MBi", mo, MW)), (W("MI", io_, MW // 2), W("MIi", io_, MW // 2))], 2.8)
+                Ap = sm((Of, W("acc", 0, 2)), n=2)
+                ts(W("ai", 0, 32), W("ONE", 0, 32), part(Ap, 0, 2), part(Ap, 1, 2), A.mult, A.add)
+                ts(W("ai", 32, 32), W("ai", 0, 32), 7, None, A.bitwise_and); cp(W("MI", io_ - 32, 32), W("ai", 32, 32))
+            send("m%d" % z, [(W("MB", mo, MW), W("MBi", mo, MW)), (W("MI", io_ - 32, 160), W("MIi", 160 * z, 160))], 2.8)
         act(H("pw2"), H("ps2"), F.Exp, bias=-122 * LN2, scale=LN2)
         act(H("mx"), sm(("Hm", H("pw2"))), F.Sign)
-        act(H("mp"), sm([("I", H("ps2")), ("I128", H("mx"))]), F.Relu, bias=-132.0)
+        act(H("mp"), sm([("I", H("ps2")), ("I256", H("mx"))]), F.Relu, bias=-260.0)
         if last:
             Ef = W("EZ", eo + 1024, 512)
-            update(h, E, "MB", mo, Ef)
+            update(h, E, "MB", mo, Ef, True)
             ts(W("q1", o, 512), Ef, 17 * Q, -18.0, A.is_equal, A.mult)
-            act(W("q2", o, 512), sm(("Iiq", Ef), ("I", W("q1", o, 512)), n=512), F.Identity, bias=-1.0)
-            ts(H("s4"), On, 17.0, -18.0, A.is_equal, A.mult); tt(H("O0"), H("s4"), On, A.add)
+            act(W("q2", o, 512), sm([("Iiq", Ef), ("I", W("q1", o, 512))], n=512), F.Identity, bias=-1.0)
+            ts(H("s4"), On, 17.0, -18.0, A.is_equal, A.mult); act(H("O0"), sm([("I", H("s4")), ("I", On)]), F.Identity, bias=63.0)
+            tt(W("og", o, 512), sm([("Im2iq", Ef), ("I", H("O0"), 8)], n=512), W("q2", o, 512), A.min)
+            tried = IND(W("og", o, 512), W("zu", 4 * h, 4))
+            fetch(H("zc"), tried, True)
         win, g0 = R("X", 0, 4112), 1024 * h
         mxv, lanes = R("mxs", g0 + 15, g0 + 1024, 16), lambda k: R("Ws", 15 - k, 143 - k)
+        dd, ad, xcr, n = W("dd", g0, 1024), W("ad", g0, 1024), W("xcr", g0, 1024), OPT["cx"]
         if OPT["pd"][h]:
-            xc = H("xc"); part = [("I", mxv)]
-            (act(xc, IND(win, W("cu", 4 * h, 4)), F.Copy) if OPT["xcs"] else cp(xc, IND(win, W("cu", 4 * h, 4))))
+            xc = H("xc"); big = [("I", mxv)]
+            fetch(xc, IND(win, W("cu", 4 * h, 4)), OPT["xcs"])
             for j in range(2):
-                y, o_ = W("dd", g0 + 512 * j, 512), IND(win, W("at", 64 * h + 32 * j, 32))
-                (act(y, o_, F.Copy) if OPT["ys"][j] else cp(y, o_))
+                fetch(part(dd, j, 2), IND(win, part(H("at"), j, 2)), OPT["ys"][j])
             for j in range(2):
-                act(W("ad", g0 + 512 * j, 512), planes([[("I", R("dd", g0 + k, g0 + 1024, 16)), ("Im1", xc)] for k in range(8 * j, 8 * j + 8)]), F.Abs)
-            SM = sm([("I8k", b1), ("I8k", Pp), ("Bm8k", Ph)], *[[(lanes(k), W("ad", g0 + 64 * k, 64)) for k in range(8 * j, 8 * j + 8)] for j in range(2)])
+                act(part(ad, j, 2), planes([[("I", R("dd", g0 + k, g0 + 1024, 16)), ("Im1", xc)] for k in range(8 * j, 8 * j + 8)]), F.Abs)
+            sums = [[(lanes(k), part(ad, k, 16)) for k in range(8 * j, 8 * j + 8)] for j in range(2)]
         else:
-            xc = R("xcr", g0, g0 + 1024, 16); part = [("I", xc), ("I", mxv)]
-            for j in range(2):
-                q = g0 + 512 * j
-                act(W("xcr", q, 512), IND(win, W("cu", 64 * h + 32 * j, 32)), F.Copy)
-                tt(W("dd", q, 512), IND(win, W("at", 64 * h + 32 * j, 32)), W("xcr", q, 512), A.subtract)
-                act(W("ad", q, 512), W("dd", q, 512), F.Abs)
-            SM = sm([("I8k", b1), ("I8k", Pp), ("Bm8k", Ph)], [(lanes(k), R("ad", g0 + k, g0 + 1024, 16)) for k in range(16)])
-        ts(H("clash"), SM, thr, None, A.is_le)
-        tt(H("key3"), H("clash"), H("u"), A.mult)
-        tt(W("FO", fo, 64), sm([("Im251", ONE), ("B", H("mp")), ("I256", Ph)], ("Bm256", H("clash"))), H("ps2"), A.max)
-        tt(W("FO", fo + 64, 64), H("key3"), sm(("Bh", H("key3"))), A.is_gt)
+            xc = R("xcr", g0, g0 + 1024, 16); big = [("I", xc), ("I", mxv)]
+            for j in range(n):
+                act(part(xcr, j, n), IND(win, part(H("cu"), j, n)), F.Copy)
+                tt(part(dd, j, n), IND(win, part(H("at"), j, n)), part(xcr, j, n), A.subtract)
+                act(part(ad, j, n), part(dd, j, n), F.Abs)
+            sums = [[(lanes(k), R("ad", g0 + k, g0 + 1024, 16)) for k in range(16)]]
+        ts(H("clash"), sm([("I64q", b1), ("I64q", Pp), ("Bm8k", Ph)], *sums, gate=part(dd, 0, 2)), thr, None, A.is_le)
+        tt(W("FO", fo + 64, 64), H("clash"), H("u"), A.mult)
+        tt(W("FO", fo, 64), sm([("Im251", ONE), ("B", H("mp")), ("I256", Ph)], ("Bm256", H("clash")), gate=part(ad, 0, 2)), H("ps2"), A.max)
         if not last:
             send("f%d" % z, [(W("FO", fo, 128), W("FI", fo, 128))], 2.2)
-        scan(W("mxs", g0, 1024), R("m0"), W("dd", g0, 1024), A.add, A.max)
+        scan(W("mxs", g0, 1024), R("m0"), dd, A.add, A.max)
         act(H("rf"), sm([("Imh", ONE), ("I" if OPT["pd"][h] else "I2", xc), ("I", mxv)]), F.Identity, bias=12582912.0, scale=0.5)
         act(H("rb"), H("rf"), F.Identity, bias=-12582912.0)
-        act(H("Yb"), sm(part + [("Bm8k", Ph)], ("B4k", H("clash"))), F.Identity, bias=8192.0)
+        if t in OPT["xr"]:
+            act(H("Yb"), sm(big), F.Copy)
+        else:
+            act(H("Yb"), sm(big + [("Bm8k", Ph)], ("B4k", H("clash")), gate=part(ad, 1, 2)), F.Identity, bias=8192.0)
         if last:
-            p9, Bo = W("FO", fo, 64), W("FO", fo + 64, 64)
-            tt(H("vb"), sm(("Om32", Pp), ("Bk", Bo)), H("O0"), A.max)
-            tt(W("og", o, 512), sm([("I63", R("ONE")), ("Im2iq", Ef)], ("I", H("vb"), 8), n=512), W("q2", o, 512), A.min)
+            p9, Bo = W("FO", fo, 64), H("Bh")
+            tt(Bo, W("FO", fo + 64, 64), sm(("Bh", W("FO", fo + 64, 64))), A.is_gt)
+            tt(H("vb"), sm([("Im33", ONE), ("I32", Ph)], ("Bk", Bo), gate=H("clash")), H("zc"), A.max); cp(tried, H("vb"))
             store("yg%d" % h, W("og", o, 512), 2.2, "Y", (o, o + 512))
             ts(H("s1"), p9, -1.0, -2.0, A.is_ge, A.add); ts(H("s2"), p9, -5.0, None, A.add); tt(H("op"), H("s1"), H("s2"), A.max)
-            act(H("s3"), p9, F.Relu, bias=1.0, scale=-3.75); record(H("nf"), "MI", io_, "MB", mo, t, H("s3"))
+            act(H("s3"), p9, F.Relu, bias=1.0, scale=-3.75); record(H("nf"), ndv, PK, "MB", mo, t, H("s3"))
             ts(H("n"), H("nf"), 4095, None, A.bitwise_and); cp(H("yf"), H("n"))
             ts(H("dv1"), H("nf"), 12, 15, A.arith_shift_right, A.bitwise_and); ts(H("od"), H("dv1"), -1.0, None, A.add)
 
@@ -370,10 +417,21 @@ def build():
             cur[0] = 1 if lo + n == 8 else 0
             hs = sm([(R("Ww", 15 - k, 143 - k), R("Yb", 16 * lo + k, 16 * (lo + n), 16)) for k in range(16)], n=n)
             cp(W("hi", lo, n), hs); ts(W("hi", 8 + lo, n), W("hi", lo, n), 31, None, A.bitwise_and)
-            ts(W("hf", lo, n), hs, 500000.0, 4128.0, A.is_ge, A.mult); tt(W("hf", 8 + lo, n), W("hf", lo, n), W("cpos", lo, n), A.add)
-            tt(W("hi", 16 + lo, n), W("hf", 8 + lo, n), W("hi", 8 + lo, n), A.add)
-            ts(W("hu", lo, n), W("hi", 16 + lo, n), -512.0 * lo, None, A.add)
-            cp(IND(R("X", 512 * lo, XW), W("hu", lo, n)), W("rb", 16 * lo, 16 * n))
+            if t in OPT["xr"]:
+                tt(W("hi", 16 + lo, n), W("cpos", lo, n), W("hi", 8 + lo, n), A.add)
+                ts(W("hu", lo, n), W("hi", 16 + lo, n), -512.0 * lo, None, A.add)
+                col = IND(W("X", 512 * lo, 512 * n), W("hu", lo, n))
+                fetch(W("old", 16 * lo, 16 * n), col, True)
+                for h in range(lo // 4, (lo + n) // 4):
+                    H, Ph = lambda name: W(name, 64 * h, 64), W("MB", MW * (2 * t + h) + 192, 64)
+                    tt(H("keep"), sm([("Iq", ONE), ("Bmq", Ph)], ("Bq", H("clash")), gate=H("rb")), H("old"), A.min)
+                    tt(H("new"), sm([("Imq", ONE), ("Bq", Ph), ("I", H("rb"))], ("Bmq", H("clash"))), H("keep"), A.max)
+                cp(col, W("new", 16 * lo, 16 * n))
+            else:
+                ts(W("hf", lo, n), hs, 500000.0, 4128.0, A.is_ge, A.mult); tt(W("hf", 8 + lo, n), W("hf", lo, n), W("cpos", lo, n), A.add)
+                tt(W("hi", 16 + lo, n), W("hf", 8 + lo, n), W("hi", 8 + lo, n), A.add)
+                ts(W("hu", lo, n), W("hi", 16 + lo, n), -512.0 * lo, None, A.add)
+                cp(IND(R("X", 512 * lo, XW), W("hu", lo, n)), W("rb", 16 * lo, 16 * n))
             if n == 4:
                 store("yx%d" % cur[0], W("X", 512 * lo, 2048), 3.0, "YS"[cur[0]], (512 * lo, 512 * lo + 2048))
     store("yp", R("op"), 2.0, "Y"); store("yn", R("yf"), 2.0, "Y"); store("yd", R("od"), 2.0, "Y")
@@ -406,15 +464,15 @@ def replay(ops, s, hop, sc):
     return max(fin.values())
 
 
-CASES = ((0.12, {}), (0.05, {}), (0.25, {"L": 1.5, "G": 2.0}), (0.12, {"P": 1.5}), (0.12, {"V": 1.25, "S": 1.25, "P": 1.25}))
+CASES = ((0.14, {}), (0.2, {"V": 1.25, "S": 1.25, "P": 1.25, "L": 1.2}))
 
 
-def plan(ops, rounds):
+def plan(ops, rounds, moves):
     deps, rs, n = depend(ops), np.random.RandomState(OPT["seed"]), len(ops)
     dp = [0.0] * n
     best = schedule(ops, deps, dp); score = sum(replay(ops, best, h, sc) for h, sc in CASES)
     for _ in range(rounds):
-        t0 = rs.rand() * max(best["fin"]); amp = OPT["amp"] * rs.rand()
+        t0 = rs.rand() * max(best["start"]); amp = OPT["amp"] * rs.rand()
         d2 = [x + (amp * float(y) if t0 <= st < t0 + OPT["span"] else 0.0) for x, y, st in zip(dp, rs.randn(n), best["start"])]
         s = schedule(ops, deps, d2)
         if s is None:
@@ -422,12 +480,11 @@ def plan(ops, rounds):
         sc2 = sum(replay(ops, s, h, sc) for h, sc in CASES)
         if sc2 <= score:
             best, score, dp = s, sc2, d2
-    return best
+    return tie(ops, deps, *refine(ops, deps, best["order"], best["bank"], moves, rs)) if moves else best
 
 
-def schedule(ops, deps0, dp):
+def schedule(ops, deps, dp):
     n, HOP = len(ops), OPT["hop"]
-    deps = [set(d) for d in deps0]
     succ = [[] for _ in ops]
     for i in range(n):
         for j in deps[i]:
@@ -442,7 +499,7 @@ def schedule(ops, deps0, dp):
         if tile[i]:
             users.setdefault(tile[i], []).append(i)
     todo = {v: len(u) for v, u in users.items()}
-    outer = {v: set(j for i in u for j in deps0[i]) - set(u) for v, u in users.items()}
+    outer = {v: set(j for i in u for j in deps[i]) - set(u) for v, u in users.items()}
     bank, held, lastuse = {}, [None] * 8, [{} for _ in range(8)]
     left = [len(d) for d in deps]
     ready = {e: [] for e in "VSPGY"}
@@ -488,7 +545,6 @@ def schedule(ops, deps0, dp):
         ready[e].remove(i); did[i] = True
         if b is not None:
             v = tile[i]
-            deps[i].update(j for e2, j in lastuse[b].items() if e2 != e)
             bank[v] = b; lastuse[b][e] = i; todo[v] -= 1
             held[b] = v if todo[v] else None
         start[i] = s; free[e] = s + ops[i]["cost"]; fin[i] = free[e] + ops[i]["lat"]; order.append(i)
@@ -497,20 +553,127 @@ def schedule(ops, deps0, dp):
             rdy[k] = max(rdy[k], free[e] if e == "P" and ops[k]["eng"] == "P" else fin[i] + HOP)
             if left[k] == 0:
                 ready[ops[k]["eng"]].append(k)
-    pos, cnt, seen, done, waits, marked = {}, {}, {e: {} for e in ready}, {}, {}, set()
+    return dict(tie(ops, deps, order, bank), start=start)
+
+
+def refine(ops, deps, order, bank, moves, rs):
+    n, eng = len(ops), [o["eng"] for o in ops]
+    anc, need, users = [0] * n, [], {}
+    for i in range(n):
+        keep, far = [], 0
+        for j in sorted(deps[i], reverse=True):
+            if not far >> j & 1:
+                keep.append(j)
+            far |= anc[j] | 1 << j
+        anc[i] = far; need.append(keep)
     for i in order:
-        o = ops[i]; e = o["eng"]
+        if ops[i]["tile"]:
+            users.setdefault(ops[i]["tile"], []).append(i)
+    first = {u[0]: v for v, u in users.items()}
+    for u in users.values():
+        for a, b in zip(u, u[1:]):
+            if eng[a] != eng[b] and not anc[b] >> a & 1:
+                need[b].append(a)
+    cost = [[o["cost"] * sc.get(o["eng"], 1.0) for o in ops] for h, sc in CASES]
+    lat = [[o["lat"] * (sc.get("L", 1.0) if o.get("remote") else 1.0) + h for o in ops] for h, sc in CASES]
+
+    def arcs(order, bank):
+        last, prv, at, timed, plain = {}, [-1] * n, {}, [None] * n, [None] * n
+        for i in order:
+            e = eng[i]; prv[i] = at.get(e, -1); at[e] = i
+            a = need[i]
+            if i in first:
+                b = bank[first[i]]
+                if b in last:
+                    a = a + users[last[b]]
+                last[b] = first[i]
+            plain[i] = a
+            timed[i] = [j for j in a if eng[j] != "P"] if e == "P" else a
+        return prv, timed, plain
+
+    def times(order, prv, timed, c, old=None, lo=0):
+        co, la = cost[c], lat[c]
+        end, fin = (old[0][:], old[1][:]) if old else ([0.0] * (n + 1), [0.0] * n)
+        for i in order[lo:]:
+            t = end[prv[i]]
+            for j in timed[i]:
+                if fin[j] > t:
+                    t = fin[j]
+            t += co[i]; end[i] = t; fin[i] = t + la[i]
+        return end, fin
+
+    prv, timed, plain = arcs(order, bank)
+    tm = [times(order, prv, timed, c) for c in range(len(CASES))]
+    score = sum(max(t[1]) for t in tm)
+    best = (score, order, bank)
+    for it in range(moves):
+        c = rs.randint(len(CASES)); end, fin = tm[c]
+        i, path = fin.index(max(fin)), []
+        while i >= 0:
+            p = prv[i]
+            if p >= 0 and end[p] >= end[i] - cost[c][i] - 1e-9:
+                path.append((p, i, True)); i = p
+            else:
+                j = max(timed[i], key=lambda j: fin[j]) if timed[i] else -1
+                if j >= 0 and j not in need[i]:
+                    path.append((j, i, False))
+                i = j
+        a, b, queue = path[rs.randint(len(path))]
+        order2, bank2 = order, bank
+        if queue:
+            for _ in range(rs.randint(4) if rs.randint(2) else 0):
+                if prv[a] >= 0:
+                    a = prv[a]
+            if "up" in ops[b]:
+                continue
+            lo, hi, after, x = order.index(a), order.index(b), {a}, b
+            while prv[x] != a:
+                x = prv[x]; after.add(x)
+            for k in order[lo:hi + 1]:
+                if k not in after and (any(j in after for j in plain[k]) or (k != b and prv[k] in after)):
+                    after.add(k)
+            if b in after:
+                continue
+            seg = order[lo:hi + 1]
+            order2 = order[:lo] + [k for k in seg if k not in after] + [k for k in seg if k in after] + order[hi + 1:]
+        else:
+            v, pos = first[b], {x: k for k, x in enumerate(order)}
+            lo, hi = pos[b], max(pos[k] for k in users[v])
+            busy = set(bank[w] for w, u in users.items() if pos[u[0]] <= hi and max(pos[k] for k in u) >= lo)
+            free = [x for x in range(8) if x not in busy]
+            if not free:
+                continue
+            bank2 = dict(bank); bank2[v] = free[rs.randint(len(free))]
+        prv2, timed2, plain2 = arcs(order2, bank2)
+        tm2 = [times(order2, prv2, timed2, c, tm[c], lo) for c in range(len(CASES))]
+        sc2 = sum(max(t[1]) for t in tm2)
+        if sc2 <= score - OPT["temp"] * (1 - it / moves) * math.log(1 - rs.rand()):
+            order, bank, prv, timed, plain, tm, score = order2, bank2, prv2, timed2, plain2, tm2, sc2
+            if score < best[0]:
+                best = (score, order, bank)
+    return best[1], best[2]
+
+
+def tie(ops, deps, order, bank):
+    pos, cnt, seen, done, waits, marked = {}, {}, {e: {} for e in "VSPGY"}, {}, {}, set()
+    rank, lastuse, begun = {}, [{} for _ in range(8)], set()
+    for k, i in enumerate(order):
+        o = ops[i]; e = o["eng"]; rank[i] = k
         key = o["sem"] or "s" + e
         cnt[key] = cnt.get(key, 0) + 1; pos[i] = (key, cnt[key])
-        w = []
-        for j in sorted(deps[i], key=lambda j: -start[j]):
+        need, w = set(deps[i]), []
+        if o["tile"]:
+            use = lastuse[bank[o["tile"]]]
+            need.update(j for e2, j in use.items() if e2 != e or o["tile"] not in begun)
+            use[e] = i; begun.add(o["tile"])
+        for j in sorted(need, key=lambda j: -rank[j]):
             if e == "P" and ops[j]["eng"] == "P":
                 continue
-            k, v = pos[j]
-            if seen[e].get(k, 0) < v:
+            k2, v = pos[j]
+            if seen[e].get(k2, 0) < v:
                 w.append(j); marked.add(j)
-                for k2, v2 in done[j].items():
-                    seen[e][k2] = max(seen[e].get(k2, 0), v2)
+                for k3, v3 in done[j].items():
+                    seen[e][k3] = max(seen[e].get(k3, 0), v3)
         waits[i] = w
         done[i] = {} if o.get("remote") else dict(seen[e])
         done[i][key] = cnt[key]
@@ -522,7 +685,7 @@ def schedule(ops, deps0, dp):
     for i in order:
         if i in marked:
             k = pos[i][0]; tot[k] = tot.get(k, 0) + 1; val[i] = tot[k]
-    return dict(order=order, waits=waits, val=val, pos=pos, last=lastof, start=start, fin=fin, bank=bank)
+    return dict(order=order, waits=waits, val=val, pos=pos, last=lastof, bank=bank)
 
 
 PLAN = {}
@@ -538,7 +701,7 @@ def rank_program(g, core, T, topo):
     if rank is None:
         return
     if not PLAN:
-        PLAN["ops"] = build(); PLAN["s"] = plan(PLAN["ops"], OPT["rounds"])
+        PLAN["ops"] = build(); PLAN["s"] = plan(PLAN["ops"], OPT["rounds"], OPT["moves"])
     ops, s = PLAN["ops"], PLAN["s"]
     nr = len(T.cores)
     nxt, prv = T.cores[(rank + 1) % nr], T.cores[(rank - 1) % nr]

@@ -4,37 +4,41 @@ from concourse.bass import DstId, RemoteDMATransfer
 from concourse.mybir import AluOpType as A, ActivationFunctionType as F
 
 NV = 5
-OPT = dict(selv=0, seed=0, amp=2.5, span=4.0, rounds=60, moves=30000, temp=0.06, gap=0.2, pe=0.00045, hop=0.12, bias=2.0, call=0.5, lat=0.0,
-           ov=0.01, osc=0.03, keep=2, pd=(0, 0), xcs=1, ys=(1, 0), rmw=0, zcs=0, xr=(4,), c2=1, cu=1, cx=2)
+OPT = dict(selv=0, seed=0, amp=0.8, span=6.0, rounds=4000, moves=40000, temp=0.06, heat=0.15, slow=1.05, cap=7, pe=0.00056, hop=0.19, bias=3.0, call=0.5,
+           lat=0.0, ov=0.01, osc=0.03, pd=(0, 0), xcs=1, ys=(1, 1), xr=(4,), c2=2, cu=1, cx=2, z1s=(1, 1), zos=1, rbv=0, absv=0, mg=1, lat0=1.9, kb=0.0048,
+           foldm=0, hd=1, nv=8, bhs=0, f2=(1,) * 8)
 XW = 8224
 LN2 = math.log(2.0)
 Q = 65536.0
-MW = 320
-SCALED = dict(I32=("I", 32), Iq=("I", Q), Imq=("I", -Q), Im1=("I", -1), Om256=("O", -256), Bh=("B", 0.5), Im60k=("I", -61440), I64q=("I", 64 * Q),
-              O256=("O", 256), Bm4=("B", -4), Bm1=("B", -1), Os=("O", 2.0 ** 126), Ims=("I", -2.0 ** 126), Bm8k=("B", -8192),
-              B4k=("B", 4096), Im224=("I", -224), Im256=("I", -256), I4=("I", 4), Im64q=("I", -64 * Q), Im251=("I", -251), I256=("I", 256),
-              Bm256=("B", -256), Imh=("I", -0.5), I2=("I", 2), I4k=("I", 4096), Iiq=("I", 1 / Q), Im2iq=("I", -2 / Q), Im33=("I", -33),
-              Bq=("B", Q), Bmq=("B", -Q), **{"Iv%d" % t: ("I", Q * (t + 1)) for t in range(1, NV)})
-MATS = ["I", "B", "O", "L2", "D", "Is", "MP", "MA", "T33", "Hm", "Bk", "Bj"] + list(SCALED)
+MK = 128 * Q
+EW = 704
+BLOCK = dict(Oh=(0, 0.5), I128=(128, 0), I32=(32, 0), Iq=(Q, 0), I256=(256, 0), Om256=(0, -256), Tp=(132 * Q, 0), Tb=(-131 * Q, 0), Bh=(0.5, 0.5),
+             M1=(-57344, 65536), I60k=(61440, 0), Im128=(-128, 0), Iiq=(1 / Q, 0), Ifl=(2.0 ** 26, 0), M3=(2.0 ** 26, -0.25),
+             M2=(-4, 256), I4=(4, 0), Os=(0, 2.0 ** 126), Hm=(0.5, -0.5), Im1536=(-1536, 0), Im2k=(-2048, 0),
+             Im256=(-256, 0), Im1=(-1, 0), I512=(512, 0), M4=(-512, 512), Im512=(-512, 0), Oq=(0, Q), Bmh=(-1 / MK, -1 / MK),
+             Bm8h=(-8192 / MK, -8192 / MK), I256h=(256 / MK, 0), Im251=(-251, 0), Bm256=(-256, -256), B4k=(4096, 4096), I4k=(4096, 0),
+             Im64q=(-64 * Q, 0), **{"Iv%d" % t: (Q * (t + 1) / MK, 0) for t in range(NV)},
+             Imh=(-0.5, 0), Imq=(-Q, 0), Im129=(-129, 0), Bq=(Q, Q), Bmq=(-Q, -Q), Bqh=(Q / MK, Q / MK), Bmqh=(-Q / MK, -Q / MK), Om2k=(0, -2048))
+MATS = ["I", "B", "O", "L3", "D", "Is", "MP", "Bk", "Bkm", "Bkq", "Bj"] + list(BLOCK)
 BF, F32, I32, U16 = "bfloat16", "float32", "int32", "uint16"
 SCRATCH = {}
-for _d, _l in ((BF, dict(X=XW, exr=1024, q1=1024, q2=1024, ne=1024, dl=1024, sel=1024, Sg=1024, Zn=1024, EZ=12 * 512, EZi=8 * 512, og=1024, MB=10 * MW,
-                         MBi=8 * MW, FO=10 * 128, FI=8 * 128, F0=128, xcr=2048, dd=2048, ad=2048, mxs=2048, m0=1024, CM=128 * len(MATS), ONE=512,
+for _d, _l in ((BF, dict(X=XW, exr=1024, q1=1024, ne=1024, dl=1024, sel=1024, Sg=1024, Zn=1024, EZ=10 * EW, Z1=2 * EW, Z2=2 * EW, og=1024,
+                         FO=10 * 128, FI=8 * 128, F0=128, xs=2048, xcr=2048, dd=2048, ad=2048, mxs=2048, m0=1024, CM=128 * len(MATS), ONE=512,
                          Ws=144, Ww=144, cpos=8, ramp=64)),
-               (F32, dict(hf=16, dk=1024, Ks=1024, MI=32 + 5 * 288, MIi=8 * 160, CF=512, col=16, cp0=8, thr=8, acc=8, dg=64)),
-               (I32, dict(dnI=1024, coli=8, wtI=4, thI=4, hi=24, ai=64)), (U16, dict(at=128, cu=128, hu=8, zu=8)),
-               (BF, dict.fromkeys("psr dvr dvx0 O0 u b1 pwc P pcx pf key Jh Pp key2 J2h vb Bh2 vj neo ps4 ps2 pw2 mx mp clash key3 khi klo "
-                                  "Yb rb s1 s2 s3 s4 op od xc zc zm Bh old keep new".split(), 128)),
-               (F32, dict.fromkeys("diff chi key7 kr sf yf rf cs zs".split(), 128)),
-               (I32, dict.fromkeys("nmr n dv1 ki kc kd t1 ta t3 t4 nf ndi".split(), 128))):
+               (F32, dict(hf=16, dk=1024, MI=32 + 5 * 288, MIi=8 * 160, PZ=320, CF=5 * 128, col=16, cp0=8, thr=8, acc=8, dg=64)),
+               (I32, dict(dnI=1024, coli=8, wtI=4, thI=4, hi=24, ai=64)), (U16, dict(cu=8, hu=8, zu=8, at=128, cw=128)),
+               (BF, dict.fromkeys("psr dvr dvx0 u b1 pwc P pcx key Jh Pp key2 J2h vb Bh2 vj neo ps4 ps2 pw2 mx mp clash khi klo "
+                                  "Yb rb s1 s2 s3 s4 op od xc zc zm Bh old keep new Tv Tw zero Wb Ro".split(), 128)),
+               (F32, dict.fromkeys("diff chi key7 kr sf yf rf cs zs t1 nx0 hw dh".split(), 128)),
+               (I32, dict.fromkeys("nmr n dv1 ki kc kd ta t3 t4 nf ri".split(), 128))):
     for _k, _w in _l.items():
         SCRATCH[_k] = ("sbuf", [128, _w], _d)
 for _b in range(8):
     SCRATCH["B%d" % _b] = ("psum", [128, 512], F32)
 LOADS = ["ps", "dv", "ex0", "dn0", "nm", "ex1", "xt", "dn1", "wt", "th"]
 STORES = ["yn", "yp", "yd", "yg0", "yg1", "yx0", "yx1"]
-SEMAPHORES = ["sV", "sS", "sP", "sG", "sent"] + ["l" + x for x in LOADS] + ["o" + x for x in STORES] + \
-             ["%s%d" % (k, t) for k in "emf" for t in range(2 * NV - 2)]
+SEMAPHORES = ["sV", "sS", "sP", "sG"] + ["l" + x for x in LOADS] + ["o" + x for x in STORES] + \
+             ["%s%s%d" % (x, k, t) for x in ("", "x") for k in "emf" for t in range(2 * NV - 2)]
 
 
 def R(name, lo=0, hi=None, step=1):
@@ -141,17 +145,17 @@ def build():
         tiles[0] += 1
         return W("#%d" % tiles[0], 0, n)
 
-    def sm(*pieces, n=64, gate=None):
-        whole = fresh(n)
+    def sm(*pieces, n=64, gate=None, onto=None, stay=False):
+        whole = onto or fresh(n)
         pieces = [p if isinstance(p, list) else [p] for p in pieces]
         pieces = [p for p in pieces if p]
         for a, piece in enumerate(pieces):
             calls, rd, c = [], [gate], 0.0
             for b, term in enumerate(piece):
                 l, r = M(term[0]) if isinstance(term[0], str) else term[0], term[1]
-                outs = [R(whole[1], d, 512, 8) for d in range(8)] if len(term) == 3 else [whole]
+                outs = [R(whole[1], d, 512, 8) for d in range(term[2])] if len(term) == 3 else [whole]
                 for d, o in enumerate(outs):
-                    first, end = a == 0 and b == 0, a == len(pieces) - 1 and b == len(piece) - 1
+                    first, end = a == 0 and b == 0 and not onto, a == len(pieces) - 1 and b == len(piece) - 1 and not stay
                     alone = first and end
                     calls.append(("matmul", (o, l, r, alone or (first and d == 0), alone or (end and d == len(outs) - 1)), {}))
                     c += max(64, _n(r)) * (4 if SCRATCH[r[1]][2] == F32 else 1) * OPT["pe"]
@@ -174,8 +178,10 @@ def build():
     def store(name, src, lat, q, cols=None):
         add(q, [("store", (src, name, cols), {})], [src], [], 0.06, lat=lat, sem="o" + name)
 
-    def send(sem, pairs, lat):
-        add("G", [("send", (sem, pairs), {})], [p[0] for p in pairs], [p[1] for p in pairs], OPT["call"], lat=lat + OPT["lat"], sem=sem, remote=True)
+    def send(sem, srcs, dst, alu, lat):
+        add("G", [("send", (sem, srcs, dst, alu), {})], srcs, [W("@" + sem, 0, 1)], OPT["call"], issue=True)
+        kb = len(srcs) * _n(dst) * (4 if SCRATCH[dst[1]][2] == F32 else 2) / 8
+        add("D", [], [W("@" + sem, 0, 1)] + srcs, [dst], kb * OPT["kb"], lat=lat, sem=sem, remote=True)
 
     def iota(out, pat, base, cm):
         kw = {} if SCRATCH[out[1]][2] == I32 else {"allow_small_or_imprecise_dtypes": True}
@@ -183,6 +189,9 @@ def build():
 
     def fill(out, v):
         iota(out, [[0, _n(out)]], v, 0)
+
+    def diag(out, a, v):
+        add("G", [("affine_select", (out, a, [[-1, 128]], A.not_equal, float(v), 0, 1), {})], [a], [out], 0.17 + 256 * 0.00083)
 
     c = lambda j: W("col", j, 1)
     ci = lambda j: W("coli", j, 1)
@@ -195,35 +204,52 @@ def build():
     cp(W("col", 0, 2), W("coli", 1, 2))
     ts(M("B"), R("chi"), c(1), None, A.is_equal); ts(M("I"), R("diff"), 0.0, None, A.is_equal); tt(M("O"), M("B"), M("I"), A.subtract)
     act(M("Is"), M("I"), F.Exp, bias=-200.0, scale=200.0 + 124 * LN2, more=1.3)
-    ts(c(2), c(0), 1.5, None, A.add); ts(c(3), c(0), 1.0, None, A.add); ts(c(5), c(0), 0.5, -8.0, A.mult, A.add)
-    ts(c(8), c(0), 32.0, None, A.mult); ts(R("cpos"), R("cp0"), c(8), None, A.add)
-    ts(R("s1"), R("diff"), 0.0, 15.0 / 16, A.is_lt, A.mult); ts(R("s2"), M("I"), -1.0 / 16, -7.0 / 16, A.mult, A.add)
-    tt(R("op"), R("s1"), R("s2"), A.add); tt(R("od"), R("op"), M("B"), A.mult); ts(M("L2"), R("od"), 2.0 ** 62, 2.0 ** 61, A.mult, A.mult)
+    act(c(2), c(0), F.Identity, bias=1.5); act(c(3), c(0), F.Identity, bias=1.0); act(c(5), c(0), F.Identity, bias=-16.0, scale=0.5)
+    act(c(8), c(0), F.Copy, scale=32.0); act(R("cpos"), R("cp0"), F.Identity, bias=c(8))
+    ts(R("s1"), R("diff"), 0.0, 15.0 / 16, A.is_lt, A.mult); ts(R("s2"), R("s1"), -7.0 / 16, 2.0 ** 62, A.add, A.mult)
+    ts(R("op"), M("O"), 2.0 ** 61, None, A.mult); tt(M("L3"), R("op"), R("s2"), A.mult)
     ts(R("s3"), R("diff"), -1.0, None, A.is_equal); tt(R("vj"), R("s3"), M("B"), A.mult); tt(R("s4"), M("I"), R("vj"), A.subtract)
     ts(M("D"), R("s4"), 2.0 ** 62, 2.0 ** 61, A.mult, A.mult)
-    for j, (nme, (base, v)) in enumerate(SCALED.items()):
+    fill(R("zero"), 0)
+    late = list(BLOCK).index("Tb" if OPT["mg"] == 3 else "M2" if OPT["mg"] == 2 else "I4k")
+    for j, (nme, (a, b)) in enumerate(BLOCK.items()):
+        base, v = ("I", a) if b == 0 else ("O", b) if a == 0 else ("B", b)
         if abs(v) > 1e29:
             ts(M(nme), M(base), v / 2.0 ** 63, 2.0 ** 63, A.mult, A.mult)
-        elif j % 3 == 0:
+        elif b == 0 and j >= late and OPT["mg"]:
+            diag(M(nme), R("zero"), a)
+        elif j % 2 == 0 and j < OPT["nv"]:
             ts(M(nme), M(base), float(v), None, A.mult)
         else:
             act(M(nme), M(base), F.Copy, scale=float(v))
-    act(M("Bk"), M("B"), F.Copy, scale=c(3)); act(M("Bj"), M("B"), F.Copy, scale=c(5))
-    tt(M("Hm"), M("I"), M("Bh"), A.subtract)
-    ts(R("key"), M("I"), -32.0 * Q, 33.0 * Q, A.mult, A.add); tt(M("T33"), R("key"), M("B"), A.mult)
-    ts(R("neo"), M("I"), 272.0, 112.0, A.mult, A.add); tt(M("MA"), R("neo"), M("B"), A.mult)
-    Bf, Bf37, Of, If = (W("CF", 128 * j, 128) for j in range(4))
-    act(Bf, M("B"), F.Copy); act(Bf37, M("B"), F.Copy, scale=37.0); fill(Of, 1); fill(R("ONE"), 1); act(If, M("I"), F.Copy)
+        if a and b and a != b:
+            diag(M(nme), M(nme), a)
+    act(M("Bk"), M("B"), F.Copy, scale=c(3)); act(M("Bj"), M("B"), F.Copy, scale=c(5)); act(M("Bkm"), M("Bk"), F.Copy, scale=-1.0)
+    act(M("Bkq"), M("Bk"), F.Copy, scale=Q)
+    Bfh, Bf592, Of, If, If16 = (W("CF", 128 * j, 128) for j in range(5))
+    act(Bfh, M("B"), F.Copy, scale=0.5); act(Bf592, M("B"), F.Copy, scale=592.0); fill(Of, 1); fill(R("ONE"), 1); act(If, M("I"), F.Copy)
+    act(If16, M("I"), F.Copy, scale=16.0)
+    for h in range(2):
+        fill(W("Z1", EW * h + 576, 128), int(MK))
+        if not all(OPT["f2"]):
+            fill(W("Z2", EW * h + 512, 192), int(MK))
+        if OPT["foldm"]:
+            fill(W("PZ", 160 * h, 96), 0)
     fill(R("Ws"), 0); cp(R("Ws", 15, 143, 16), R("CM", M("B")[2], M("B")[3], 16))
     ts(R("key2"), R("Ws", 15, 143), 2.0 ** 63, 2.0 ** 63, A.mult, A.mult); tt(M("MP"), R("key2"), M("Is"), A.add)
-    ts(c(9), W("wtI", 0, 1), 32.0, None, A.add); ts(R("Ww"), R("Ws"), c(9), None, A.mult)
+    ts(c(9), W("wtI", 0, 1), 32.0, None, A.add)
+    if not OPT["hd"]:
+        ts(R("Ww"), R("Ws"), c(9), None, A.mult)
     ts(c(10), W("thI", 0, 1), -8192.0, None, A.add)
     ts(c(11), W("ONE", 0, 1), -2.0 ** -60, 2.0 ** -63, A.mult, A.mult)
     iota(W("rf", 0, 64), [[0, 4], [1, 16]], 0, 0); ts(ci(3), ci(0), 1, None, A.add); ts(ci(4), ci(3), 15, None, A.bitwise_and); cp(c(13), ci(4))
     ts(W("cs", 0, 64), W("rf", 0, 64), c(0), 16384.0, A.is_equal, A.mult); ts(W("yf", 0, 64), W("rf", 0, 64), c(13), -8192.0, A.is_equal, A.mult)
     tt(R("dg"), W("cs", 0, 64), W("yf", 0, 64), A.add); ts(c(12), c(0), 14.5, 8192.0, A.is_lt, A.mult)
+    if OPT["hd"]:
+        act(R("Wb"), M("B"), F.Copy, scale=c(9)); act(c(14), c(12), F.Copy, scale=1024.0)
+        act(W("dh", 0, 64), R("dg"), F.Copy, scale=1024.0); act(W("dh", 64, 64), R("dg"), F.Copy, scale=1024.0)
     iota(R("ramp"), [[8, 64]], 0, 0)
-    fill(W("m0", 0, 512), 0); fill(W("m0", 512, 512), 0); ms(R("m0", 0, 1024, 16), -1024.0); fill(R("X", 4096, 4112), 0); fill(W("MI", 0, 32), 0)
+    fill(W("m0", 0, 512), 0); fill(W("m0", 512, 512), 0); ms(R("m0", 0, 1024, 16), -1024.0); fill(R("X", 4096, 4112), -1024); fill(W("MI", 0, 32), 0)
     ONE = W("ONE", 0, 64)
     ts(R("s1"), R("psr"), 0.0, 4.0, A.is_ge, A.mult); tt(R("F0"), R("s1"), R("psr"), A.add)
     act(R("sf"), R("dvr"), F.Identity, bias=4096.0, scale=4096.0)
@@ -231,7 +257,7 @@ def build():
 
     def marks(h, tile):
         for d in range(8):
-            ts(R("Zn", 512 * h + d, 512 * h + 512, 8), tile, float(d + 1), 32 * Q, A.is_equal, A.mult)
+            ts(R("Zn", 512 * h + d, 512 * h + 512, 8), tile, float(d + 1), MK, A.is_equal, A.mult)
         return W("Zn", 512 * h, 512)
 
     def names(z):
@@ -240,141 +266,132 @@ def build():
     for h in range(2):
         cur[0] = h
         o, H = 512 * h, lambda name: W(name, 64 * h, 64)
-        tt(W("Ks", o + 1, 511), W("dnI", o, 511), W("dnI", o + 1, 511), A.subtract)
-        act(W("dk", o + 1, 511), W("Ks", o + 1, 511), F.Identity, bias=-4096.0); ms(R("dk", o, o + 512, 8), 4194304.0)
+        before = fresh(511); ts(before, W("dnI", o, 511), -4096.0, None, A.add)
+        tt(W("dk", o + 1, 511), before, W("dnI", o + 1, 511), A.subtract); ms(R("dk", o, o + 512, 8), 4194304.0)
         ts(H("key7"), R("dnI", o + 7, o + 512, 8), 32768.0, None, A.add)
         ts(H("ta"), R("dnI", o, o + 512, 8), 5, None, A.arith_shift_right); cp(H("khi"), H("ta"))
         ts(H("t4"), R("dnI", o, o + 512, 8), 31, None, A.bitwise_and); cp(H("klo"), H("t4"))
         ex, q1, Z = W("exr", o, 512), W("q1", o, 512), marks(h, H("dvx0"))
-        ts(q1, ex, -2.0, 18.0, A.is_equal, A.mult)
-        tt(W("EZ", o, 512), sm([("Iq", R("ONE")), ("Iq", ex), ("Iq", q1)], n=512), Z, A.max)
-        act(W("dl", o, 512), sm([("I", ex), ("I", q1), ("Iiq", Z)], n=512), F.Relu, bias=-31.0)
-        act(H("O0"), sm([("I", R("dl", o + d, o + 512, 8)) for d in range(8)]), F.Copy)
-        tt(W("MI", names(h), 64), H("sf"), H("nmr"), A.add)
+        ts(q1, ex, -2.0, 34.0, A.is_equal, A.mult)
+        tt(W("EZ", EW * h, 512), sm([("Iq", R("ONE")), ("Iq", ex), ("Iq", q1)], n=512), Z, A.max)
+        act(W("dl", o, 512), sm([("I", ex), ("I", q1), ("Iiq", Z)], n=512), F.Relu, bias=-127.0)
+        act(W("EZ", EW * h + 512, 64), sm([("I", R("dl", o + d, o + 512, 8)) for d in range(8)]), F.Copy)
+        tt(W("MI", names(h), 64), H("sf"), H("nmr"), A.add); cp(H("nx0"), H("nmr"))
+    if 2 in OPT["pd"]:
+        ms(R("xs"), 0.0)
 
-    def diagonal(out, tile, tmp):
-        scan(tmp, R("dg"), tile, A.add, A.min); ts(out, R(tmp[1], tmp[2] + 15, tmp[3], 16), c(12), None, A.add)
+    def diagonal(out, tile, tmp, times=1.0):
+        scan(tmp, R("dg"), tile, A.add, A.min); ts(out, R(tmp[1], tmp[2] + 15, tmp[3], 16), c(12), times, A.add, A.mult)
 
-    def update(h, E, mb, mo, out, final=False):
-        Rr, Tv, dP, Ph = (W(mb, mo + 64 * j, 64) for j in range(4))
-        ne, dl, n = W("ne", 512 * h, 512), W("dl", 512 * h, 512), OPT["cu"]
-        tt(ne, sm(("Iq", Rr, 8), n=512), E, A.is_equal)
-        strip = sm(("I4", E), ("Imq", Tv, 8), n=512, gate=Rr)
-        Z = None if OPT["rmw"] or final else marks(h, dP)
-        for j in range(n):
-            act(part(dl, j, n), part(strip, j, n), F.Relu, bias=32 * Q)
-        for j in range(n):
-            rest = sm([("I", part(E, j, n)), ("Im64q", part(ne, j, n))], ("Im1", part(dl, j, n)), n=512 // n)
-            if Z:
-                tt(part(out, j, n), rest, part(Z, j, n), A.max)
-            else:
-                act(part(out, j, n), rest, F.Relu)
-        if Z:
-            return
-        zu, zc, zm = W("zu", 4 * h, 4), W("zc", 64 * h, 64), W("zm", 64 * h, 64)
-        diagonal(zu, sm([("I", R("ramp")), ("B", dP), ("Bm1", Ph)]), W("zs", 64 * h, 64))
-        if final:
-            return
-        act(zm, Ph, F.Copy, scale=32 * Q)
-        fetch(zc, IND(out, zu), OPT["zcs"])
-        tt(IND(out, zu), zc, zm, A.add)
+    def record(out, ndv, nx, dP, Ph, t, b1):
+        tt(out, sm([(If, nx), ("I4k", dP), ("Iv%d" % t, Ph)], ("Im64q", b1)), ndv, A.max)
 
-    def record(out, ndv, PK, mb, mo, t, b1):
-        tt(out, sm([(If, PK), ("I4k", W(mb, mo + 128, 64)), ("Iv%d" % t if t else "Iq", W(mb, mo + 192, 64))], ("Im64q", b1)), ndv, A.max)
+    def differs(out, tile, big, scalar):
+        act(out, tile, F.Abs, scale=big) if scalar else ts(out, tile, 0.0, big, A.not_equal, A.mult)
 
     def visit(t, h):
         cur[0] = h
         last, z, o = t == NV - 1, 2 * t + h, 512 * h
         H = lambda name: W(name, 64 * h, 64)
-        eo, mo, io_, fo = 512 * z, MW * z, names(z), 128 * z
+        eo, io_, fo = EW * z, names(z), 128 * z
         ps, Bh = H("F0") if t == 0 else W("FI", fo - 256, 64), H("Bh")
         if t:
             tt(Bh, W("FI", fo - 192, 64), sm(("Bh", W("FI", fo - 192, 64))), A.is_gt)
-        ndv, PK = W("MI", io_, 64), W("MI", io_ + 64, 64)
-        Ro, Tv, dP, Ph, On = (W("MB", mo + 64 * j, 64) for j in range(5))
-        P, Jh, Pp, pf, pcx, b1, E = H("P"), H("Jh"), H("Pp"), H("pf"), H("pcx"), H("b1"), W("EZ", eo, 512)
-        if t == 0:
-            Oo, thr = H("O0"), c(10)
-        else:
-            Oo, thr = W("MBi", mo - 2 * MW + 256, 64), W("thr", t, 1)
-            update(h, W("EZi", eo - 1024, 512), "MBi", mo - 2 * MW, E)
-            if h == 0:
-                act(thr, W("MIi", 160 * (2 * t - 1), 1), F.Identity, bias=c(10), scale=32.0)
-        if not last:
-            send("e%d" % z, [(E, W("EZi", eo, 512))], 2.7)
+        ndv, n2, PK = W("MI", io_, 64), W("MI", io_ + 64, 64), W("PZ", 160 * h + 96, 64)
+        E, Oo, dP, Ph = W("EZ", eo, 512), W("EZ", eo + 512, 64), W("EZ", eo + 576, 64), W("EZ", eo + 640, 64)
+        P, Pp, pcx, b1, Tv = H("P"), H("Pp"), H("pcx"), H("b1"), H("Tv")
+        nx, thr = (W("MIi", 160 * (z - 2) + 96, 64), W("thr", t, 1)) if t else (H("nx0"), c(10))
+        if t and h == 0:
+            act(thr, W("MIi", 160 * (2 * t - 1), 1), F.Identity, bias=c(10), scale=32.0)
         first = fresh(512)
         scan(first, W("dk", o, 512), E, A.add, A.min)
         tt(H("kr"), R(first[1], 7, 512, 8), H("key7"), A.add)
         low = 0.0 if t else 1.0
-        act(H("u"), ps, F.Exp, bias=(123 - low) * LN2, scale=-LN2); act(b1, ps, F.Relu, bias=1.0 - low, scale=-3.75 if t else -1.0)
+        act(H("u"), ps, F.Exp, bias=(123 - low) * LN2, scale=-LN2); ts(b1, ps, 0.5 - low, None, A.is_le)
         act(H("ps4"), ps, F.Relu, bias=low)
-        tt(P, H("u"), sm([("L2", b1), ("Bh", H("u"))]), A.is_gt)
+        tt(P, H("u"), sm([("L3", b1), ("Oh", H("u"))]), A.is_gt)
         if t > 0:
-            record(ndv, W("MIi", 160 * (z - 2) + 32, 64), W("MIi", 160 * (z - 2) + 96, 64), "MBi", mo - 2 * MW, t - 1, b1)
-        cp(H("ndi"), ndv); ts(H("n"), H("ndi"), 4095, None, A.bitwise_and)
+            record(ndv, W("MIi", 160 * (z - 2) + 32, 64), nx, dP, Ph, t - 1, b1)
         sel, Sg, n = W("sel", o, 512), W("Sg", o, 512), OPT["c2"]
-        if OPT["selv"] and t:
-            row = sm(("I", P, 8), n=512)
+        selv = OPT["selv"] and t
+        if selv:
+            row = sm(("Iiq", P, 8), n=512)
         else:
-            row = sm([("I", E)] if t else [("Iq", W("exr", o, 512)), ("Iq", W("q1", o, 512))], ("I64q", P, 8), n=512, gate=ps)
+            row = sm([("Iiq", E)] if t else [("I", W("exr", o, 512)), ("I", W("q1", o, 512))], ("I128", P, 8), n=512, gate=ps)
         for j in range(n):
-            if OPT["selv"] and t:
+            if selv:
                 tt(part(sel, j, n), part(row, j, n), part(E, j, n), A.mult)
             else:
-                act(part(sel, j, n), part(row, j, n), F.Relu, bias=(low - 64) * Q)
+                act(part(sel, j, n), part(row, j, n), F.Relu, bias=low - 128)
         for j in range(n):
-            act(part(Sg, j, n), sm(("B", part(sel, j, n)), n=512 // n), F.Sign, bias=c(2), scale=-1.0 / Q)
-        act(pf, sm([("Im1", b1), ("I", P)]), F.Relu)
-        tt(pcx, sm([("T33", P), ("Imq", pf)]), H("kr"), A.is_le)
-        act(H("pwc"), sm([("I", H("ps4")), ("I256", P), ("Om256", pf), ("O256", pcx)]), F.Exp, bias=-381 * LN2, scale=LN2)
-        tt(H("ki"), sm([("I32", H("khi")), ("I", H("klo")), ("Iq", ONE), ("Im60k", pcx)]), H("kr"), A.min)
+            act(part(Sg, j, n), sm(("B", part(sel, j, n)), n=512 // n), F.Sign, bias=c(2), scale=-1.0)
+        tt(pcx, sm([("Tb", b1), ("Tp", P)]), H("kr"), A.is_gt)
+        act(H("pwc"), sm([("I", H("ps4")), ("Om256", pcx)]), F.Exp, bias=-125 * LN2, scale=LN2)
+        tt(H("ki"), sm([("I32", H("khi")), ("I", H("klo")), ("I60k", b1), ("M1", P), ("I60k", pcx)]), H("kr"), A.min)
         ts(H("kc"), H("ki"), 4095, None, A.bitwise_and); ts(H("kd"), H("ki"), 12, 15, A.arith_shift_right, A.bitwise_and)
         G = sm([("MP", P)] + ([("Is", Bh)] if t else []), [("D", R("Sg", o + d, o + 512, 8)) for d in range(8)], gate=part(sel, 0, n))
         tt(H("key"), G, H("pwc"), A.min)
         tt(Pp, H("key"), sm(("Bh", H("key"))), A.is_gt)
         tt(PK, H("kc"), Pp, A.mult)
-        K = sm((Bf, PK))
-        K37 = sm([(If, ndv), ("I64q", b1)], ("I64q", Pp), (Bf37, PK), gate=H("key"))
-        if OPT["pd"][h]:
-            tt(H("t1"), K, H("n"), A.mult); diagonal(W("cu", 4 * h, 4), K, H("cs"))
-        else:
-            cp(H("cu"), K); tt(H("t1"), K, H("n"), A.mult)
-        ts(H("ta"), H("t1"), 5, None, A.arith_shift_right)
-        tt(H("t3"), K37, H("ta"), A.add); ts(H("t4"), H("t3"), 4095 | 19 << 22, None, A.bitwise_and)
+        K = sm((Bfh, PK))
+        K37 = sm([(If16, nx), ("Ifl", b1)], ("M3", Pp), (Bf592, PK), gate=H("key"))
+        tt(H("t1"), K, nx, A.mult)
+        diagonal(W("cu", 4 * h, 4), K, H("cs"), 2.0) if OPT["pd"][h] else ts(H("cw"), K, 2.0, None, A.mult)
+        tt(H("t3"), K37, H("t1"), A.add); ts(H("t4"), H("t3"), 4, 4095 | 3 << 22, A.arith_shift_right, A.bitwise_and)
         ts(H("at"), H("t4"), 4096.0, None, A.min)
-        tt(dP, H("kd"), Pp, A.mult); act(Ph, dP, F.Sign)
-        act(Jh, sm([("Im1", P), ("I", Pp)]), F.Relu, acc=None if last else W("acc", h, 1))
-        tt(H("ps2"), sm(([("I", ps), ("Im1", H("ps4"))] if t else []) + [("O256", Pp), ("Bm4", Jh)]), H("ps4"), A.min)
-        tt(H("key2"), sm([("Ims", P), ("Os", Pp)]), H("key"), A.min)
+        tt(dP, H("kd"), Pp, A.mult); ts(Ph, dP, 0.5, MK, A.is_ge, A.mult)
+        tt(H("ps2"), sm(([("I", ps), ("Im1", H("ps4"))] if t else []) + [("I4", P), ("M2", Pp)]), H("ps4"), A.min)
+        tt(H("key2"), sm(("Os", Pp)), H("key"), A.min)
         act(H("J2h"), sm(("Hm", H("key2"))), F.Sign, bias=c(11))
-        act(H("vj"), sm([("Im256", b1), ("Im256", pf), ("Im224", Pp), ("Bj", H("J2h"))]), F.Relu, bias=301.0)
-        Rp = sm([("Bk", pf), ("Bk", Jh)]); act(Ro, Rp, F.Copy); tt(H("neo"), Rp, Oo, A.is_equal)
         if t:
             act(H("Bh2"), sm([("I", Bh), ("Im1", Pp)]), F.Relu)
-        tt(Tv, sm([("MA", P), ("Im256", pcx), ("Im256", Pp)] + ([("Bk", H("Bh2"))] if t else [])), H("vj"), A.max)
-        act(On, sm([("I", Oo), ("Im256", Pp), ("Im256", H("neo"))]), F.Relu)
+        mine = [("Im128", P), ("I256", b1), ("I256", pcx), ("Im256", Pp)] + ([("Bk", H("Bh2"))] if t else [])
+        zu = W("zu", 4 * h, 4)
+        diagonal(zu, sm([("I", R("ramp")), ("B", dP), ("Bmh", Ph)]), H("zs"))
+        z1, z2, zo = W("Z1", EW * h, 512), W("Z2", EW * h, 512), W("Z1", EW * h + 512, 64)
         if not last:
+            two_ = OPT["f2"][z]
+            if two_:
+                tt(z2, sm(("Bkq", Pp, 8), n=512), E, A.is_equal)
+            else:
+                differs(z1, sm(("Iiq", E), ("Bkm", Pp, 8), n=512, gate=H("key")), MK, OPT["z1s"][h])
+            act(H("vj"), sm([("Im2k", P), ("Im1536", Pp), ("Bj", H("J2h"))]), F.Relu, bias=1501.0)
+            tt(Tv, sm(mine), H("vj"), A.max)
+            differs(zo, sm([("I", Oo), ("Bkm", Pp)]), 64.0, OPT["zos"])
+            act(z1 if two_ else z2, sm([("Iiq", E), ("I512", b1, 1), ("M4", P, 1), ("I512", pcx, 1), ("Im512", Pp, 1)], [("I4k", z2)] if two_ else [],
+                                       ("Im1", Tv, 8), n=512, gate=H("key2")), F.Relu, scale=-Q)
+            tt(H("zc"), IND(E, zu), Ph, A.max); cp(IND(E, zu), H("zc"))
+            send("e%d" % z, [W("EZ", eo, EW), W("Z1", EW * h, EW), W("Z2", EW * h, EW)][:3 - two_], W("EZ", eo + 2 * EW, EW), 3, OPT["lat0"])
+            if OPT["foldm"]:
+                tt(n2, sm(("Oq", Pp)), nx, A.min)
+            else:
+                tt(H("sf"), sm(("Oq", Pp)), nx, A.min); tt(n2, H("sf"), PK, A.add)
+            act(H("Jh"), sm([("Im1", P), ("I", Pp)]), F.Relu, acc=W("acc", h, 1))
             if h == 1:
                 Ap = sm((Of, W("acc", 0, 2)), n=2)
                 ts(W("ai", 0, 32), W("ONE", 0, 32), part(Ap, 0, 2), part(Ap, 1, 2), A.mult, A.add)
                 ts(W("ai", 32, 32), W("ai", 0, 32), 7, None, A.bitwise_and); cp(W("MI", io_ - 32, 32), W("ai", 32, 32))
-            send("m%d" % z, [(W("MB", mo, MW), W("MBi", mo, MW)), (W("MI", io_ - 32, 160), W("MIi", 160 * z, 160))], 2.8)
+            send("m%d" % z, [W("MI", io_ - 32, 160), W("PZ", 160 * h, 160)][:1 + OPT["foldm"]], W("MIi", 160 * z, 160), OPT["foldm"], OPT["lat0"])
         act(H("pw2"), H("ps2"), F.Exp, bias=-122 * LN2, scale=LN2)
         act(H("mx"), sm(("Hm", H("pw2"))), F.Sign)
         act(H("mp"), sm([("I", H("ps2")), ("I256", H("mx"))]), F.Relu, bias=-260.0)
         if last:
-            Ef = W("EZ", eo + 1024, 512)
-            update(h, E, "MB", mo, Ef, True)
-            ts(W("q1", o, 512), Ef, 17 * Q, -18.0, A.is_equal, A.mult)
-            act(W("q2", o, 512), sm([("Iiq", Ef), ("I", W("q1", o, 512))], n=512), F.Identity, bias=-1.0)
-            ts(H("s4"), On, 17.0, -18.0, A.is_equal, A.mult); act(H("O0"), sm([("I", H("s4")), ("I", On)]), F.Identity, bias=63.0)
-            tt(W("og", o, 512), sm([("Im2iq", Ef), ("I", H("O0"), 8)], n=512), W("q2", o, 512), A.min)
-            tried = IND(W("og", o, 512), W("zu", 4 * h, 4))
+            act(H("vj"), sm([("Im2k", P), ("Om2k", Pp), ("Bj", H("J2h"))]), F.Relu, bias=-35.0)
+            tt(H("Tw"), sm(mine + [("Om2k", P)]), H("vj"), A.max)
+            ts(H("s4"), ndv, Q, None, A.is_ge); tt(H("neo"), sm(("Bk", Pp)), Oo, A.is_equal)
+            act(H("zm"), sm([("I", Oo), ("Im256", H("s4")), ("Im256", H("neo"))]), F.Relu)
+            tt(Tv, sm([("I", H("zm")), ("I128", ONE), ("Im2k", P), ("Im2k", Pp)]), H("Tw"), A.max)
+            ne, dl, Ef = W("ne", o, 512), W("dl", o, 512), W("q1", o, 512)
+            tt(ne, sm(("Bkq", Pp, 8), n=512), E, A.is_equal)
+            tt(z2, sm(("Im1", E), ("Iq", Tv, 8), n=512, gate=H("key2")), E, A.min)
+            act(Ef, sm(("Im256", ne), ("Iiq", z2), n=512), F.Relu)
+            act(dl, Ef, F.Abs, bias=-16.0); ts(W("og", o, 512), dl, -1.0, 15.0, A.mult, A.add)
+            tried = IND(W("og", o, 512), zu)
             fetch(H("zc"), tried, True)
         win, g0 = R("X", 0, 4112), 1024 * h
         mxv, lanes = R("mxs", g0 + 15, g0 + 1024, 16), lambda k: R("Ws", 15 - k, 143 - k)
         dd, ad, xcr, n = W("dd", g0, 1024), W("ad", g0, 1024), W("xcr", g0, 1024), OPT["cx"]
-        if OPT["pd"][h]:
+        if OPT["pd"][h] == 1:
             xc = H("xc"); big = [("I", mxv)]
             fetch(xc, IND(win, W("cu", 4 * h, 4)), OPT["xcs"])
             for j in range(2):
@@ -383,31 +400,40 @@ def build():
                 act(part(ad, j, 2), planes([[("I", R("dd", g0 + k, g0 + 1024, 16)), ("Im1", xc)] for k in range(8 * j, 8 * j + 8)]), F.Abs)
             sums = [[(lanes(k), part(ad, k, 16)) for k in range(8 * j, 8 * j + 8)] for j in range(2)]
         else:
-            xc = R("xcr", g0, g0 + 1024, 16); big = [("I", xc), ("I", mxv)]
+            xc = R("xs" if OPT["pd"][h] else "xcr", g0, g0 + 1024, 16); big = [("I", xc), ("I", mxv)]
+            if OPT["pd"][h]:
+                fetch(xc, IND(win, W("cu", 4 * h, 4)), OPT["xcs"])
             for j in range(n):
-                act(part(xcr, j, n), IND(win, part(H("cu"), j, n)), F.Copy)
+                if OPT["pd"][h]:
+                    scan(part(xcr, j, n), W("m0", 0, 1024 // n), part(W("xs", g0, 1024), j, n), A.add, A.max)
+                else:
+                    act(part(xcr, j, n), IND(win, part(H("cw"), j, n)), F.Copy)
                 tt(part(dd, j, n), IND(win, part(H("at"), j, n)), part(xcr, j, n), A.subtract)
                 act(part(ad, j, n), part(dd, j, n), F.Abs)
             sums = [[(lanes(k), R("ad", g0 + k, g0 + 1024, 16)) for k in range(16)]]
-        ts(H("clash"), sm([("I64q", b1), ("I64q", Pp), ("Bm8k", Ph)], *sums, gate=part(dd, 0, 2)), thr, None, A.is_le)
+        ts(H("clash"), sm(("Bm8h", Ph), *sums, gate=part(dd, 0, 2)), thr, None, A.is_le)
         tt(W("FO", fo + 64, 64), H("clash"), H("u"), A.mult)
-        tt(W("FO", fo, 64), sm([("Im251", ONE), ("B", H("mp")), ("I256", Ph)], ("Bm256", H("clash")), gate=part(ad, 0, 2)), H("ps2"), A.max)
+        tt(W("FO", fo, 64), sm([("Im251", ONE), ("B", H("mp")), ("I256h", Ph)], ("Bm256", H("clash")), gate=part(ad, 0, 2)), H("ps2"), A.max)
         if not last:
-            send("f%d" % z, [(W("FO", fo, 128), W("FI", fo, 128))], 2.2)
+            send("f%d" % z, [W("FO", fo, 128)], W("FI", fo, 128), 0, OPT["lat0"])
         scan(W("mxs", g0, 1024), R("m0"), dd, A.add, A.max)
-        act(H("rf"), sm([("Imh", ONE), ("I" if OPT["pd"][h] else "I2", xc), ("I", mxv)]), F.Identity, bias=12582912.0, scale=0.5)
-        act(H("rb"), H("rf"), F.Identity, bias=-12582912.0)
         if t in OPT["xr"]:
-            act(H("Yb"), sm(big), F.Copy)
+            act(H("Yb"), sm(big), F.Relu)
         else:
-            act(H("Yb"), sm(big + [("Bm8k", Ph)], ("B4k", H("clash")), gate=part(ad, 1, 2)), F.Identity, bias=8192.0)
+            act(H("Yb"), sm(big + [("Bm8h", Ph)], ("B4k", H("clash")), gate=part(ad, 1, 2)), F.Relu, bias=8192.0)
+        both = [("I", xc), ("I", H("Yb"))]
+        if t in OPT["xr"] or not OPT["rbv"]:
+            act(H("rf"), sm([("Imh", ONE)] + both), F.Identity, bias=12582912.0, scale=0.5)
+            act(H("rb"), H("rf"), F.Identity, bias=-12582912.0)
+        else:
+            ts(H("ri"), sm(both), 0.5, -0.25, A.mult, A.add)
         if last:
             p9, Bo = W("FO", fo, 64), H("Bh")
             tt(Bo, W("FO", fo + 64, 64), sm(("Bh", W("FO", fo + 64, 64))), A.is_gt)
-            tt(H("vb"), sm([("Im33", ONE), ("I32", Ph)], ("Bk", Bo), gate=H("clash")), H("zc"), A.max); cp(tried, H("vb"))
+            tt(H("vb"), sm([("Im129", ONE), ("Iiq", Ph)], ("Bk", Bo), gate=H("clash")), H("zc"), A.max); cp(tried, H("vb"))
             store("yg%d" % h, W("og", o, 512), 2.2, "Y", (o, o + 512))
             ts(H("s1"), p9, -1.0, -2.0, A.is_ge, A.add); ts(H("s2"), p9, -5.0, None, A.add); tt(H("op"), H("s1"), H("s2"), A.max)
-            act(H("s3"), p9, F.Relu, bias=1.0, scale=-3.75); record(H("nf"), ndv, PK, "MB", mo, t, H("s3"))
+            act(H("s3"), p9, F.Relu, bias=1.0, scale=-3.75); record(H("nf"), ndv, PK, dP, Ph, t, H("s3"))
             ts(H("n"), H("nf"), 4095, None, A.bitwise_and); cp(H("yf"), H("n"))
             ts(H("dv1"), H("nf"), 12, 15, A.arith_shift_right, A.bitwise_and); ts(H("od"), H("dv1"), -1.0, None, A.add)
 
@@ -415,23 +441,29 @@ def build():
         visit(t, 0); visit(t, 1)
         for lo, n in (((0, 4), (4, 4)) if t == NV - 1 else ((0, 8),)):
             cur[0] = 1 if lo + n == 8 else 0
-            hs = sm([(R("Ww", 15 - k, 143 - k), R("Yb", 16 * lo + k, 16 * (lo + n), 16)) for k in range(16)], n=n)
-            cp(W("hi", lo, n), hs); ts(W("hi", 8 + lo, n), W("hi", lo, n), 31, None, A.bitwise_and)
+            if OPT["hd"]:
+                scan(W("hw", 16 * lo, 16 * n), W("dh", 0, 16 * n), sm((R("Wb"), W("Yb", 16 * lo, 16 * n)), n=16 * n), A.add, A.min)
+                hs = R("hw", 16 * lo + 15, 16 * (lo + n), 16)
+                ts(W("hi", lo, n), hs, c(14), None, A.add)
+            else:
+                hs = sm([(R("Ww", 15 - k, 143 - k), R("Yb", 16 * lo + k, 16 * (lo + n), 16)) for k in range(16)], n=n)
+                cp(W("hi", lo, n), hs)
+            ts(W("hi", 8 + lo, n), W("hi", lo, n), 31, None, A.bitwise_and)
             if t in OPT["xr"]:
                 tt(W("hi", 16 + lo, n), W("cpos", lo, n), W("hi", 8 + lo, n), A.add)
                 ts(W("hu", lo, n), W("hi", 16 + lo, n), -512.0 * lo, None, A.add)
                 col = IND(W("X", 512 * lo, 512 * n), W("hu", lo, n))
                 fetch(W("old", 16 * lo, 16 * n), col, True)
                 for h in range(lo // 4, (lo + n) // 4):
-                    H, Ph = lambda name: W(name, 64 * h, 64), W("MB", MW * (2 * t + h) + 192, 64)
-                    tt(H("keep"), sm([("Iq", ONE), ("Bmq", Ph)], ("Bq", H("clash")), gate=H("rb")), H("old"), A.min)
-                    tt(H("new"), sm([("Imq", ONE), ("Bq", Ph), ("I", H("rb"))], ("Bmq", H("clash"))), H("keep"), A.max)
+                    H, Ph = lambda name: W(name, 64 * h, 64), W("EZ", EW * (2 * t + h) + 640, 64)
+                    tt(H("keep"), sm([("Iq", ONE), ("Bmqh", Ph)], ("Bq", H("clash")), gate=H("rb")), H("old"), A.min)
+                    tt(H("new"), sm([("Imq", ONE), ("Bqh", Ph), ("I", H("rb"))], ("Bmq", H("clash"))), H("keep"), A.max)
                 cp(col, W("new", 16 * lo, 16 * n))
             else:
-                ts(W("hf", lo, n), hs, 500000.0, 4128.0, A.is_ge, A.mult); tt(W("hf", 8 + lo, n), W("hf", lo, n), W("cpos", lo, n), A.add)
+                ts(W("hf", lo, n), W("hi", lo, n), 200000.0, 4128.0, A.is_ge, A.mult); tt(W("hf", 8 + lo, n), W("hf", lo, n), W("cpos", lo, n), A.add)
                 tt(W("hi", 16 + lo, n), W("hf", 8 + lo, n), W("hi", 8 + lo, n), A.add)
                 ts(W("hu", lo, n), W("hi", 16 + lo, n), -512.0 * lo, None, A.add)
-                cp(IND(R("X", 512 * lo, XW), W("hu", lo, n)), W("rb", 16 * lo, 16 * n))
+                cp(IND(R("X", 512 * lo, XW), W("hu", lo, n)), W("ri" if OPT["rbv"] else "rb", 16 * lo, 16 * n))
             if n == 4:
                 store("yx%d" % cur[0], W("X", 512 * lo, 2048), 3.0, "YS"[cur[0]], (512 * lo, 512 * lo + 2048))
     store("yp", R("op"), 2.0, "Y"); store("yn", R("yf"), 2.0, "Y"); store("yd", R("od"), 2.0, "Y")
@@ -445,7 +477,7 @@ def depend(ops):
             deps[i].update(j for j, y, w in hist.get(x[1], []) if w and _meet(x, y))
         for x in o["wr"]:
             deps[i].update(j for j, y, w in hist.get(x[1], []) if _meet(x, y))
-        for x in set(o["rd"]):
+        for x in set([] if o.get("issue") else o["rd"]):
             hist.setdefault(x[1], []).append((i, x, False))
         for x in set(o["wr"]):
             hist[x[1]] = [e for e in hist.get(x[1], []) if e[1] != x] + [(i, x, True)]
@@ -464,23 +496,145 @@ def replay(ops, s, hop, sc):
     return max(fin.values())
 
 
-CASES = ((0.14, {}), (0.2, {"V": 1.25, "S": 1.25, "P": 1.25, "L": 1.2}))
+CASES = ((0.165, {}), (0.2, {"V": 1.3, "S": 1.3, "P": 1.3, "L": 1.2, "D": 2.0}))
 
 
 def plan(ops, rounds, moves):
     deps, rs, n = depend(ops), np.random.RandomState(OPT["seed"]), len(ops)
-    dp = [0.0] * n
-    best = schedule(ops, deps, dp); score = sum(replay(ops, best, h, sc) for h, sc in CASES)
-    for _ in range(rounds):
-        t0 = rs.rand() * max(best["start"]); amp = OPT["amp"] * rs.rand()
-        d2 = [x + (amp * float(y) if t0 <= st < t0 + OPT["span"] else 0.0) for x, y, st in zip(dp, rs.randn(n), best["start"])]
-        s = schedule(ops, deps, d2)
-        if s is None:
-            continue
-        sc2 = sum(replay(ops, s, h, sc) for h, sc in CASES)
-        if sc2 <= score:
-            best, score, dp = s, sc2, d2
-    return tie(ops, deps, *refine(ops, deps, best["order"], best["bank"], moves, rs)) if moves else best
+    need, eng, tile, lat = direct(deps)[0], [o["eng"] for o in ops], [o["tile"] for o in ops], [o["lat"] for o in ops]
+    hop, up = OPT["hop"], [bool(o.get("up")) for o in ops]
+    cost = [o["cost"] * (OPT["slow"] if o["eng"] in "VSP" else 1) for o in ops]
+    loads = [i for i in range(n) if up[i]]
+    for a, b in zip(loads, loads[1:]):
+        need[b].append(a)
+    inline = lambda j, i: eng[j] == eng[i] == "P" or (up[j] and up[i])
+    succ = [[] for _ in ops]
+    for i in range(n):
+        for j in need[i]:
+            succ[j].append(i)
+    before = [[(j, 0.0 if inline(j, i) else lat[j] + hop) for j in need[i]] for i in range(n)]
+    after = [[(k, 0.0 if inline(i, k) else lat[i] + hop) for k in succ[i]] for i in range(n)]
+    timed = [[j for j in need[i] if not inline(j, i)] for i in range(n)]
+    users, hold = {}, {}
+    for i in range(n):
+        if tile[i]:
+            users[tile[i]] = users.get(tile[i], 0) + 1
+            hold[tile[i]] = hold.get(tile[i], 0.28) + cost[i] + (0.0 if eng[i] == "P" else hop)
+    cc = [[o["cost"] * sc.get(o["eng"], 1.0) for o in ops] for h, sc in CASES]
+    ll = [[o["lat"] * (sc.get("L", 1.0) if o.get("remote") else 1.0) + h for o in ops] for h, sc in CASES]
+
+    def issue(start):
+        left, todo, bank, idle, last = [len(x) for x in need], dict(users), {}, list(range(8)), [{} for _ in range(8)]
+        fins, free, order, wait = [[0.0] * n for _ in CASES], [dict.fromkeys("VSPGYD", 0.0) for _ in CASES], [], []
+        for i in sorted(range(n), key=lambda i: (-1 if up[i] else start[i], i)):
+            wait.append(i)
+            while True:
+                i = next((k for k in wait if not left[k] and (not tile[k] or tile[k] in bank or idle)), None)
+                if i is None:
+                    break
+                wait.remove(i)
+                v, e, more = tile[i], eng[i], timed[i]
+                if v:
+                    if v not in bank:
+                        b = min(idle, key=lambda b: max([fins[0][j] for j in last[b].values()] + [0.0]))
+                        idle.remove(b); bank[v] = b
+                        more = more + [j for e2, j in last[b].items() if not e2 == e == "P"]
+                    else:
+                        b = bank[v]
+                        more = more + [j for e2, j in last[b].items() if e2 != e]
+                    last[b][e] = i; todo[v] -= 1
+                    if not todo[v]:
+                        idle.append(b)
+                for fin, at, co, la in zip(fins, free, cc, ll):
+                    t = at[e]
+                    for j in more:
+                        if fin[j] > t:
+                            t = fin[j]
+                    t += co[i]; at[e] = t; fin[i] = t + la[i]
+                order.append(i)
+                for k in succ[i]:
+                    left[k] -= 1
+        return None if wait else (sum(max(x) for x in fins), order, bank)
+
+    key = np.zeros(n)
+    for i in range(n - 1, -1, -1):
+        key[i] = min([key[k] - g for k, g in after[i]] + [-lat[i]]) - cost[i]
+    hh = np.array([o["h"] for o in ops])
+    key, best, cur = key + OPT["bias"] * hh, None, None
+    for it in range(rounds):
+        end = pack(before, succ, eng, cost, key, [0.0] * n)
+        back = np.array(pack(after, need, eng, cost, -np.array(end) - lat, lat, tile, hold))
+        start = back.max() - back
+        r = issue(start.tolist())
+        if cur is None or (r and r[0] <= cur[0] - OPT["heat"] * (1 - it / rounds) * math.log(1 - rs.rand())):
+            cur, base = r, start
+            if r and (best is None or r[0] < best[0]):
+                best = r
+        t0 = rs.rand() * base.max()
+        win = (base >= t0) & (base < t0 + OPT["span"])
+        if rs.rand() < 0.3:
+            key = base + win * (hh - 0.5) * rs.randn() * 1.5
+        else:
+            key = base + win * OPT["amp"] * rs.rand() * rs.randn(n)
+    return tie(ops, deps, *(refine(ops, deps, best[1], best[2], moves, rs) if moves else best[1:]))
+
+
+def direct(deps):
+    anc, need = [0] * len(deps), []
+    for i in range(len(deps)):
+        keep, far = [], 0
+        for j in sorted(deps[i], reverse=True):
+            if not far >> j & 1:
+                keep.append(j)
+            far |= anc[j] | 1 << j
+        anc[i] = far; need.append(keep)
+    return need, anc
+
+
+def pack(links, back, eng, cost, key, first, tile=None, hold=None):
+    n = len(eng)
+    left, seen, end = [len(x) for x in links], [False] * n, [0.0] * n
+    st, en, use, upto = {e: [] for e in "VSPGYD"}, {e: [] for e in "VSPGYD"}, np.zeros(6000, np.int8), {}
+    for top in np.argsort(key, kind="stable").tolist():
+        seen[top] = True
+        stack = [] if left[top] else [top]
+        while stack:
+            i = stack.pop()
+            t = first[i]
+            for j, g in links[i]:
+                if end[j] + g > t:
+                    t = end[j] + g
+            s, e, c, v = st[eng[i]], en[eng[i]], cost[i], tile[i] if tile else None
+            while True:
+                k = m = len(s); lo = 0
+                while lo < k:
+                    mid = (lo + k) // 2
+                    if e[mid] > t:
+                        k = mid
+                    else:
+                        lo = mid + 1
+                while k < m and s[k] < t + c - 1e-9:
+                    if e[k] > t:
+                        t = e[k]
+                    k += 1
+                if v is None or v in upto:
+                    break
+                a, b = int(t * 20), int((t + hold[v]) * 20) + 1
+                full = np.flatnonzero(use[a:b] >= OPT["cap"])
+                if not len(full):
+                    use[a:b] += 1; upto[v] = b
+                    break
+                t = (a + int(full[-1]) + 1) / 20 + 1e-6
+            if v is not None:
+                b = int((t + c + 0.2) * 20) + 1
+                if b > upto[v]:
+                    use[upto[v]:b] += 1; upto[v] = b
+            s.insert(k, t); e.insert(k, t + c); end[i] = t + c
+            for j in back[i]:
+                left[j] -= 1
+                if not left[j] and seen[j]:
+                    stack.append(j)
+    return end
 
 
 def schedule(ops, deps, dp):
@@ -558,14 +712,7 @@ def schedule(ops, deps, dp):
 
 def refine(ops, deps, order, bank, moves, rs):
     n, eng = len(ops), [o["eng"] for o in ops]
-    anc, need, users = [0] * n, [], {}
-    for i in range(n):
-        keep, far = [], 0
-        for j in sorted(deps[i], reverse=True):
-            if not far >> j & 1:
-                keep.append(j)
-            far |= anc[j] | 1 << j
-        anc[i] = far; need.append(keep)
+    (need, anc), users = direct(deps), {}
     for i in order:
         if ops[i]["tile"]:
             users.setdefault(ops[i]["tile"], []).append(i)
@@ -656,12 +803,15 @@ def refine(ops, deps, order, bank, moves, rs):
 
 def tie(ops, deps, order, bank):
     pos, cnt, seen, done, waits, marked = {}, {}, {e: {} for e in "VSPGY"}, {}, {}, set()
-    rank, lastuse, begun = {}, [{} for _ in range(8)], set()
+    rank, lastuse, begun, left, landed = {}, [{} for _ in range(8)], set(), {}, {}
     for k, i in enumerate(order):
         o = ops[i]; e = o["eng"]; rank[i] = k
-        key = o["sem"] or "s" + e
+        key = "" if o.get("issue") else o["sem"] or "s" + e
         cnt[key] = cnt.get(key, 0) + 1; pos[i] = (key, cnt[key])
         need, w = set(deps[i]), []
+        if e == "D":
+            waits[i], done[i] = [j for j in need if ops[j].get("issue")], {key: 1}
+            continue
         if o["tile"]:
             use = lastuse[bank[o["tile"]]]
             need.update(j for e2, j in use.items() if e2 != e or o["tile"] not in begun)
@@ -670,30 +820,35 @@ def tie(ops, deps, order, bank):
             if e == "P" and ops[j]["eng"] == "P":
                 continue
             k2, v = pos[j]
-            if seen[e].get(k2, 0) < v:
+            if ops[j].get("remote"):
+                if not seen[e].get("x" + k2) and any(x[1] == y[1] and _meet(x, y) for x in o["wr"] for y in ops[j]["rd"]):
+                    left.setdefault(i, []).append(j); seen[e]["x" + k2] = 1
+                    w.append(j)
+                if not any(x[1] == y[1] and _meet(x, y) for x in o["rd"] + o["wr"] for y in ops[j]["wr"]):
+                    continue
+                if seen[e].get(k2, 0) < v:
+                    landed.setdefault(i, []).append(j); seen[e][k2] = v
+                    w.append(j)
+            elif seen[e].get(k2, 0) < v:
                 w.append(j); marked.add(j)
                 for k3, v3 in done[j].items():
                     seen[e][k3] = max(seen[e].get(k3, 0), v3)
         waits[i] = w
-        done[i] = {} if o.get("remote") else dict(seen[e])
+        done[i] = dict(seen[e])
         done[i][key] = cnt[key]
     lastof = {}
     for i in order:
         lastof[pos[i][0]] = i
+    lastof.pop("")
     marked.update(lastof.values())
     val, tot = {}, {}
     for i in order:
         if i in marked:
             k = pos[i][0]; tot[k] = tot.get(k, 0) + 1; val[i] = tot[k]
-    return dict(order=order, waits=waits, val=val, pos=pos, last=lastof, bank=bank)
+    return dict(order=order, waits=waits, val=val, pos=pos, last=lastof, bank=bank, left=left, landed=landed)
 
 
 PLAN = {}
-
-
-def _share(engs, parts):
-    m = len(engs) // parts
-    return [sum(1 << e for e in engs[j * m:(j + 1) * m]) for j in range(parts)]
 
 
 def rank_program(g, core, T, topo):
@@ -726,11 +881,18 @@ def rank_program(g, core, T, topo):
     def hbm(name, cols):
         return T[name][:] if cols is None else T[name][:, cols[0]:cols[1]]
 
-    sent = 0
     for i in s["order"]:
-        o = ops[i]; q = Qu[o["eng"]]
+        o = ops[i]
+        if o["eng"] == "D":
+            continue
+        q = Qu[o["eng"]]
         for j in s["waits"][i]:
-            q.wait_ge(T.sem[s["pos"][j][0]], count(j))
+            if not ops[j].get("remote"):
+                q.wait_ge(T.sem[s["pos"][j][0]], count(j))
+        for j in s["left"].get(i, []):
+            q.wait_ge(T.sem["x" + ops[j]["sem"]], len(eng_out))
+        for j in s["landed"].get(i, []):
+            q.wait_ge(T.sem[ops[j]["sem"]], n_in)
         ins = None
         for name, args, kw in o["calls"]:
             if name == "load":
@@ -741,13 +903,12 @@ def rank_program(g, core, T, topo):
             elif name == "store":
                 ins = q.dma_start(hbm(args[1][:2], args[2]), ap(args[0]))
             elif name == "send":
-                masks = _share(eng_out, len(args[1]))
-                if len(masks) == 1:
-                    q.remote_dma(ap(args[1][0][1]), ap(args[1][0][0]), T.sem[args[0]], T.sem.sent, pid, rid, masks[0])
+                sem, srcs, dst, alu = args
+                if alu == 0:
+                    q.remote_dma(ap(dst), ap(srcs[0]), T.sem[sem], T.sem["x" + sem], pid, rid, topo.mask(core, nxt))
                 else:
-                    q.remote_dma_fused([RemoteDMATransfer(dst_ids=[DstId(rid=rid, pnc=pid)], dma_engine_mask=m, remote_sem=T.sem[args[0]],
-                                                          src=ap(a), dst=ap(b)) for m, (a, b) in zip(masks, args[1])], local_sem=T.sem.sent)
-                sent += len(eng_out)
+                    q.remote_dma_fused([RemoteDMATransfer(dst_ids=[DstId(rid=rid, pnc=pid)], dma_engine_mask=topo.mask(core, nxt), remote_sem=T.sem[sem],
+                                                          srcs=[ap(x) for x in srcs], dsts=[ap(dst)], alu_op=alu)], local_sem=T.sem["x" + sem])
             else:
                 a = [ap(x) for x in args]; k = {kk: ap(v) for kk, v in kw.items()}
                 if name == "tensor_tensor":
@@ -764,9 +925,11 @@ def rank_program(g, core, T, topo):
                     ins = q.activation(*a, **k)
                 elif name == "matmul":
                     ins = q.matmul(*a)
+                elif name == "affine_select":
+                    ins = q.affine_select(*a)
                 else:
                     ins = q.iota(*a, **k)
-        if o.get("remote"):
+        if o.get("issue"):
             continue
         if o["sem"]:
             ins.then_inc(T.sem[o["sem"]], 16)
@@ -774,4 +937,5 @@ def rank_program(g, core, T, topo):
             ins.then_inc(T.sem["s" + o["eng"]], 1)
     for k, j in s["last"].items():
         g.wait_ge(T.sem[k], count(j))
-    g.wait_ge(T.sem.sent, sent)
+        if ops[j].get("remote"):
+            g.wait_ge(T.sem["x" + k], len(eng_out))

import math
import numpy as np
from concourse.bass import DstId, RemoteDMATransfer
from concourse.mybir import AluOpType as A, ActivationFunctionType as F

NV = 5
OPT = dict(selv=0, seed=0, amp=0.8, span=6.0, rounds=4000, moves=40000, temp=0.06, heat=0.15, slow=1.05, cap=7, pe=0.00056, hop=0.19, bias=3.0, call=0.5,
           lat=0.0, ov=0.01, osc=0.03, pd=(0, 0), xcs=1, ys=(1, 1), xr=(4,), c2=2, cu=1, cx=2, z1s=(1, 1), zos=1, rbv=0, absv=0, mg=1, lat0=1.9, kb=0.0048,
           foldm=0, hd=1, nv=8, bhs=0, f2=(1,) * 8)
XW = 8224
LN2 = math.log(2.0)
Q = 65536.0
MK = 128 * Q
EW = 704
BLOCK = dict(Oh=(0, 0.5), I128=(128, 0), I32=(32, 0), Iq=(Q, 0), I256=(256, 0), Om256=(0, -256), Tp=(132 * Q, 0), Tb=(-131 * Q, 0), Bh=(0.5, 0.5),
             M1=(-57344, 65536), I60k=(61440, 0), Im128=(-128, 0), Iiq=(1 / Q, 0), Ifl=(2.0 ** 26, 0), M3=(2.0 ** 26, -0.25),
             M2=(-4, 256), I4=(4, 0), Os=(0, 2.0 ** 126), Hm=(0.5, -0.5), Im1536=(-1536, 0), Im2k=(-2048, 0),
             Im256=(-256, 0), Im1=(-1, 0), I512=(512, 0), M4=(-512, 512), Im512=(-512, 0), Oq=(0, Q), Bmh=(-1 / MK, -1 / MK),
             Bm8h=(-8192 / MK, -8192 / MK), I256h=(256 / MK, 0), Im251=(-251, 0), Bm256=(-256, -256), B4k=(4096, 4096), I4k=(4096, 0),
             Im64q=(-64 * Q, 0), **{"Iv%d" % t: (Q * (t + 1) / MK, 0) for t in range(NV)},
             Imh=(-0.5, 0), Imq=(-Q, 0), Im129=(-129, 0), Bq=(Q, Q), Bmq=(-Q, -Q), Bqh=(Q / MK, Q / MK), Bmqh=(-Q / MK, -Q / MK), Om2k=(0, -2048))
MATS = ["I", "B", "O", "L3", "D", "Is", "MP", "Bk", "Bkm", "Bkq", "Bj"] + list(BLOCK)
BF, F32, I32, U16 = "bfloat16", "float32", "int32", "uint16"
SCRATCH = {}
for _d, _l in ((BF, dict(X=XW, exr=1024, q1=1024, ne=1024, dl=1024, sel=1024, Sg=1024, Zn=1024, EZ=10 * EW, Z1=2 * EW, Z2=2 * EW, og=1024,
                         FO=10 * 128, FI=8 * 128, F0=128, xs=2048, xcr=2048, dd=2048, ad=2048, mxs=2048, m0=1024, CM=128 * len(MATS), ONE=512,
                         Ws=144, Ww=144, cpos=8, ramp=64)),
               (F32, dict(hf=16, dk=1024, MI=32 + 5 * 288, MIi=8 * 160, PZ=320, CF=5 * 128, col=16, cp0=8, thr=8, acc=8, dg=64)),
               (I32, dict(dnI=1024, coli=8, wtI=4, thI=4, hi=24, ai=64)), (U16, dict(cu=8, hu=8, zu=8, at=128, cw=128)),
               (BF, dict.fromkeys("psr dvr dvx0 u b1 pwc P pcx key Jh Pp key2 J2h vb Bh2 vj neo ps4 ps2 pw2 mx mp clash khi klo "
                                  "Yb rb s1 s2 s3 s4 op od xc zc zm Bh old keep new Tv Tw zero Wb Ro".split(), 128)),
               (F32, dict.fromkeys("diff chi key7 kr sf yf rf cs zs t1 nx0 hw dh".split(), 128)),
               (I32, dict.fromkeys("nmr n dv1 ki kc kd ta t3 t4 nf ri".split(), 128))):
    for _k, _w in _l.items():
        SCRATCH[_k] = ("sbuf", [128, _w], _d)
for _b in range(8):
    SCRATCH["B%d" % _b] = ("psum", [128, 512], F32)
LOADS = ["ps", "dv", "ex0", "dn0", "nm", "ex1", "xt", "dn1", "wt", "th"]
STORES = ["yn", "yp", "yd", "yg0", "yg1", "yx0", "yx1"]
SEMAPHORES = ["sV", "sS", "sP", "sG"] + ["l" + x for x in LOADS] + ["o" + x for x in STORES] + \
             ["%s%s%d" % (x, k, t) for x in ("", "x") for k in "emf" for t in range(2 * NV - 2)]


def R(name, lo=0, hi=None, step=1):
    if hi is None:
        hi = SCRATCH[name][1][1]
    return ("ap", name, lo, hi, step)


def W(name, lo, n):
    return ("ap", name, lo, lo + n, 1)


def part(x, j, parts):
    n = (x[3] - x[2]) // parts
    return W(x[1], x[2] + j * n, n)


def IND(win, off):
    return ("ind", win, off)


def M(name):
    return W("CM", 128 * MATS.index(name), 128)


def _isap(x):
    return isinstance(x, tuple) and len(x) > 0 and x[0] in ("ap", "ind")


def _parts(x):
    return [x] if x[0] == "ap" else [x[1], x[2]]


def _n(x):
    if x[0] == "ind":
        return 16 * _n(x[2])
    return len(range(x[2], x[3], x[4]))


def _meet(a, b):
    if a[3] <= b[2] or b[3] <= a[2]:
        return False
    return not (a[4] == b[4] and a[4] > 1 and (a[2] - b[2]) % a[4] != 0)


def _psum(x):
    return x[1][0] == "#"


def build():
    ops, cur, tiles = [], [0], [0]

    def add(eng, calls, reads, writes, cost, lat=0.0, sem=None, **kw):
        rd = [p for x in reads if _isap(x) for p in _parts(x)]
        wr = []
        for x in writes:
            if x[0] == "ind":
                wr.append(x[1]); rd.append(x[2])
            else:
                wr.append(x)
        tile = [x[1] for x in rd + wr if _psum(x)]
        ops.append(dict(eng=eng, calls=calls, rd=rd, wr=wr, cost=cost, lat=lat, sem=sem, h=cur[0], tile=tile[0] if tile else None, **kw))

    def two(*xs):
        return all(not _psum(p) and SCRATCH[p[1]][2] in (BF, U16) for x in xs if _isap(x) for p in _parts(x)[:1])

    def vc(out, ins, tt=False):
        n = _n(out)
        if out[0] == "ind":
            c = 3.5 * n + 60
        elif ins and ins[0][0] == "ind":
            c = 1.5 * n + 60
        elif tt:
            c = n * (1 if any(_psum(x) for x in ins) else 2)
        else:
            c = n * (0.5 if two(out, *ins) else 1)
        return OPT["ov"] + max(64, c) * 0.00083

    def tt(out, a, b, op):
        add("V", [("tensor_tensor", (out, a, b, op), {})], [a, b], [out], vc(out, [a, b], True))

    def ts(out, a, s1, s2, op0, op1=None):
        args = (out, a, s1, s2, op0) if op1 is None else (out, a, s1, s2, op0, op1)
        add("V", [("tensor_scalar", args, {})], [a, s1, s2], [out], vc(out, [a]))

    def cp(out, a):
        add("V", [("tensor_copy", (out, a), {})], [a], [out], vc(out, [a]))

    def ms(out, v):
        add("V", [("memset", (out, v), {})], [], [out], vc(out, []))

    def scan(out, d0, d1, op0, op1):
        add("V", [("tensor_tensor_scan", (out, d0, d1, 0.0, op0, op1), {})], [d0, d1], [out], vc(out, [d0, d1]))

    def act(out, a, f, bias=None, scale=None, acc=None, more=0.0):
        kw = {k: v for k, v in (("bias", bias), ("scale", scale), ("accum_out", acc)) if v is not None}
        c = _n(out) * 1.5 + 60 if a[0] == "ind" else _n(out)
        add("S", [("activation", (out, a, f), kw)], [a, bias, scale], [out] + ([acc] if acc else []), more + OPT["osc"] + max(64, c) * 0.00083)

    def fetch(out, a, scalar):
        act(out, a, F.Copy) if scalar else cp(out, a)

    def fresh(n):
        tiles[0] += 1
        return W("#%d" % tiles[0], 0, n)

    def sm(*pieces, n=64, gate=None, onto=None, stay=False):
        whole = onto or fresh(n)
        pieces = [p if isinstance(p, list) else [p] for p in pieces]
        pieces = [p for p in pieces if p]
        for a, piece in enumerate(pieces):
            calls, rd, c = [], [gate], 0.0
            for b, term in enumerate(piece):
                l, r = M(term[0]) if isinstance(term[0], str) else term[0], term[1]
                outs = [R(whole[1], d, 512, 8) for d in range(term[2])] if len(term) == 3 else [whole]
                for d, o in enumerate(outs):
                    first, end = a == 0 and b == 0 and not onto, a == len(pieces) - 1 and b == len(piece) - 1 and not stay
                    alone = first and end
                    calls.append(("matmul", (o, l, r, alone or (first and d == 0), alone or (end and d == len(outs) - 1)), {}))
                    c += max(64, _n(r)) * (4 if SCRATCH[r[1]][2] == F32 else 1) * OPT["pe"]
                rd += [l, r]
            add("P", calls, rd, [whole], c, lat=0.08)
        return whole

    def planes(groups):
        whole, calls, rd = fresh(512), [], []
        for p, terms in enumerate(groups):
            for b, (m, r) in enumerate(terms):
                calls.append(("matmul", (part(whole, p, 8), M(m), r, b == 0, b == len(terms) - 1), {})); rd += [M(m), r]
        add("P", calls, rd, [whole], 64 * len(calls) * OPT["pe"], lat=0.08)
        return whole

    def load(name, dst, lat, q="Y", cols=None):
        add(q, [("load", (dst, name[:2], cols), {})], [], [dst], 0.06 if q != "G" else 0.3, lat=lat, sem="l" + name,
            up=100.0 * (len(LOADS) - LOADS.index(name)) if q != "G" else 0.0)

    def store(name, src, lat, q, cols=None):
        add(q, [("store", (src, name, cols), {})], [src], [], 0.06, lat=lat, sem="o" + name)

    def send(sem, srcs, dst, alu, lat):
        add("G", [("send", (sem, srcs, dst, alu), {})], srcs, [W("@" + sem, 0, 1)], OPT["call"], issue=True)
        kb = len(srcs) * _n(dst) * (4 if SCRATCH[dst[1]][2] == F32 else 2) / 8
        add("D", [], [W("@" + sem, 0, 1)] + srcs, [dst], kb * OPT["kb"], lat=lat, sem=sem, remote=True)

    def iota(out, pat, base, cm):
        kw = {} if SCRATCH[out[1]][2] == I32 else {"allow_small_or_imprecise_dtypes": True}
        add("G", [("iota", (out, pat, base, cm), kw)], [], [out], 0.13 + 2 * _n(out) * 0.00083)

    def fill(out, v):
        iota(out, [[0, _n(out)]], v, 0)

    def diag(out, a, v):
        add("G", [("affine_select", (out, a, [[-1, 128]], A.not_equal, float(v), 0, 1), {})], [a], [out], 0.17 + 256 * 0.00083)

    c = lambda j: W("col", j, 1)
    ci = lambda j: W("coli", j, 1)
    load("ps", R("psr"), 2.1); load("dv", R("dvr"), 2.2); load("ex0", W("exr", 0, 512), 2.7, cols=(0, 512))
    load("dn0", W("dnI", 0, 512), 3.6, cols=(0, 512)); load("nm", R("nmr"), 3.8); load("ex1", W("exr", 512, 512), 4.3, cols=(512, 1024))
    load("xt", R("X", 0, 4096), 8.2); load("dn1", W("dnI", 512, 512), 9.2, cols=(512, 1024))
    iota(ci(0), [[1, 1]], 0, 1); iota(R("chi"), [[1, 8], [0, 16]], 0, 0); iota(R("diff"), [[-1, 128]], 0, 1); iota(R("cp0"), [[512, 8]], 0, 0)
    load("wt", W("wtI", 0, 1), 3.0, "G"); load("th", W("thI", 0, 1), 3.0, "G")
    ts(ci(1), ci(0), 15, None, A.bitwise_and); ts(ci(2), ci(0), 4, None, A.arith_shift_right)
    cp(W("col", 0, 2), W("coli", 1, 2))
    ts(M("B"), R("chi"), c(1), None, A.is_equal); ts(M("I"), R("diff"), 0.0, None, A.is_equal); tt(M("O"), M("B"), M("I"), A.subtract)
    act(M("Is"), M("I"), F.Exp, bias=-200.0, scale=200.0 + 124 * LN2, more=1.3)
    act(c(2), c(0), F.Identity, bias=1.5); act(c(3), c(0), F.Identity, bias=1.0); act(c(5), c(0), F.Identity, bias=-16.0, scale=0.5)
    act(c(8), c(0), F.Copy, scale=32.0); act(R("cpos"), R("cp0"), F.Identity, bias=c(8))
    ts(R("s1"), R("diff"), 0.0, 15.0 / 16, A.is_lt, A.mult); ts(R("s2"), R("s1"), -7.0 / 16, 2.0 ** 62, A.add, A.mult)
    ts(R("op"), M("O"), 2.0 ** 61, None, A.mult); tt(M("L3"), R("op"), R("s2"), A.mult)
    ts(R("s3"), R("diff"), -1.0, None, A.is_equal); tt(R("vj"), R("s3"), M("B"), A.mult); tt(R("s4"), M("I"), R("vj"), A.subtract)
    ts(M("D"), R("s4"), 2.0 ** 62, 2.0 ** 61, A.mult, A.mult)
    fill(R("zero"), 0)
    late = list(BLOCK).index("Tb" if OPT["mg"] == 3 else "M2" if OPT["mg"] == 2 else "I4k")
    for j, (nme, (a, b)) in enumerate(BLOCK.items()):
        base, v = ("I", a) if b == 0 else ("O", b) if a == 0 else ("B", b)
        if abs(v) > 1e29:
            ts(M(nme), M(base), v / 2.0 ** 63, 2.0 ** 63, A.mult, A.mult)
        elif b == 0 and j >= late and OPT["mg"]:
            diag(M(nme), R("zero"), a)
        elif j % 2 == 0 and j < OPT["nv"]:
            ts(M(nme), M(base), float(v), None, A.mult)
        else:
            act(M(nme), M(base), F.Copy, scale=float(v))
        if a and b and a != b:
            diag(M(nme), M(nme), a)
    act(M("Bk"), M("B"), F.Copy, scale=c(3)); act(M("Bj"), M("B"), F.Copy, scale=c(5)); act(M("Bkm"), M("Bk"), F.Copy, scale=-1.0)
    act(M("Bkq"), M("Bk"), F.Copy, scale=Q)
    Bfh, Bf592, Of, If, If16 = (W("CF", 128 * j, 128) for j in range(5))
    act(Bfh, M("B"), F.Copy, scale=0.5); act(Bf592, M("B"), F.Copy, scale=592.0); fill(Of, 1); fill(R("ONE"), 1); act(If, M("I"), F.Copy)
    act(If16, M("I"), F.Copy, scale=16.0)
    for h in range(2):
        fill(W("Z1", EW * h + 576, 128), int(MK))
        if not all(OPT["f2"]):
            fill(W("Z2", EW * h + 512, 192), int(MK))
        if OPT["foldm"]:
            fill(W("PZ", 160 * h, 96), 0)
    fill(R("Ws"), 0); cp(R("Ws", 15, 143, 16), R("CM", M("B")[2], M("B")[3], 16))
    ts(R("key2"), R("Ws", 15, 143), 2.0 ** 63, 2.0 ** 63, A.mult, A.mult); tt(M("MP"), R("key2"), M("Is"), A.add)
    ts(c(9), W("wtI", 0, 1), 32.0, None, A.add)
    if not OPT["hd"]:
        ts(R("Ww"), R("Ws"), c(9), None, A.mult)
    ts(c(10), W("thI", 0, 1), -8192.0, None, A.add)
    ts(c(11), W("ONE", 0, 1), -2.0 ** -60, 2.0 ** -63, A.mult, A.mult)
    iota(W("rf", 0, 64), [[0, 4], [1, 16]], 0, 0); ts(ci(3), ci(0), 1, None, A.add); ts(ci(4), ci(3), 15, None, A.bitwise_and); cp(c(13), ci(4))
    ts(W("cs", 0, 64), W("rf", 0, 64), c(0), 16384.0, A.is_equal, A.mult); ts(W("yf", 0, 64), W("rf", 0, 64), c(13), -8192.0, A.is_equal, A.mult)
    tt(R("dg"), W("cs", 0, 64), W("yf", 0, 64), A.add); ts(c(12), c(0), 14.5, 8192.0, A.is_lt, A.mult)
    if OPT["hd"]:
        act(R("Wb"), M("B"), F.Copy, scale=c(9)); act(c(14), c(12), F.Copy, scale=1024.0)
        act(W("dh", 0, 64), R("dg"), F.Copy, scale=1024.0); act(W("dh", 64, 64), R("dg"), F.Copy, scale=1024.0)
    iota(R("ramp"), [[8, 64]], 0, 0)
    fill(W("m0", 0, 512), 0); fill(W("m0", 512, 512), 0); ms(R("m0", 0, 1024, 16), -1024.0); fill(R("X", 4096, 4112), -1024); fill(W("MI", 0, 32), 0)
    ONE = W("ONE", 0, 64)
    ts(R("s1"), R("psr"), 0.0, 4.0, A.is_ge, A.mult); tt(R("F0"), R("s1"), R("psr"), A.add)
    act(R("sf"), R("dvr"), F.Identity, bias=4096.0, scale=4096.0)
    ts(R("op"), R("psr"), 16.0, 16.0, A.mult, A.add); ts(R("od"), R("dvr"), 1.0, None, A.add); tt(R("dvx0"), R("op"), R("od"), A.min)

    def marks(h, tile):
        for d in range(8):
            ts(R("Zn", 512 * h + d, 512 * h + 512, 8), tile, float(d + 1), MK, A.is_equal, A.mult)
        return W("Zn", 512 * h, 512)

    def names(z):
        return 32 + 288 * (z // 2) + 160 * (z % 2)

    for h in range(2):
        cur[0] = h
        o, H = 512 * h, lambda name: W(name, 64 * h, 64)
        before = fresh(511); ts(before, W("dnI", o, 511), -4096.0, None, A.add)
        tt(W("dk", o + 1, 511), before, W("dnI", o + 1, 511), A.subtract); ms(R("dk", o, o + 512, 8), 4194304.0)
        ts(H("key7"), R("dnI", o + 7, o + 512, 8), 32768.0, None, A.add)
        ts(H("ta"), R("dnI", o, o + 512, 8), 5, None, A.arith_shift_right); cp(H("khi"), H("ta"))
        ts(H("t4"), R("dnI", o, o + 512, 8), 31, None, A.bitwise_and); cp(H("klo"), H("t4"))
        ex, q1, Z = W("exr", o, 512), W("q1", o, 512), marks(h, H("dvx0"))
        ts(q1, ex, -2.0, 34.0, A.is_equal, A.mult)
        tt(W("EZ", EW * h, 512), sm([("Iq", R("ONE")), ("Iq", ex), ("Iq", q1)], n=512), Z, A.max)
        act(W("dl", o, 512), sm([("I", ex), ("I", q1), ("Iiq", Z)], n=512), F.Relu, bias=-127.0)
        act(W("EZ", EW * h + 512, 64), sm([("I", R("dl", o + d, o + 512, 8)) for d in range(8)]), F.Copy)
        tt(W("MI", names(h), 64), H("sf"), H("nmr"), A.add); cp(H("nx0"), H("nmr"))
    if 2 in OPT["pd"]:
        ms(R("xs"), 0.0)

    def diagonal(out, tile, tmp, times=1.0):
        scan(tmp, R("dg"), tile, A.add, A.min); ts(out, R(tmp[1], tmp[2] + 15, tmp[3], 16), c(12), times, A.add, A.mult)

    def record(out, ndv, nx, dP, Ph, t, b1):
        tt(out, sm([(If, nx), ("I4k", dP), ("Iv%d" % t, Ph)], ("Im64q", b1)), ndv, A.max)

    def differs(out, tile, big, scalar):
        act(out, tile, F.Abs, scale=big) if scalar else ts(out, tile, 0.0, big, A.not_equal, A.mult)

    def visit(t, h):
        cur[0] = h
        last, z, o = t == NV - 1, 2 * t + h, 512 * h
        H = lambda name: W(name, 64 * h, 64)
        eo, io_, fo = EW * z, names(z), 128 * z
        ps, Bh = H("F0") if t == 0 else W("FI", fo - 256, 64), H("Bh")
        if t:
            tt(Bh, W("FI", fo - 192, 64), sm(("Bh", W("FI", fo - 192, 64))), A.is_gt)
        ndv, n2, PK = W("MI", io_, 64), W("MI", io_ + 64, 64), W("PZ", 160 * h + 96, 64)
        E, Oo, dP, Ph = W("EZ", eo, 512), W("EZ", eo + 512, 64), W("EZ", eo + 576, 64), W("EZ", eo + 640, 64)
        P, Pp, pcx, b1, Tv = H("P"), H("Pp"), H("pcx"), H("b1"), H("Tv")
        nx, thr = (W("MIi", 160 * (z - 2) + 96, 64), W("thr", t, 1)) if t else (H("nx0"), c(10))
        if t and h == 0:
            act(thr, W("MIi", 160 * (2 * t - 1), 1), F.Identity, bias=c(10), scale=32.0)
        first = fresh(512)
        scan(first, W("dk", o, 512), E, A.add, A.min)
        tt(H("kr"), R(first[1], 7, 512, 8), H("key7"), A.add)
        low = 0.0 if t else 1.0
        act(H("u"), ps, F.Exp, bias=(123 - low) * LN2, scale=-LN2); ts(b1, ps, 0.5 - low, None, A.is_le)
        act(H("ps4"), ps, F.Relu, bias=low)
        tt(P, H("u"), sm([("L3", b1), ("Oh", H("u"))]), A.is_gt)
        if t > 0:
            record(ndv, W("MIi", 160 * (z - 2) + 32, 64), nx, dP, Ph, t - 1, b1)
        sel, Sg, n = W("sel", o, 512), W("Sg", o, 512), OPT["c2"]
        selv = OPT["selv"] and t
        if selv:
            row = sm(("Iiq", P, 8), n=512)
        else:
            row = sm([("Iiq", E)] if t else [("I", W("exr", o, 512)), ("I", W("q1", o, 512))], ("I128", P, 8), n=512, gate=ps)
        for j in range(n):
            if selv:
                tt(part(sel, j, n), part(row, j, n), part(E, j, n), A.mult)
            else:
                act(part(sel, j, n), part(row, j, n), F.Relu, bias=low - 128)
        for j in range(n):
            act(part(Sg, j, n), sm(("B", part(sel, j, n)), n=512 // n), F.Sign, bias=c(2), scale=-1.0)
        tt(pcx, sm([("Tb", b1), ("Tp", P)]), H("kr"), A.is_gt)
        act(H("pwc"), sm([("I", H("ps4")), ("Om256", pcx)]), F.Exp, bias=-125 * LN2, scale=LN2)
        tt(H("ki"), sm([("I32", H("khi")), ("I", H("klo")), ("I60k", b1), ("M1", P), ("I60k", pcx)]), H("kr"), A.min)
        ts(H("kc"), H("ki"), 4095, None, A.bitwise_and); ts(H("kd"), H("ki"), 12, 15, A.arith_shift_right, A.bitwise_and)
        G = sm([("MP", P)] + ([("Is", Bh)] if t else []), [("D", R("Sg", o + d, o + 512, 8)) for d in range(8)], gate=part(sel, 0, n))
        tt(H("key"), G, H("pwc"), A.min)
        tt(Pp, H("key"), sm(("Bh", H("key"))), A.is_gt)
        tt(PK, H("kc"), Pp, A.mult)
        K = sm((Bfh, PK))
        K37 = sm([(If16, nx), ("Ifl", b1)], ("M3", Pp), (Bf592, PK), gate=H("key"))
        tt(H("t1"), K, nx, A.mult)
        diagonal(W("cu", 4 * h, 4), K, H("cs"), 2.0) if OPT["pd"][h] else ts(H("cw"), K, 2.0, None, A.mult)
        tt(H("t3"), K37, H("t1"), A.add); ts(H("t4"), H("t3"), 4, 4095 | 3 << 22, A.arith_shift_right, A.bitwise_and)
        ts(H("at"), H("t4"), 4096.0, None, A.min)
        tt(dP, H("kd"), Pp, A.mult); ts(Ph, dP, 0.5, MK, A.is_ge, A.mult)
        tt(H("ps2"), sm(([("I", ps), ("Im1", H("ps4"))] if t else []) + [("I4", P), ("M2", Pp)]), H("ps4"), A.min)
        tt(H("key2"), sm(("Os", Pp)), H("key"), A.min)
        act(H("J2h"), sm(("Hm", H("key2"))), F.Sign, bias=c(11))
        if t:
            act(H("Bh2"), sm([("I", Bh), ("Im1", Pp)]), F.Relu)
        mine = [("Im128", P), ("I256", b1), ("I256", pcx), ("Im256", Pp)] + ([("Bk", H("Bh2"))] if t else [])
        zu = W("zu", 4 * h, 4)
        diagonal(zu, sm([("I", R("ramp")), ("B", dP), ("Bmh", Ph)]), H("zs"))
        z1, z2, zo = W("Z1", EW * h, 512), W("Z2", EW * h, 512), W("Z1", EW * h + 512, 64)
        if not last:
            two_ = OPT["f2"][z]
            if two_:
                tt(z2, sm(("Bkq", Pp, 8), n=512), E, A.is_equal)
            else:
                differs(z1, sm(("Iiq", E), ("Bkm", Pp, 8), n=512, gate=H("key")), MK, OPT["z1s"][h])
            act(H("vj"), sm([("Im2k", P), ("Im1536", Pp), ("Bj", H("J2h"))]), F.Relu, bias=1501.0)
            tt(Tv, sm(mine), H("vj"), A.max)
            differs(zo, sm([("I", Oo), ("Bkm", Pp)]), 64.0, OPT["zos"])
            act(z1 if two_ else z2, sm([("Iiq", E), ("I512", b1, 1), ("M4", P, 1), ("I512", pcx, 1), ("Im512", Pp, 1)], [("I4k", z2)] if two_ else [],
                                       ("Im1", Tv, 8), n=512, gate=H("key2")), F.Relu, scale=-Q)
            tt(H("zc"), IND(E, zu), Ph, A.max); cp(IND(E, zu), H("zc"))
            send("e%d" % z, [W("EZ", eo, EW), W("Z1", EW * h, EW), W("Z2", EW * h, EW)][:3 - two_], W("EZ", eo + 2 * EW, EW), 3, OPT["lat0"])
            if OPT["foldm"]:
                tt(n2, sm(("Oq", Pp)), nx, A.min)
            else:
                tt(H("sf"), sm(("Oq", Pp)), nx, A.min); tt(n2, H("sf"), PK, A.add)
            act(H("Jh"), sm([("Im1", P), ("I", Pp)]), F.Relu, acc=W("acc", h, 1))
            if h == 1:
                Ap = sm((Of, W("acc", 0, 2)), n=2)
                ts(W("ai", 0, 32), W("ONE", 0, 32), part(Ap, 0, 2), part(Ap, 1, 2), A.mult, A.add)
                ts(W("ai", 32, 32), W("ai", 0, 32), 7, None, A.bitwise_and); cp(W("MI", io_ - 32, 32), W("ai", 32, 32))
            send("m%d" % z, [W("MI", io_ - 32, 160), W("PZ", 160 * h, 160)][:1 + OPT["foldm"]], W("MIi", 160 * z, 160), OPT["foldm"], OPT["lat0"])
        act(H("pw2"), H("ps2"), F.Exp, bias=-122 * LN2, scale=LN2)
        act(H("mx"), sm(("Hm", H("pw2"))), F.Sign)
        act(H("mp"), sm([("I", H("ps2")), ("I256", H("mx"))]), F.Relu, bias=-260.0)
        if last:
            act(H("vj"), sm([("Im2k", P), ("Om2k", Pp), ("Bj", H("J2h"))]), F.Relu, bias=-35.0)
            tt(H("Tw"), sm(mine + [("Om2k", P)]), H("vj"), A.max)
            ts(H("s4"), ndv, Q, None, A.is_ge); tt(H("neo"), sm(("Bk", Pp)), Oo, A.is_equal)
            act(H("zm"), sm([("I", Oo), ("Im256", H("s4")), ("Im256", H("neo"))]), F.Relu)
            tt(Tv, sm([("I", H("zm")), ("I128", ONE), ("Im2k", P), ("Im2k", Pp)]), H("Tw"), A.max)
            ne, dl, Ef = W("ne", o, 512), W("dl", o, 512), W("q1", o, 512)
            tt(ne, sm(("Bkq", Pp, 8), n=512), E, A.is_equal)
            tt(z2, sm(("Im1", E), ("Iq", Tv, 8), n=512, gate=H("key2")), E, A.min)
            act(Ef, sm(("Im256", ne), ("Iiq", z2), n=512), F.Relu)
            act(dl, Ef, F.Abs, bias=-16.0); ts(W("og", o, 512), dl, -1.0, 15.0, A.mult, A.add)
            tried = IND(W("og", o, 512), zu)
            fetch(H("zc"), tried, True)
        win, g0 = R("X", 0, 4112), 1024 * h
        mxv, lanes = R("mxs", g0 + 15, g0 + 1024, 16), lambda k: R("Ws", 15 - k, 143 - k)
        dd, ad, xcr, n = W("dd", g0, 1024), W("ad", g0, 1024), W("xcr", g0, 1024), OPT["cx"]
        if OPT["pd"][h] == 1:
            xc = H("xc"); big = [("I", mxv)]
            fetch(xc, IND(win, W("cu", 4 * h, 4)), OPT["xcs"])
            for j in range(2):
                fetch(part(dd, j, 2), IND(win, part(H("at"), j, 2)), OPT["ys"][j])
            for j in range(2):
                act(part(ad, j, 2), planes([[("I", R("dd", g0 + k, g0 + 1024, 16)), ("Im1", xc)] for k in range(8 * j, 8 * j + 8)]), F.Abs)
            sums = [[(lanes(k), part(ad, k, 16)) for k in range(8 * j, 8 * j + 8)] for j in range(2)]
        else:
            xc = R("xs" if OPT["pd"][h] else "xcr", g0, g0 + 1024, 16); big = [("I", xc), ("I", mxv)]
            if OPT["pd"][h]:
                fetch(xc, IND(win, W("cu", 4 * h, 4)), OPT["xcs"])
            for j in range(n):
                if OPT["pd"][h]:
                    scan(part(xcr, j, n), W("m0", 0, 1024 // n), part(W("xs", g0, 1024), j, n), A.add, A.max)
                else:
                    act(part(xcr, j, n), IND(win, part(H("cw"), j, n)), F.Copy)
                tt(part(dd, j, n), IND(win, part(H("at"), j, n)), part(xcr, j, n), A.subtract)
                act(part(ad, j, n), part(dd, j, n), F.Abs)
            sums = [[(lanes(k), R("ad", g0 + k, g0 + 1024, 16)) for k in range(16)]]
        ts(H("clash"), sm(("Bm8h", Ph), *sums, gate=part(dd, 0, 2)), thr, None, A.is_le)
        tt(W("FO", fo + 64, 64), H("clash"), H("u"), A.mult)
        tt(W("FO", fo, 64), sm([("Im251", ONE), ("B", H("mp")), ("I256h", Ph)], ("Bm256", H("clash")), gate=part(ad, 0, 2)), H("ps2"), A.max)
        if not last:
            send("f%d" % z, [W("FO", fo, 128)], W("FI", fo, 128), 0, OPT["lat0"])
        scan(W("mxs", g0, 1024), R("m0"), dd, A.add, A.max)
        if t in OPT["xr"]:
            act(H("Yb"), sm(big), F.Relu)
        else:
            act(H("Yb"), sm(big + [("Bm8h", Ph)], ("B4k", H("clash")), gate=part(ad, 1, 2)), F.Relu, bias=8192.0)
        both = [("I", xc), ("I", H("Yb"))]
        if t in OPT["xr"] or not OPT["rbv"]:
            act(H("rf"), sm([("Imh", ONE)] + both), F.Identity, bias=12582912.0, scale=0.5)
            act(H("rb"), H("rf"), F.Identity, bias=-12582912.0)
        else:
            ts(H("ri"), sm(both), 0.5, -0.25, A.mult, A.add)
        if last:
            p9, Bo = W("FO", fo, 64), H("Bh")
            tt(Bo, W("FO", fo + 64, 64), sm(("Bh", W("FO", fo + 64, 64))), A.is_gt)
            tt(H("vb"), sm([("Im129", ONE), ("Iiq", Ph)], ("Bk", Bo), gate=H("clash")), H("zc"), A.max); cp(tried, H("vb"))
            store("yg%d" % h, W("og", o, 512), 2.2, "Y", (o, o + 512))
            ts(H("s1"), p9, -1.0, -2.0, A.is_ge, A.add); ts(H("s2"), p9, -5.0, None, A.add); tt(H("op"), H("s1"), H("s2"), A.max)
            act(H("s3"), p9, F.Relu, bias=1.0, scale=-3.75); record(H("nf"), ndv, PK, dP, Ph, t, H("s3"))
            ts(H("n"), H("nf"), 4095, None, A.bitwise_and); cp(H("yf"), H("n"))
            ts(H("dv1"), H("nf"), 12, 15, A.arith_shift_right, A.bitwise_and); ts(H("od"), H("dv1"), -1.0, None, A.add)

    for t in range(NV):
        visit(t, 0); visit(t, 1)
        for lo, n in (((0, 4), (4, 4)) if t == NV - 1 else ((0, 8),)):
            cur[0] = 1 if lo + n == 8 else 0
            if OPT["hd"]:
                scan(W("hw", 16 * lo, 16 * n), W("dh", 0, 16 * n), sm((R("Wb"), W("Yb", 16 * lo, 16 * n)), n=16 * n), A.add, A.min)
                hs = R("hw", 16 * lo + 15, 16 * (lo + n), 16)
                ts(W("hi", lo, n), hs, c(14), None, A.add)
            else:
                hs = sm([(R("Ww", 15 - k, 143 - k), R("Yb", 16 * lo + k, 16 * (lo + n), 16)) for k in range(16)], n=n)
                cp(W("hi", lo, n), hs)
            ts(W("hi", 8 + lo, n), W("hi", lo, n), 31, None, A.bitwise_and)
            if t in OPT["xr"]:
                tt(W("hi", 16 + lo, n), W("cpos", lo, n), W("hi", 8 + lo, n), A.add)
                ts(W("hu", lo, n), W("hi", 16 + lo, n), -512.0 * lo, None, A.add)
                col = IND(W("X", 512 * lo, 512 * n), W("hu", lo, n))
                fetch(W("old", 16 * lo, 16 * n), col, True)
                for h in range(lo // 4, (lo + n) // 4):
                    H, Ph = lambda name: W(name, 64 * h, 64), W("EZ", EW * (2 * t + h) + 640, 64)
                    tt(H("keep"), sm([("Iq", ONE), ("Bmqh", Ph)], ("Bq", H("clash")), gate=H("rb")), H("old"), A.min)
                    tt(H("new"), sm([("Imq", ONE), ("Bqh", Ph), ("I", H("rb"))], ("Bmq", H("clash"))), H("keep"), A.max)
                cp(col, W("new", 16 * lo, 16 * n))
            else:
                ts(W("hf", lo, n), W("hi", lo, n), 200000.0, 4128.0, A.is_ge, A.mult); tt(W("hf", 8 + lo, n), W("hf", lo, n), W("cpos", lo, n), A.add)
                tt(W("hi", 16 + lo, n), W("hf", 8 + lo, n), W("hi", 8 + lo, n), A.add)
                ts(W("hu", lo, n), W("hi", 16 + lo, n), -512.0 * lo, None, A.add)
                cp(IND(R("X", 512 * lo, XW), W("hu", lo, n)), W("ri" if OPT["rbv"] else "rb", 16 * lo, 16 * n))
            if n == 4:
                store("yx%d" % cur[0], W("X", 512 * lo, 2048), 3.0, "YS"[cur[0]], (512 * lo, 512 * lo + 2048))
    store("yp", R("op"), 2.0, "Y"); store("yn", R("yf"), 2.0, "Y"); store("yd", R("od"), 2.0, "Y")
    return ops


def depend(ops):
    deps, hist = [set() for _ in ops], {}
    for i, o in enumerate(ops):
        for x in o["rd"]:
            deps[i].update(j for j, y, w in hist.get(x[1], []) if w and _meet(x, y))
        for x in o["wr"]:
            deps[i].update(j for j, y, w in hist.get(x[1], []) if _meet(x, y))
        for x in set([] if o.get("issue") else o["rd"]):
            hist.setdefault(x[1], []).append((i, x, False))
        for x in set(o["wr"]):
            hist[x[1]] = [e for e in hist.get(x[1], []) if e[1] != x] + [(i, x, True)]
        deps[i].discard(i)
    return deps


def replay(ops, s, hop, sc):
    fin, free = {}, {}
    for i in s["order"]:
        o = ops[i]; e = o["eng"]; t = free.get(e, 0.0)
        for j in s["waits"][i]:
            t = max(t, fin[j] + hop)
        free[e] = t + o["cost"] * sc.get(e, 1.0)
        fin[i] = free[e] + o["lat"] * (sc.get("L", 1.0) if o.get("remote") else 1.0)
    return max(fin.values())


CASES = ((0.165, {}), (0.2, {"V": 1.3, "S": 1.3, "P": 1.3, "L": 1.2, "D": 2.0}))


def plan(ops, rounds, moves):
    deps, rs, n = depend(ops), np.random.RandomState(OPT["seed"]), len(ops)
    need, eng, tile, lat = direct(deps)[0], [o["eng"] for o in ops], [o["tile"] for o in ops], [o["lat"] for o in ops]
    hop, up = OPT["hop"], [bool(o.get("up")) for o in ops]
    cost = [o["cost"] * (OPT["slow"] if o["eng"] in "VSP" else 1) for o in ops]
    loads = [i for i in range(n) if up[i]]
    for a, b in zip(loads, loads[1:]):
        need[b].append(a)
    inline = lambda j, i: eng[j] == eng[i] == "P" or (up[j] and up[i])
    succ = [[] for _ in ops]
    for i in range(n):
        for j in need[i]:
            succ[j].append(i)
    before = [[(j, 0.0 if inline(j, i) else lat[j] + hop) for j in need[i]] for i in range(n)]
    after = [[(k, 0.0 if inline(i, k) else lat[i] + hop) for k in succ[i]] for i in range(n)]
    timed = [[j for j in need[i] if not inline(j, i)] for i in range(n)]
    users, hold = {}, {}
    for i in range(n):
        if tile[i]:
            users[tile[i]] = users.get(tile[i], 0) + 1
            hold[tile[i]] = hold.get(tile[i], 0.28) + cost[i] + (0.0 if eng[i] == "P" else hop)
    cc = [[o["cost"] * sc.get(o["eng"], 1.0) for o in ops] for h, sc in CASES]
    ll = [[o["lat"] * (sc.get("L", 1.0) if o.get("remote") else 1.0) + h for o in ops] for h, sc in CASES]

    def issue(start):
        left, todo, bank, idle, last = [len(x) for x in need], dict(users), {}, list(range(8)), [{} for _ in range(8)]
        fins, free, order, wait = [[0.0] * n for _ in CASES], [dict.fromkeys("VSPGYD", 0.0) for _ in CASES], [], []
        for i in sorted(range(n), key=lambda i: (-1 if up[i] else start[i], i)):
            wait.append(i)
            while True:
                i = next((k for k in wait if not left[k] and (not tile[k] or tile[k] in bank or idle)), None)
                if i is None:
                    break
                wait.remove(i)
                v, e, more = tile[i], eng[i], timed[i]
                if v:
                    if v not in bank:
                        b = min(idle, key=lambda b: max([fins[0][j] for j in last[b].values()] + [0.0]))
                        idle.remove(b); bank[v] = b
                        more = more + [j for e2, j in last[b].items() if not e2 == e == "P"]
                    else:
                        b = bank[v]
                        more = more + [j for e2, j in last[b].items() if e2 != e]
                    last[b][e] = i; todo[v] -= 1
                    if not todo[v]:
                        idle.append(b)
                for fin, at, co, la in zip(fins, free, cc, ll):
                    t = at[e]
                    for j in more:
                        if fin[j] > t:
                            t = fin[j]
                    t += co[i]; at[e] = t; fin[i] = t + la[i]
                order.append(i)
                for k in succ[i]:
                    left[k] -= 1
        return None if wait else (sum(max(x) for x in fins), order, bank)

    key = np.zeros(n)
    for i in range(n - 1, -1, -1):
        key[i] = min([key[k] - g for k, g in after[i]] + [-lat[i]]) - cost[i]
    hh = np.array([o["h"] for o in ops])
    key, best, cur = key + OPT["bias"] * hh, None, None
    for it in range(rounds):
        end = pack(before, succ, eng, cost, key, [0.0] * n)
        back = np.array(pack(after, need, eng, cost, -np.array(end) - lat, lat, tile, hold))
        start = back.max() - back
        r = issue(start.tolist())
        if cur is None or (r and r[0] <= cur[0] - OPT["heat"] * (1 - it / rounds) * math.log(1 - rs.rand())):
            cur, base = r, start
            if r and (best is None or r[0] < best[0]):
                best = r
        t0 = rs.rand() * base.max()
        win = (base >= t0) & (base < t0 + OPT["span"])
        if rs.rand() < 0.3:
            key = base + win * (hh - 0.5) * rs.randn() * 1.5
        else:
            key = base + win * OPT["amp"] * rs.rand() * rs.randn(n)
    return tie(ops, deps, *(refine(ops, deps, best[1], best[2], moves, rs) if moves else best[1:]))


def direct(deps):
    anc, need = [0] * len(deps), []
    for i in range(len(deps)):
        keep, far = [], 0
        for j in sorted(deps[i], reverse=True):
            if not far >> j & 1:
                keep.append(j)
            far |= anc[j] | 1 << j
        anc[i] = far; need.append(keep)
    return need, anc


def pack(links, back, eng, cost, key, first, tile=None, hold=None):
    n = len(eng)
    left, seen, end = [len(x) for x in links], [False] * n, [0.0] * n
    st, en, use, upto = {e: [] for e in "VSPGYD"}, {e: [] for e in "VSPGYD"}, np.zeros(6000, np.int8), {}
    for top in np.argsort(key, kind="stable").tolist():
        seen[top] = True
        stack = [] if left[top] else [top]
        while stack:
            i = stack.pop()
            t = first[i]
            for j, g in links[i]:
                if end[j] + g > t:
                    t = end[j] + g
            s, e, c, v = st[eng[i]], en[eng[i]], cost[i], tile[i] if tile else None
            while True:
                k = m = len(s); lo = 0
                while lo < k:
                    mid = (lo + k) // 2
                    if e[mid] > t:
                        k = mid
                    else:
                        lo = mid + 1
                while k < m and s[k] < t + c - 1e-9:
                    if e[k] > t:
                        t = e[k]
                    k += 1
                if v is None or v in upto:
                    break
                a, b = int(t * 20), int((t + hold[v]) * 20) + 1
                full = np.flatnonzero(use[a:b] >= OPT["cap"])
                if not len(full):
                    use[a:b] += 1; upto[v] = b
                    break
                t = (a + int(full[-1]) + 1) / 20 + 1e-6
            if v is not None:
                b = int((t + c + 0.2) * 20) + 1
                if b > upto[v]:
                    use[upto[v]:b] += 1; upto[v] = b
            s.insert(k, t); e.insert(k, t + c); end[i] = t + c
            for j in back[i]:
                left[j] -= 1
                if not left[j] and seen[j]:
                    stack.append(j)
    return end


def schedule(ops, deps, dp):
    n, HOP = len(ops), OPT["hop"]
    succ = [[] for _ in ops]
    for i in range(n):
        for j in deps[i]:
            succ[j].append(i)
    pri = [0.0] * n
    for i in range(n - 1, -1, -1):
        pri[i] = ops[i]["cost"] + ops[i]["lat"] + max([pri[k] + HOP for k in succ[i]] + [0.0])
    pri = [p + x - OPT["bias"] * o["h"] + o.get("up", 0.0) for p, x, o in zip(pri, dp, ops)]
    tile = [o["tile"] for o in ops]
    users = {}
    for i in range(n):
        if tile[i]:
            users.setdefault(tile[i], []).append(i)
    todo = {v: len(u) for v, u in users.items()}
    outer = {v: set(j for i in u for j in deps[i]) - set(u) for v, u in users.items()}
    bank, held, lastuse = {}, [None] * 8, [{} for _ in range(8)]
    left = [len(d) for d in deps]
    ready = {e: [] for e in "VSPGY"}
    for i in range(n):
        if left[i] == 0:
            ready[ops[i]["eng"]].append(i)
    free = {e: 0.0 for e in ready}
    fin, start, order, rdy, did = [0.0] * n, [0.0] * n, [], [0.0] * n, [False] * n
    while len(order) < n:
        pick = None
        idle = [b for b in range(8) if held[b] is None]
        for force in (False, True):
            for e, lst in ready.items():
                st, bk = {}, {}
                for i in lst:
                    s, v = max(free[e], rdy[i]), tile[i]
                    if v:
                        if v in bank:
                            b = bank[v]
                        elif idle and (force or len(idle) > OPT["keep"] or all(did[j] for j in outer[v])):
                            b = min(idle, key=lambda b: max([fin[j] for e2, j in lastuse[b].items() if e2 != e] + [0.0]))
                        else:
                            continue
                        bk[i] = b
                        for e2, j in lastuse[b].items():
                            if e2 != e:
                                s = max(s, fin[j] + HOP)
                    st[i] = s
                if not st:
                    continue
                best = max(st, key=lambda i: pri[i])
                cand = [i for i in st if i == best or st[i] + ops[i]["cost"] <= st[best] + OPT["gap"]]
                first = min(st[i] for i in cand)
                i = max((i for i in cand if st[i] <= first + 0.03), key=lambda i: pri[i])
                if pick is None or st[i] < pick[0]:
                    pick = (st[i], i, bk.get(i))
            if pick:
                break
        if pick is None:
            return None
        s, i, b = pick
        e = ops[i]["eng"]
        ready[e].remove(i); did[i] = True
        if b is not None:
            v = tile[i]
            bank[v] = b; lastuse[b][e] = i; todo[v] -= 1
            held[b] = v if todo[v] else None
        start[i] = s; free[e] = s + ops[i]["cost"]; fin[i] = free[e] + ops[i]["lat"]; order.append(i)
        for k in succ[i]:
            left[k] -= 1
            rdy[k] = max(rdy[k], free[e] if e == "P" and ops[k]["eng"] == "P" else fin[i] + HOP)
            if left[k] == 0:
                ready[ops[k]["eng"]].append(k)
    return dict(tie(ops, deps, order, bank), start=start)


def refine(ops, deps, order, bank, moves, rs):
    n, eng = len(ops), [o["eng"] for o in ops]
    (need, anc), users = direct(deps), {}
    for i in order:
        if ops[i]["tile"]:
            users.setdefault(ops[i]["tile"], []).append(i)
    first = {u[0]: v for v, u in users.items()}
    for u in users.values():
        for a, b in zip(u, u[1:]):
            if eng[a] != eng[b] and not anc[b] >> a & 1:
                need[b].append(a)
    cost = [[o["cost"] * sc.get(o["eng"], 1.0) for o in ops] for h, sc in CASES]
    lat = [[o["lat"] * (sc.get("L", 1.0) if o.get("remote") else 1.0) + h for o in ops] for h, sc in CASES]

    def arcs(order, bank):
        last, prv, at, timed, plain = {}, [-1] * n, {}, [None] * n, [None] * n
        for i in order:
            e = eng[i]; prv[i] = at.get(e, -1); at[e] = i
            a = need[i]
            if i in first:
                b = bank[first[i]]
                if b in last:
                    a = a + users[last[b]]
                last[b] = first[i]
            plain[i] = a
            timed[i] = [j for j in a if eng[j] != "P"] if e == "P" else a
        return prv, timed, plain

    def times(order, prv, timed, c, old=None, lo=0):
        co, la = cost[c], lat[c]
        end, fin = (old[0][:], old[1][:]) if old else ([0.0] * (n + 1), [0.0] * n)
        for i in order[lo:]:
            t = end[prv[i]]
            for j in timed[i]:
                if fin[j] > t:
                    t = fin[j]
            t += co[i]; end[i] = t; fin[i] = t + la[i]
        return end, fin

    prv, timed, plain = arcs(order, bank)
    tm = [times(order, prv, timed, c) for c in range(len(CASES))]
    score = sum(max(t[1]) for t in tm)
    best = (score, order, bank)
    for it in range(moves):
        c = rs.randint(len(CASES)); end, fin = tm[c]
        i, path = fin.index(max(fin)), []
        while i >= 0:
            p = prv[i]
            if p >= 0 and end[p] >= end[i] - cost[c][i] - 1e-9:
                path.append((p, i, True)); i = p
            else:
                j = max(timed[i], key=lambda j: fin[j]) if timed[i] else -1
                if j >= 0 and j not in need[i]:
                    path.append((j, i, False))
                i = j
        a, b, queue = path[rs.randint(len(path))]
        order2, bank2 = order, bank
        if queue:
            for _ in range(rs.randint(4) if rs.randint(2) else 0):
                if prv[a] >= 0:
                    a = prv[a]
            if "up" in ops[b]:
                continue
            lo, hi, after, x = order.index(a), order.index(b), {a}, b
            while prv[x] != a:
                x = prv[x]; after.add(x)
            for k in order[lo:hi + 1]:
                if k not in after and (any(j in after for j in plain[k]) or (k != b and prv[k] in after)):
                    after.add(k)
            if b in after:
                continue
            seg = order[lo:hi + 1]
            order2 = order[:lo] + [k for k in seg if k not in after] + [k for k in seg if k in after] + order[hi + 1:]
        else:
            v, pos = first[b], {x: k for k, x in enumerate(order)}
            lo, hi = pos[b], max(pos[k] for k in users[v])
            busy = set(bank[w] for w, u in users.items() if pos[u[0]] <= hi and max(pos[k] for k in u) >= lo)
            free = [x for x in range(8) if x not in busy]
            if not free:
                continue
            bank2 = dict(bank); bank2[v] = free[rs.randint(len(free))]
        prv2, timed2, plain2 = arcs(order2, bank2)
        tm2 = [times(order2, prv2, timed2, c, tm[c], lo) for c in range(len(CASES))]
        sc2 = sum(max(t[1]) for t in tm2)
        if sc2 <= score - OPT["temp"] * (1 - it / moves) * math.log(1 - rs.rand()):
            order, bank, prv, timed, plain, tm, score = order2, bank2, prv2, timed2, plain2, tm2, sc2
            if score < best[0]:
                best = (score, order, bank)
    return best[1], best[2]


def tie(ops, deps, order, bank):
    pos, cnt, seen, done, waits, marked = {}, {}, {e: {} for e in "VSPGY"}, {}, {}, set()
    rank, lastuse, begun, left, landed = {}, [{} for _ in range(8)], set(), {}, {}
    for k, i in enumerate(order):
        o = ops[i]; e = o["eng"]; rank[i] = k
        key = "" if o.get("issue") else o["sem"] or "s" + e
        cnt[key] = cnt.get(key, 0) + 1; pos[i] = (key, cnt[key])
        need, w = set(deps[i]), []
        if e == "D":
            waits[i], done[i] = [j for j in need if ops[j].get("issue")], {key: 1}
            continue
        if o["tile"]:
            use = lastuse[bank[o["tile"]]]
            need.update(j for e2, j in use.items() if e2 != e or o["tile"] not in begun)
            use[e] = i; begun.add(o["tile"])
        for j in sorted(need, key=lambda j: -rank[j]):
            if e == "P" and ops[j]["eng"] == "P":
                continue
            k2, v = pos[j]
            if ops[j].get("remote"):
                if not seen[e].get("x" + k2) and any(x[1] == y[1] and _meet(x, y) for x in o["wr"] for y in ops[j]["rd"]):
                    left.setdefault(i, []).append(j); seen[e]["x" + k2] = 1
                    w.append(j)
                if not any(x[1] == y[1] and _meet(x, y) for x in o["rd"] + o["wr"] for y in ops[j]["wr"]):
                    continue
                if seen[e].get(k2, 0) < v:
                    landed.setdefault(i, []).append(j); seen[e][k2] = v
                    w.append(j)
            elif seen[e].get(k2, 0) < v:
                w.append(j); marked.add(j)
                for k3, v3 in done[j].items():
                    seen[e][k3] = max(seen[e].get(k3, 0), v3)
        waits[i] = w
        done[i] = dict(seen[e])
        done[i][key] = cnt[key]
    lastof = {}
    for i in order:
        lastof[pos[i][0]] = i
    lastof.pop("")
    marked.update(lastof.values())
    val, tot = {}, {}
    for i in order:
        if i in marked:
            k = pos[i][0]; tot[k] = tot.get(k, 0) + 1; val[i] = tot[k]
    return dict(order=order, waits=waits, val=val, pos=pos, last=lastof, bank=bank, left=left, landed=landed)


PLAN = {}


def rank_program(g, core, T, topo):
    rank = T.rank_of(core)
    if rank is None:
        return
    if not PLAN:
        PLAN["ops"] = build(); PLAN["s"] = plan(PLAN["ops"], OPT["rounds"], OPT["moves"])
    ops, s = PLAN["ops"], PLAN["s"]
    nr = len(T.cores)
    nxt, prv = T.cores[(rank + 1) % nr], T.cores[(rank - 1) % nr]
    rid, pid = topo.addr(nxt)[0], topo.addr(nxt)[1]
    eng_out, n_in = list(topo.engines(core, nxt)), len(topo.engines(prv, core))
    Qu = {"V": g.vector, "S": g.scalar, "P": g.tensor, "G": g, "Y": g.sync}

    def ap(x):
        if not _isap(x):
            return x
        if x[0] == "ind":
            return ap(x[1]).indirect(ap(x[2]))
        t = T["B%d" % s["bank"][x[1]]] if _psum(x) else T[x[1]]
        return t[:, x[2]:x[3]] if x[4] == 1 else t[:, x[2]:x[3]:x[4]]

    def count(j):
        o = ops[j]
        if o.get("remote"):
            return n_in
        return 16 if o["sem"] else s["val"][j]

    def hbm(name, cols):
        return T[name][:] if cols is None else T[name][:, cols[0]:cols[1]]

    for i in s["order"]:
        o = ops[i]
        if o["eng"] == "D":
            continue
        q = Qu[o["eng"]]
        for j in s["waits"][i]:
            if not ops[j].get("remote"):
                q.wait_ge(T.sem[s["pos"][j][0]], count(j))
        for j in s["left"].get(i, []):
            q.wait_ge(T.sem["x" + ops[j]["sem"]], len(eng_out))
        for j in s["landed"].get(i, []):
            q.wait_ge(T.sem[ops[j]["sem"]], n_in)
        ins = None
        for name, args, kw in o["calls"]:
            if name == "load":
                if o["eng"] == "G":
                    ins = q.dma_start(ap(args[0]), hbm(args[1], args[2]), allow_slow_non_contiguous=True)
                else:
                    ins = q.dma_start(ap(args[0]), hbm(args[1], args[2]))
            elif name == "store":
                ins = q.dma_start(hbm(args[1][:2], args[2]), ap(args[0]))
            elif name == "send":
                sem, srcs, dst, alu = args
                if alu == 0:
                    q.remote_dma(ap(dst), ap(srcs[0]), T.sem[sem], T.sem["x" + sem], pid, rid, topo.mask(core, nxt))
                else:
                    q.remote_dma_fused([RemoteDMATransfer(dst_ids=[DstId(rid=rid, pnc=pid)], dma_engine_mask=topo.mask(core, nxt), remote_sem=T.sem[sem],
                                                          srcs=[ap(x) for x in srcs], dsts=[ap(dst)], alu_op=alu)], local_sem=T.sem["x" + sem])
            else:
                a = [ap(x) for x in args]; k = {kk: ap(v) for kk, v in kw.items()}
                if name == "tensor_tensor":
                    ins = q.tensor_tensor(*a)
                elif name == "tensor_scalar":
                    ins = q.tensor_scalar(*a)
                elif name == "tensor_copy":
                    ins = q.tensor_copy(*a)
                elif name == "memset":
                    ins = q.memset(*a)
                elif name == "tensor_tensor_scan":
                    ins = q.tensor_tensor_scan(*a)
                elif name == "activation":
                    ins = q.activation(*a, **k)
                elif name == "matmul":
                    ins = q.matmul(*a)
                elif name == "affine_select":
                    ins = q.affine_select(*a)
                else:
                    ins = q.iota(*a, **k)
        if o.get("issue"):
            continue
        if o["sem"]:
            ins.then_inc(T.sem[o["sem"]], 16)
        elif i in s["val"]:
            ins.then_inc(T.sem["s" + o["eng"]], 1)
    for k, j in s["last"].items():
        g.wait_ge(T.sem[k], count(j))
        if ops[j].get("remote"):
            g.wait_ge(T.sem["x" + k], len(eng_out))
